import numpy as np, ml_dtypes
CORES = [48,51,52,55]
N = 4
import mx_ref
BF = ml_dtypes.bfloat16
def gentries(a):
    return np.ascontiguousarray(a.reshape(8, 16, -1).transpose(0, 2, 1)).reshape(8, -1)
def gtable(e):
    e = np.asarray(e); return np.ascontiguousarray(e.reshape(8, -1, 16).transpose(0, 2, 1)).reshape(128, -1).astype(np.int32)
def gcols(t, e):
    v = np.concatenate([t.reshape(8, 16, -1, 4), np.zeros((8, 16, 1, 4), BF)], axis=2)
    return np.ascontiguousarray(np.stack([v[g][:, e[g]] for g in range(8)])).reshape(128, -1)
def tile(rs):
    return np.stack(rs, axis=2).reshape(128, -1).astype(BF)
def pick(q, e):
    c = np.concatenate([q[0].reshape(128, -1, 4), np.zeros((128, 1, 4), np.uint8)], axis=1); s = np.concatenate([q[1], np.ones((16, 1), np.uint8)], axis=1)
    return (np.ascontiguousarray(c[:, e].reshape(128, -1)), np.ascontiguousarray(s[:, e]))
def join(*qs):
    return (np.concatenate([q[0] for q in qs], axis=1), np.concatenate([q[1] for q in qs], axis=1))
def put(q, e, v):
    c, s = q[0].reshape(128, -1, 4).copy(), q[1].copy(); c[:, e] = v[0].reshape(128, -1, 4); s[:, e] = v[1]
    return (c.reshape(128, -1), s)
def pk(c, s):
    return (np.ascontiguousarray(c), mx_ref.live(s))
def emit(q):
    return q[0], q[1]
def packed(v, rng):
    q = [mx_ref.quantize(np.ascontiguousarray(v[r])) for r in range(N)]
    return np.stack([a for a, b in q]), np.stack([mx_ref.plane(b, rng) for a, b in q])
def values_of_codes():
    e, c = np.zeros((128, 128, 4), np.float32), np.zeros((128, 2, 4), np.uint8)
    e[np.arange(128), np.arange(128), 0] = 1
    c[:127, :, 0] = np.arange(256).reshape(2, 128).T[:127]
    return mx_ref.matmul(mx_ref.quantize(e.reshape(128, 512).astype(BF)), (c.reshape(128, 8), np.full((16, 2), 127, np.uint8))).T.reshape(-1).astype(np.float64)
CODE_VALUE, SCALE_VALUE = values_of_codes(), 2.0 ** (np.arange(256) - 127.0)
def decode(q):
    return (CODE_VALUE[q[0]].reshape(16, 8, -1, 4) * SCALE_VALUE[q[1]][:, None, :, None] + 0.0).reshape(128, -1).astype(np.float32)
def f(rng, *shape):
    return mx_ref.flush((rng.standard_normal(shape, dtype=np.float32) * np.exp2(rng.integers(-2, 3, shape[:-1] + (1,)))).astype(BF))
def wide(rng, *shape, cols=0):
    v = rng.standard_normal(shape, dtype=np.float32) * np.exp2(rng.integers(-12, 13, shape)).astype(np.float32)
    if cols: v *= np.repeat(np.exp2(rng.integers(-cols, cols + 1, shape[:-2] + (1, shape[-1] // 4))) * (rng.random(shape[:-2] + (1, shape[-1] // 4)) > 0.0625), 4, axis=-1).astype(np.float32)
    return mx_ref.flush(v.astype(BF))
C, H, R = 384, 160, 3
def big(v):
    v = v.astype(np.float32)
    v[np.abs(v) < np.float32(2.0 ** -16)] = 0
    return v.astype(BF)
def numbers_of(rng):
    return {"x": big(f(rng, N, 128, 4 * C)), "u": np.array(f(rng, N, 128, 512)), "v": np.array(f(rng, N, 128, 512))}
def layers(rng, still=[]):
    w = big(f(rng, N, 128, 2048)).reshape(N, 8, 16, 4, 8, 16, 4)
    for i in still: w[:, :, :, :, :, i] = 0
    return w
def weights(rng, w):
    c, s = packed(np.ascontiguousarray(w).reshape(N, 128, 2048), rng)
    return {"wc": c, "ws": s}
def holes(rng):
    return np.sort(np.argsort(rng.random((N, 8, C - 1)), axis=2)[:, :, :H], axis=2)
def throws(rng, a):
    free = np.ones((N, 8, 2 * C), bool)
    free[:, :, C:] = False
    np.put_along_axis(free, a, False, axis=2)
    np.put_along_axis(free, C + np.roll(a, -1, axis=0), True, axis=2)
    e = np.zeros((N, 8, C), np.int64)
    for i in range(C - 1, -1, -1):
        k = (0.5 + rng.random((N, 8, C))) * free[:, :, i:i + C]
        k[:, :, C - 1] = 2.0 * free[:, :, i + C - 1]
        e[:, :, i] = i + np.argmax(k, axis=2)
        np.put_along_axis(free, e[:, :, i:i + 1], False, axis=2)
    return e
def lists(e):
    return np.stack([gtable(e[r]) for r in range(N)])
def meet(rng, e):
    used, out = [False] * C, []
    e = e.tolist()
    for i, k in zip(rng.permutation(C).tolist(), rng.integers(0, 4, C).tolist()):
        j = e[i] + (0, 1, 1 - C, -C)[k]
        if 0 <= j < C and j != i and not used[i] and not used[j]:
            used[i] = used[j] = True
            out += [i, j]
    return np.array(out + [int(i) for i in rng.permutation(C) if not used[i]])
def setup_inputs(rng):
    return {**numbers_of(rng), "p": lists(throws(rng, holes(rng))), **weights(rng, layers(rng))}
def setup_inputs_ties(rng):
    d = numbers_of(rng)
    o = rng.permutation(N)
    x = d["x"].reshape(N, 8, 16, C, 4)
    k = rng.integers(0, 3, (N, 8, C))
    k[o[2]] = 1
    x[:, :, 0] = 0
    x[:, :, 0, :, 0] = k.astype(np.float32).astype(BF)
    u = d["u"].reshape(N, 128, 128, 4)
    u[:, :, ::16] = 0
    for r in range(N):
        for h in range(0, 128, 16): u[r, h, h, 0] = 0.0 if r == o[0] else -1.0 if r == o[1] else 1.0
    return {"x": x.reshape(N, 128, 4 * C), "u": u.reshape(N, 128, 512), "v": d["v"], "p": lists(throws(rng, holes(rng))), **weights(rng, layers(rng, [0]))}
def setup_inputs_near(rng):
    d = numbers_of(rng)
    o = rng.permutation(N) % 4
    low = rng.permutation(8)[:4]
    x = d["x"].astype(np.float32).reshape(N, 8, 16, C, 4)
    u = d["u"].reshape(N, 128, 128, 4)
    x[:, :, 0] = 0
    x[:, :, 8:] = 0
    u[:, :, ::16] = 0
    for r in range(N):
        k = 1.0 if o[r] == 0 else 2.0 ** -30
        if o[r] < 3:
            s = rng.integers(0, 16, (8, C))
            x[r, :, 8] = ((s[:, :, None] >> np.arange(4)) & 1) * np.exp2(np.arange(4) - 23.0)
        else:
            x[r, :, 8, :, 0] = rng.integers(8, 16, (8, C)) * rng.choice([-1.0, 1.0], (8, C)) * 2.0 ** -27
            for g in low: x[r, g, 8:10, :, 0] = rng.integers(8, 15, (2, C)) * 2.0 ** -30
        if o[r] < 2:
            x[r, :, 0, :, 0] = rng.choice([-1.0, 1.0], (8, C))
            x[r, :, 11, :, 0] = 2.0 ** -10
        if o[r] == 2:
            for g in rng.permutation(8)[:4]: x[r, g, 0, rng.integers(C), 0] = 2.0 ** 29
        for h in range(0, 128, 16):
            u[r, h + 8, h] = k
            if o[r] < 2:
                u[r, h, h, 0] = k
                u[r, h + 11, h, 0] = k
            if o[r] == 2: u[r, h, h, 0] = 1.0
            if o[r] == 3 and h // 16 in low: u[r, h + 9, h] = -k
    still = [0, 8, 9, 10, 11, 12, 13, 14, 15]
    w = layers(rng, still)
    w[:, :, still] = 0
    return {"x": x.reshape(N, 128, 4 * C).astype(BF), "u": u.reshape(N, 128, 512), "v": d["v"], "p": lists(throws(rng, holes(rng))), **weights(rng, w)}
def setup_inputs_huge(rng):
    d = numbers_of(rng)
    h, o = rng.permutation(8), rng.permutation(N)
    c = rng.choice([-1.0, 1.0], (N, 1, 1, C, 1))
    c[o == 0] = 1.0
    x = (0.9 + 0.1 * rng.random((N, 8, 16, C, 4))) * 2.0 ** 30
    x[:, h[4:]] *= c
    a = (0.9 + 0.1 * rng.random((N, 8, 16, 8, 4))) * 2.0 ** 30
    for r in range(N):
        if o[r] == 0: a[r] *= -1.0
        elif o[r] % 2 == 1:
            a[r] *= -1.0
            a[r, h[4:]] = 0
        else: a[r, h[:4]] = 0
    u = d["u"].reshape(N, 128, 128, 4)
    u[:, :, ::16] = a.reshape(N, 128, 8, 4).astype(np.float32).astype(BF)
    w = np.zeros((N, 128, 4, 128, 4), np.float32)
    i = np.arange(128)
    for b in range(4): w[:, i, b, i, b] = -1
    return {"x": x.astype(np.float32).reshape(N, 128, 4 * C).astype(BF), "u": u.reshape(N, 128, 512), "v": d["v"], "p": lists(throws(rng, holes(rng))), **weights(rng, w.astype(BF))}
def setup_inputs_edges(rng):
    d = numbers_of(rng)
    h, a = rng.permutation(8), holes(rng)
    a[:, h[:2]] = np.arange(H)
    a[:, h[2:4]] = np.arange(C - 1 - H, C - 1)
    e = throws(rng, a)
    e[:, h[:2]] = np.arange(C) + H
    x = d["x"].reshape(N, 8, 16, C, 4)
    x[:, :, :3] = 0
    for r in range(N):
        for g in range(8):
            n = np.zeros(C, np.int64)
            n[meet(rng, e[r, g])] = np.arange(C - 1, -1, -1)
            for i in range(3): x[r, g, i, :, 0] = ((n >> (6 - 3 * i)) & 7).astype(np.float32).astype(BF)
    k = np.exp2(rng.integers(-2, 3, (N, 8, 1, C, 1)))
    b = (2 * rng.integers(0, 8, (N, 8, 8, C, 4)) + 1) * 2.0 ** -16 * k
    b[:, :, 0, :, 0] = 1.96875 * k[:, :, 0, :, 0]
    b *= rng.choice([-1.0, 1.0], b.shape)
    x[:, :, 8:] = b.astype(np.float32).astype(BF)
    u = d["u"].reshape(N, 128, 128, 4)
    u[:, :, ::16] = 0
    for g in range(0, 128, 16):
        for i in range(3): u[:, g + i, g, 0] = 2.0 ** (6 - 3 * i)
    return {"x": x.reshape(N, 128, 4 * C), "u": u.reshape(N, 128, 512), "v": d["v"], "p": lists(e), **weights(rng, layers(rng, [0, 1, 2, 8, 9, 10, 11, 12, 13, 14, 15]))}
def setup_inputs_spread(rng):
    d = setup_inputs(rng)
    d["x"] = big(wide(rng, N, 128, 4 * C, cols=6))
    return d
def check_inputs(d):
    b = []
    for k in ("x", "u", "v"):
        a = np.abs(d[k].astype(np.float32))
        if not (np.isfinite(a).all() and ((a == 0) | (a >= 2.0 ** -30) & (a <= 2.0 ** 30)).all()): b.append("a value of " + k)
    e = np.stack([gentries(d["p"][r]) for r in range(N)]).astype(np.int64)
    t, s = e - np.arange(C), np.sort(e, axis=2)
    if ((t < 0) | (t >= C)).any(): b.append("p: a landing out of its column's bounds")
    if (s[:, :, 1:] == s[:, :, :-1]).any(): b.append("p: equal landings")
    if (np.count_nonzero(e >= C, axis=2) != H).any(): b.append("p: the number of crossing landings")
    k = np.concatenate([s[:, :, :C - H], np.roll(s[:, :, C - H:], 1, axis=0) - C], axis=2)
    if (np.sort(k, axis=2) != np.arange(C)).any(): b.append("p: crossing landings aren't the next rank's holes")
    none, least, most = [emit(mx_ref.quantize(np.full((128, 16), k, np.float32).astype(BF)))[1][0, 0] for k in (0.0, 2.0 ** -30, 2.0 ** 30)]
    for r in range(N):
        if ((d["wc"][r] == 0x7F) | (d["wc"][r] == 0xFF)).any(): b.append("wc: a code that is no number")
        s = mx_ref.live(d["ws"][r])
        if ((s != none) & ((s < least) | (s > most))).any(): b.append("ws: a scale out of range")
    return b
def reference(x, u, v, p, wc, ws):
    qu = [mx_ref.quantize(u[r]) for r in range(N)]
    lay = [pk(wc[r], ws[r]) for r in range(N)]
    now = [x[r] for r in range(N)]
    land = np.stack([gentries(p[r]) for r in range(N)]).astype(np.int64)
    for t in range(R):
        for r in range(N):
            s = mx_ref.matmul(qu[r], mx_ref.quantize(now[r]))[::16] + np.float32(0.0)
            o = np.argsort(-s, axis=1, kind="stable")
            a, b = o[:, ::2], o[:, 1::2]
            la, lb = np.take_along_axis(land[r], a, axis=1), np.take_along_axis(land[r], b, axis=1)
            ok = (a <= lb) & (lb < a + C) & (b <= la) & (la < b + C)
            np.put_along_axis(land[r], a, np.where(ok, lb, la), axis=1)
            np.put_along_axis(land[r], b, np.where(ok, la, lb), axis=1)
        back, hits = np.argsort(land, axis=2), np.sort(land, axis=2)
        given = [mx_ref.quantize(gcols(now[r], back[r][:, C - H:])) for r in range(N)]
        new = []
        for r in range(N):
            both = np.concatenate([now[r], decode(given[r - 1]).astype(BF)], axis=1)
            e = np.zeros((8, C), np.int64)
            np.put_along_axis(e, hits[r][:, :C - H], back[r][:, :C - H], axis=1)
            np.put_along_axis(e, hits[r - 1][:, C - H:] - C, np.stack([C + np.arange(H)] * 8), axis=1)
            z = ((gcols(both, e).astype(np.float32) + now[r].astype(np.float32)) * np.float32(0.5)).astype(BF)
            q = mx_ref.quantize(z)
            new.append(tile([mx_ref.matmul(pick(lay[r], np.arange(128 * b, 128 * b + 128)), q) * np.float32(0.03125) + z[:, b::4].astype(np.float32) for b in range(4)]))
        now = new
    y, ol = np.zeros((N, 128, C), np.float32), np.zeros((N, 8, C), np.float32)
    oc, osc = np.zeros((N, 128, 4 * C), np.uint8), np.zeros((N, 16, C), np.uint8)
    for r in range(N):
        q = mx_ref.quantize(now[r])
        y[r] = mx_ref.matmul(mx_ref.quantize(v[r]), q)
        ol[r] = land[r]
        oc[r], osc[r] = emit(q)
    return {"y": y, "ol": ol, "oc": oc, "osc": osc}

@@ -1,0 +1,432 @@
+from concourse.bass import IndirectOffsetOnAxis
+from concourse.mybir import dt, AluOpType, ActivationFunctionType
+
+C = 384
+ROUNDS = 3
+BIG = 2.0 ** 96
+HOLD = 1048576
+DROP = 2 ** 27
+NA = 1
+Q8 = "float8_e4m3fn_x4"
+A_ = AluOpType
+FN = ActivationFunctionType
+COPY = FN.Copy
+INTS = "P24 T16 T1 k24 kb kc ic pi pm k1 k3 xi xj L L2 I I2 cx cx2 r r2 oi own y2 rf b1 b2 b3 b4".split()
+FLOATS = "rs RA KA wa fk".split()
+PARTS = {"rs": 24, "e2": 2, "xi": 2, "X1": 2, "M": 2, "zt0": 4, "zt1": 4, "Ce": 3}
+for _i in range(6):
+    PARTS["C%d" % _i] = 4
+PARTS["C5"] = 4 + NA
+for _i in range(1, ROUNDS + 1):
+    PARTS["xt%da" % _i] = PARTS["xt%db" % _i] = 4
+
+
+def _ncols(a):
+    return max(128, 64 * (a + 1))
+
+
+SCRATCH = {"LI": ("sbuf", [128, 24 * len(INTS)], "int32"), "LF": ("sbuf", [128, 24 * len(FLOATS)], "float32")}
+
+
+def _sb(name, cols, dtype):
+    SCRATCH[name] = ("sbuf", [128, cols], dtype)
+
+
+for _i in range(ROUNDS + 1):
+    _sb("xt%d" % _i, 4 * C, "bfloat16")
+    _sb("qx%d" % _i, C, Q8)
+    _sb("sx%d" % _i, C, "uint8")
+    SCRATCH["wd%d" % _i] = ("dram", [8, C], "float32")
+for _i in range(ROUNDS):
+    _sb("land%d" % _i, C, Q8)
+    _sb("lans%d" % _i, C, "uint8")
+    _sb("sl%d" % _i, 24, "int32")
+    _sb("al%d" % _i, 24, "int32")
+for _i in range(4):
+    _sb("win%d" % _i, 896, "bfloat16")
+    _sb("eq%d" % _i, 128, Q8)
+    _sb("es%d" % _i, 128, "uint8")
+for _i in range(6):
+    _sb("C%d" % _i, 4 * _ncols(_i), "bfloat16")
+    _sb("cq%d" % _i, _ncols(_i), Q8)
+    _sb("cs%d" % _i, _ncols(_i), "uint8")
+for _n, _c, _d in (
+        ("Ce", 4 * C, "bfloat16"), ("ceq", C, Q8), ("ces", C, "uint8"), ("sg", NA * C, "bfloat16"),
+        ("ut", 512, "bfloat16"), ("uq", 128, Q8), ("us", 128, "uint8"), ("u16q", 128, Q8), ("u16s", 128, "uint8"),
+        ("vt", 512, "bfloat16"), ("vq", 128, Q8), ("vs", 128, "uint8"),
+        ("wq", 512, Q8), ("wsc", 512, "uint8"), ("xh", 4 * C, "bfloat16"), ("et", 520, "bfloat16"),
+        ("zt", 4 * C, "bfloat16"), ("zf", 4 * C, "bfloat16"), ("zq", C, Q8), ("zs", C, "uint8"),
+        ("gt0", 512, "bfloat16"), ("gt", 512, "bfloat16"), ("gq", 128, Q8), ("gs", 128, "uint8"),
+        ("zb", 520, "bfloat16"), ("junk", 24 * C, "bfloat16"),
+        ("D", C, "float32"), ("mb", C, "float32"), ("kf", 8, "float32"), ("d0", C, "float32"),
+        ("c2", C, "float32"), ("M", C, "float32"), ("h", C, "float32"), ("U8", 8, "int32"), ("idx", 2, "int32"),
+        ("pP", 24, "uint16"), ("rp", 24, "uint16"), ("upo", 8, "uint16"), ("e1", C, "float32"), ("ru", 24, "uint16"),
+        ("WT", C, "float32"), ("WN", C, "float32"), ("WS", C, "float32"),
+        ("e2", C, "float32"), ("Lu", 24, "uint16"), ("TLW", 768, "float32"), ("e3", C, "float32"),
+        ("e4", C, "float32"), ("tz", 24, "int32"), ("S", C, "float32"),
+        ("X0", 48, "float32"), ("X1", 48, "float32"), ("so", 48, "float32"), ("tl", 24, "uint16"),
+        ("ysb", C, "float32")):
+    _sb(_n, _c, _d)
+for _i in range(8):
+    SCRATCH["P%d" % _i] = ("psum", [128, 512], "float32")
+SEMAPHORES = (["sV", "sA", "sT", "sG", "loc", "lx", "ly", "lp", "lu", "lv", "lw", "ls", "oy0", "oy1", "ool", "oc0", "oc1"]
+              + ["oos%d" % k for k in range(4)] + ["dw%d" % k for k in range(4)] + ["ig%d" % k for k in range(4)]
+              + ["aq%d" % k for k in range(3)] + ["al%d" % k for k in range(3)])
+
+
+def rank_program(g, core, T, topo):
+    rank = T.rank_of(core)
+    if rank is None:
+        return
+    nxt = T.cores[(rank + 1) % len(T.cores)]
+    rid, pid = topo.addr(nxt)[:2]
+    mask = topo.mask(core, nxt)
+    neng = len(topo.engines(core, nxt))
+    prv = T.cores[(rank - 1) % len(T.cores)]
+    peng = len(topo.engines(prv, core))
+    V, AC, PE = g.vector, g.scalar, g.tensor
+    queue = {"V": V, "A": AC, "T": PE, "G": g, "S": g.sync}
+    own = {"V": "sV", "A": "sA", "T": "sT", "G": "sG"}
+    cnt, known = {}, {q: {} for q in queue}
+    wr, rd = {}, {}
+
+    def ex(keys):
+        return [p for k in keys for p in (["%s.%d" % (k, i) for i in range(PARTS[k])] if k in PARTS else [k])]
+
+    def before(q, R, W, adds=False):
+        toks = []
+        for k in ex(R):
+            if k in wr:
+                toks.append(wr[k])
+        for k in ex(W):
+            for t in ([wr[k]] if k in wr else []) + rd.get(k, []):
+                if adds and t[2] == q:
+                    continue
+                toks.append(t)
+        best = {}
+        for t in toks:
+            if known[q].get(t[0], 0) < t[1] and (t[0] not in best or best[t[0]][1] < t[1]):
+                best[t[0]] = t
+        keep = [t for t in best.values() if not any(o is not t and o[3].get(t[0], 0) >= t[1] for o in best.values())]
+        for t in keep:
+            queue[q].wait_ge(T.sem[t[0]], t[1])
+            for s, c in list(t[3].items()) + [(t[0], t[1])]:
+                known[q][s] = max(known[q].get(s, 0), c)
+
+    def after(q, sem, n, R, W):
+        cnt[sem] = cnt.get(sem, 0) + n
+        clk = dict(known[q])
+        clk[sem] = cnt[sem]
+        tok = (sem, cnt[sem], q, clk)
+        for k in ex(R):
+            rd[k] = [t for t in rd.get(k, []) if t[0] != sem] + [tok]
+        for k in ex(W):
+            wr[k] = tok
+            rd[k] = []
+
+    def op(q, R, W, f, adds=False):
+        before(q, R, W, adds)
+        f().then_inc(T.sem[own[q]], 1)
+        after(q, own[q], 1, R, W)
+
+    def dma(q, sem, R, W, f):
+        before(q, R, W)
+        f().then_inc(T.sem[sem], 16)
+        after(q, sem, 16, R, W)
+
+    def b8(v):
+        return v.bitcast(dt.uint8)
+
+    def li(name, lo=0, hi=24):
+        o = 24 * INTS.index(name)
+        return T.LI[:, o + lo:o + hi]
+
+    def lf(name, lo=0, hi=24):
+        o = 24 * FLOATS.index(name)
+        return T.LF[:, o + lo:o + hi]
+
+    def ts(R, W, out, in0, s1, s2, op0, op1=None):
+        if op1 is None:
+            op("V", R, W, lambda: V.tensor_scalar(out, in0, s1, None, op0))
+        else:
+            op("V", R, W, lambda: V.tensor_scalar(out, in0, s1, s2, op0, op1))
+
+    def tt(R, W, out, a, b, o):
+        op("V", R, W, lambda: V.tensor_tensor(out, a, b, o))
+
+    def cp(R, W, out, a):
+        op("V", R, W, lambda: V.tensor_copy(out, a))
+
+    def act(R, W, out, a, scale=None):
+        if scale is None:
+            op("A", R, W, lambda: AC.activation(out, a, COPY))
+        else:
+            op("A", R, W, lambda: AC.activation(out, a, COPY, scale=scale))
+
+    def quant(R, W, q, s, t):
+        op("V", R, W, lambda: V.quantize_mx(q, s, t))
+
+    def scan(R, W, out, d0, d1, init, o0, o1):
+        op("V", R, W, lambda: V.tensor_tensor_scan(out, d0, d1, init, o0, o1))
+
+    def mm(R, W, out, lq, ls_, rq, rs_, start=True, stop=True):
+        op("T", R, W, lambda: PE.matmul_mx(out, lq, ls_, rq, rs_, start, stop), not start)
+
+    def arrives(key, sem, n):
+        cnt[sem] = n
+        wr[key] = (sem, n, "-", {})
+
+    for t in range(ROUNDS):
+        arrives("land%d" % t, "aq%d" % t, 2 * peng)
+        arrives("al%d" % t, "al%d" % t, peng)
+
+    dma("S", "lx", [], ["xt0a"], lambda: g.sync.dma_start(T.xt0[:, 0:768], T.x[:, 0:768]))
+    dma("A", "lu", [], ["ut"], lambda: AC.dma_start(T.ut[:], T.u[:]))
+    dma("A", "ly", [], ["xt0b"], lambda: AC.dma_start(T.xt0[:, 768:1536], T.x[:, 768:1536]))
+    dma("S", "lp", [], ["pi"], lambda: g.sync.dma_start(li("pi"), T.p[:]))
+
+    op("G", [], ["P24"], lambda: g.iota(li("P24"), [[0, 24]], 0, 1))
+    op("G", [], ["D"], lambda: g.iota(T.D[:], [[0, 24], [1, 16]], 0, 0, allow_small_or_imprecise_dtypes=True))
+    op("G", [], ["U8"], lambda: g.iota(T.U8[:], [[16, 8]], 0, 0))
+    op("G", [], ["T16"], lambda: g.iota(li("T16"), [[16, 24]], 0, 0))
+    op("G", [], ["T1"], lambda: g.iota(li("T1"), [[1, 24]], 0, 0))
+    op("V", [], ["zb"], lambda: V.memset(T.zb[:], 0.0))
+    op("V", [], ["rs"], lambda: V.memset(lf("rs"), 0.0))
+    op("V", [], ["X0"], lambda: V.memset(T.X0[:], 0.0))
+    ts(["P24"], ["k24"], li("k24"), li("P24"), 15, None, A_.bitwise_and)
+    ts(["P24"], ["idx"], T.idx[:, 0:1], li("P24", 0, 1), 4, None, A_.logical_shift_right)
+    cp(["k24"], ["kf"], T.kf[:, 0:1], li("k24", 0, 1))
+    op("G", ["zb"], ["et"], lambda: g.affine_select(T.et[:], T.zb[:, 0:520], [[1, 520]], A_.not_equal, 1.0, -4, -4))
+    op("G", ["zb"], ["gt0"], lambda: g.affine_select(
+        T.gt0[:], T.zb[:, 0:512], [[16, 8], [0, 64]], A_.is_gt, 1.0, 0, -1))
+    op("G", ["gt0"], ["gt"], lambda: g.affine_select(T.gt[:], T.gt0[:], [[16, 8], [0, 64]], A_.is_ge, 0.0, 15, -1))
+    for a in range(6):
+        lo, hi = 256 * a, max(512, 256 * a + 256)
+        act(["zb"], ["C%d" % a], T["C%d" % a][:, lo:hi], T.zb[:, 0:hi - lo])
+    act(["zb"], ["Ce.0"], T.Ce[:, 0:512], T.zb[:, 0:512])
+    ts(["D", "kf"], ["mb"], T.mb[:], T.D[:], T.kf[:, 0:1], BIG, A_.not_equal, A_.mult)
+    ts(["D", "kf"], ["d0"], T.d0[:], T.D[:], T.kf[:, 0:1], BIG, A_.is_equal, A_.mult)
+    cp(["U8"], ["upo"], T.upo[:], T.U8[:])
+    tt(["T16", "k24"], ["ic"], li("ic"), li("T16"), li("k24"), A_.add)
+    op("V", [], ["d0"], lambda: V.memset(T.d0[:, 0:C:16], BIG))
+    ts(["k24"], ["kb"], li("kb"), li("k24"), HOLD, None, A_.mult)
+    ts(["ic"], ["pm"], li("pm"), li("ic"), 1024, 524288, A_.mult, A_.add)
+    ts(["k24"], ["k1"], li("k1"), li("k24"), 24, None, A_.mult)
+    tt(["pm", "pi"], ["wa"], lf("wa"), li("pm"), li("pi"), A_.add)
+    dma("S", "dw0", ["wa"], ["wd0"], lambda: g.sync.dma_start(T.wd0[:], lf("wa")))
+    tt(["kb", "T16"], ["kc"], li("kc"), li("T16"), li("kb"), A_.add)
+    tt(["k1", "T1"], ["k3"], li("k3"), li("k1"), li("T1"), A_.add)
+    ts(["kb"], ["fk"], lf("fk"), li("kb"), -1, 15 * HOLD + 511, A_.mult, A_.add)
+    ts(["kc"], ["KA"], lf("KA"), li("kc"), -1 - 15 * HOLD, None, A_.add)
+    cp(["k3"], ["pP"], T.pP[:], li("k3"))
+    ts(["mb"], ["c2"], T.c2[:], T.mb[:], (DROP + HOLD) / BIG, -float(DROP), A_.mult, A_.add)
+    quant(["ut"], ["uq"], T.uq[:, 0:128], T.us[:, 0:128], T.ut[:])
+    cp(["uq", "upo"], ["u16q"], T.u16q[:, 0:128].bitcast(dt.uint32),
+       T.uq[:, 0:128].bitcast(dt.uint32).indirect(T.upo[:, 0:8]))
+    act(["uq", "upo"], ["u16s"], T.u16s[:, 0:128], T.us[:, 0:128].indirect(T.upo[:, 0:8]))
+    dma("S", "lw", ["xt0a", "xt0b"], ["wq"], lambda: g.sync.dma_start(b8(T.wq[:, 0:512]), T.wc[:]))
+    dma("S", "ls", [], ["wsc"], lambda: g.sync.dma_start(T.wsc[:, 0:512], T.ws[:]))
+    dma("S", "lv", [], ["vt"], lambda: g.sync.dma_start(T.vt[:], T.v[:]))
+
+    def spread(i):
+        dma("G", "ig%d" % i, ["wd%d" % i, "idx"], ["WT"], lambda: g.indirect_dma_start(
+            T.WT[:], None, T["wd%d" % i][:], IndirectOffsetOnAxis(ap=T.idx[:, 0:1], axis=0), bounds_check=7))
+
+    spread(0)
+
+    def scores(t, c):
+        qx, sx, k = T["qx%d" % t], T["sx%d" % t], "P%d" % (2 + c)
+        lo, hi = 192 * c, 192 * c + 192
+        kq = "qx%d%s" % (t, "ab"[c])
+        quant(["xt%d%s" % (t, "ab"[c])], [kq], qx[:, lo:hi], sx[:, lo:hi], T["xt%d" % t][:, 4 * lo:4 * hi])
+        if t < ROUNDS:
+            mm(["u16q", "u16s", kq], [k], T[k][:, 0:192], T.u16q[:, 0:128], T.u16s[:, 0:128], qx[:, lo:hi], sx[:, lo:hi])
+            if c == 0:
+                if t == 0:
+                    act(["zb"], ["Ce.1"], T.Ce[:, 512:1024], T.zb[:, 0:512])
+                act([k], ["S0", "turn0"], T.S[:, 0:192], T[k][:, 0:192])
+                if t == 0:
+                    act(["zb"], ["Ce.2"], T.Ce[:, 1024:1536], T.zb[:, 0:512])
+        else:
+            mm(["vq", kq], [k], T[k][:, 0:192], T.vq[:, 0:128], T.vs[:, 0:128], qx[:, lo:hi], sx[:, lo:hi])
+
+    for t in range(ROUNDS):
+        xt, qx, sx = T["xt%d" % t], T["qx%d" % t], T["sx%d" % t]
+        kx = ["xt%da" % t, "xt%db" % t]
+        kq = "qx%d" % t
+
+        def half(b):
+            act(kx, ["winx%d" % b], T["win%d" % b][:, 0:C], xt[:, b:4 * C:4], 2.0 ** -6)
+
+        if t == 0:
+            scores(0, 0)
+            scores(0, 1)
+        before("G", [kq + "a", kq + "b"], [])
+        g.remote_dma(b8(T["land%d" % t][:, 0:C]), b8(qx[:, 0:C]), T.sem["aq%d" % t], T.sem.loc, pid, rid, mask)
+        g.remote_dma(T["lans%d" % t][:, 0:C], sx[:, 0:C], T.sem["aq%d" % t], T.sem.loc, pid, rid, mask)
+        cnt["loc"] = cnt.get("loc", 0) + 2 * neng
+        if t == 0:
+            for b in range(4):
+                quant(["et"], ["eq%d" % b], T["eq%d" % b][:, 0:128], T["es%d" % b][:, 0:128], T.et[:, 4 - b:516 - b])
+        tt(["P2", "mb", "turn0"], ["M.0"], T.M[:, 0:192], T.P2[:, 0:192], T.mb[:, 0:192], A_.add)
+        tt(["P3", "mb"], ["M.1", "turn1"], T.M[:, 192:384], T.P3[:, 0:192], T.mb[:, 192:384], A_.add)
+        act(["P3", "turn1"], ["S1"], T.S[:, 192:384], T.P3[:, 0:192])
+        scan(["d0", "M"], ["h"], T.h[:], T.d0[:], T.M[:], BIG, A_.add, A_.min)
+
+        for n in range(NA):
+            b = 3 - n
+            w = 16 * (20 + b)
+            op("A", ["S0", "S1", "h"], ["sg%d" % n], lambda: AC.activation(
+                T.sg[:, C * n:C * n + w], T.S[:, 0:w], FN.Sign, bias=T.h[:, w + 15:w + 16], scale=-1.0))
+            op("A", ["sg%d" % n], ["C5.%d" % (4 + n), "rs.%d" % (20 + b)], lambda: AC.activation(
+                T.C5[:, b:4 * w:4], T.sg[:, C * n:C * n + w], FN.Relu, accum_out=lf("rs", 20 + b, 21 + b)))
+
+        def compare(a):
+            Ct = T["C%d" % a]
+            mine = [b for b in (3, 2, 1, 0) if a < 5 or b < 4 - NA]
+            for b in mine + [b for b in (3, 2, 1, 0) if b not in mine]:
+                w = 16 * (4 * a + b) + 16
+                lo = 0 if b in mine else w - 16
+                ts(["S0", "S1", "h"], ["C%d.%d" % (a, b)], Ct[:, 4 * lo + b:4 * w:4], T.S[:, lo:w], T.h[:, w - 1:w], None,
+                   A_.is_lt)
+            for b in mine:
+                j = 4 * a + b
+                if j:
+                    op("A", ["C%d.%d" % (a, b)], ["rs.%d" % j, "junk%d" % j], lambda: AC.activation(
+                        T.junk[:, C * j:C * j + 16 * j], Ct[:, b:64 * j:4], COPY, accum_out=lf("rs", j, j + 1)))
+
+        def count(a, start=False, stop=False):
+            n = _ncols(a)
+            quant(["C%d" % a], ["cq%d" % a], T["cq%d" % a][:, 0:n], T["cs%d" % a][:, 0:n], T["C%d" % a][:, 0:4 * n])
+            mm(["gq", "cq%d" % a], ["P1"], T.P1[:, 0:n], T.gq[:, 0:128], T.gs[:, 0:128],
+               T["cq%d" % a][:, 0:n], T["cs%d" % a][:, 0:n], start, stop)
+
+        compare(5)
+        if t == 0:
+            quant(["gt"], ["gq"], T.gq[:, 0:128], T.gs[:, 0:128], T.gt[:])
+        compare(4)
+        count(5, start=True)
+        compare(3)
+        count(4)
+        for c in range(2):
+            lo, hi = 192 * c, 192 * c + 192
+            tt(["h", "P%d" % (2 + c), "S%d" % c], ["Ce.%d" % (2 * c), "eqs%d" % c] + (["Ce.1"] if c == 0 else []),
+               T.Ce[:, 4 * lo:4 * hi:4], T.h[:, lo:hi], T["P%d" % (2 + c)][:, 0:192], A_.is_equal)
+        count(3)
+        compare(2)
+        quant(["Ce", "eqs0", "eqs1"], ["ceq"], T.ceq[:, 0:C], T.ces[:, 0:C], T.Ce[:])
+        mm(["gq", "ceq"], ["P1"], T.P1[:, 0:C], T.gq[:, 0:128], T.gs[:, 0:128], T.ceq[:, 0:C], T.ces[:, 0:C], False, False)
+        compare(1)
+        count(2)
+        compare(0)
+        count(1)
+        count(0, stop=True)
+        k = "rp" if t else "pP"
+        act(["WT", k], ["WN"], T.WN[:], T.WT[:, 0:C].indirect(T[k][:, 0:24]))
+        for c in range(2):
+            act(["zb"], ["TLW"] if c else ["TLWa"], T.TLW[:, 384 * c:384 * c + 384], T.zb[:, 0:384])
+        for b in range(4):
+            half(b)
+            if t == 0:
+                act(["zb"], ["gap%d" % b], T["win%d" % b][:, 384:512], T.zb[:, 0:128])
+        act(kx, ["xh"], T.xh[:], xt[:], 2.0 ** -6)
+        for b in range(4):
+            mm(["eq%d" % b, "land%d" % t], ["P%d" % (4 + b)], T["P%d" % (4 + b)][:, 0:C], T["eq%d" % b][:, 0:128],
+               T["es%d" % b][:, 0:128], T["land%d" % t][:, 0:C], T["lans%d" % t][:, 0:C])
+        for b in range(4):
+            act(["P%d" % (4 + b)], ["wind%d" % b], T["win%d" % b][:, 512:896], T["P%d" % (4 + b)][:, 0:C], 2.0 ** -6)
+        tt(["KA", "rs"], ["RA"], lf("RA"), lf("KA"), lf("rs"), A_.subtract)
+        scan(["c2", "P1"], ["e1"], T.e1[:], T.c2[:], T.P1[:, 0:C], 0.0, A_.add, A_.max)
+        tt(["e1", "RA"], ["rf"], li("rf"), T.e1[:, 15:C:16], lf("RA"), A_.add)
+        cp(["rf"], ["ru"], T.ru[:], li("rf"))
+        cp(["ru", "WN"], ["WS"], T.WS[:, 0:C].indirect(T.ru[:, 0:24]), T.WN[:])
+        scan(["c2", "WS"], ["e2.0"], T.e2[:, 0:192], T.c2[:, 0:192], T.WS[:, 0:C:2], 0.0, A_.add, A_.max)
+        scan(["c2", "WS"], ["e2.1"], T.e2[:, 192:384], T.c2[:, 0:192], T.WS[:, 1:C:2], 0.0, A_.add, A_.max)
+        cp(["e2"], ["xi.0"], li("xi"), T.e2[:, 15:C:16])
+        cp(["e2"], ["xi.1"], li("xj"), T.e2[:, 15:C:16])
+        ts(["xi"], ["L"], li("L", 0, 48), li("xi", 0, 48), 1023, None, A_.bitwise_and)
+        ts(["xi"], ["I"], li("I", 0, 36), li("xi", 0, 36), 10, 511, A_.logical_shift_right, A_.bitwise_and)
+        tt(["L", "I"], ["cx"], li("cx", 0, 36), li("L", 12, 48), li("I", 0, 36), A_.subtract)
+        tt(["L"], ["X1.0"], T.X1[:, 0:48:2], li("L", 12, 36), li("L", 0, 24), A_.subtract)
+        ts(["cx"], ["r"], li("r", 0, 36), li("cx", 0, 36), -191.5, 1.0 / 384, A_.add, A_.mult)
+        cp(["L"], ["X1.1"], T.X1[:, 1:48:2], li("L"))
+        tt(["r"], ["X0"], T.X0[:, 1:48:2], li("r", 0, 24), li("r", 12, 36), A_.is_equal)
+        scan(["X0", "X1"], ["so"], T.so[:], T.X0[:], T.X1[:], 0.0, A_.mult, A_.add)
+        cp(["so"], ["Lu"], T.Lu[:], T.so[:, 1:48:2])
+        kw = "wd%d" % (t + 1)
+        if t == ROUNDS - 1:
+            cp(["so"], ["wa"], lf("wa"), T.so[:, 1:48:2])
+            dma("S", "dw%d" % (t + 1), ["wa"], [kw], lambda: g.sync.dma_start(T[kw][:], lf("wa")))
+        cp(["Lu", "WS"], ["TLW", "TLWa"], T.TLW[:, 0:768].indirect(T.Lu[:, 0:12]), T.WS[:, 0:C:2])
+        cp(["Lu", "WS"], ["TLW", "TLWa"], T.TLW[:, 0:768].indirect(T.Lu[:, 12:24]), T.WS[:, 1:C:2])
+        scan(["c2", "TLW"], ["e3"], T.e3[:], T.c2[:], T.TLW[:, 384:768], 0.0, A_.add, A_.max)
+        ksl = "sl%d" % t
+        ts(["e3", "fk"], [ksl], T[ksl][:], T.e3[:, 15:C:16], lf("fk", 0, 1), 2.0 ** -10, A_.subtract, A_.mult)
+        before("G", [ksl], [])
+        g.remote_dma(T["al%d" % t][:], T[ksl][:], T.sem["al%d" % t], T.sem.loc, pid, rid, mask)
+        cnt["loc"] += neng
+        scan(["c2", "TLW", "TLWa"], ["e4"], T.e4[:], T.c2[:], T.TLW[:, 0:384], 0.0, A_.add, A_.max)
+        if t < ROUNDS - 1:
+            ts(["xi"], ["y2"], li("y2"), li("xi"), 1023 * 1024, None, A_.bitwise_and)
+        cp(["e4"], ["oi"], li("oi"), T.e4[:, 15:C:16])
+        if t < ROUNDS - 1:
+            tt(["so", "y2"], ["wa"], lf("wa"), T.so[:, 1:48:2], li("y2"), A_.add)
+        ts(["oi"], ["own"], li("own"), li("oi"), 10, 511, A_.logical_shift_right, A_.bitwise_and)
+        if t < ROUNDS - 1:
+            dma("S", "dw%d" % (t + 1), ["wa"], [kw], lambda: g.sync.dma_start(T[kw][:], lf("wa")))
+        spread(t + 1)
+        ts(["rf"], ["b1"], li("b1"), li("rf"), 31, None, A_.bitwise_and)
+        ts(["rf"], ["b2"], li("b2"), li("rf"), 5, None, A_.logical_shift_right)
+        ts(["b1"], ["b3"], li("b3"), li("b1"), 12, None, A_.mult)
+        tt(["b3", "b2"], ["b4"], li("b4"), li("b3"), li("b2"), A_.add)
+        cp(["b4"], ["rp"], T.rp[:], li("b4"))
+        if t == 0:
+            quant(["vt"], ["vq"], T.vq[:, 0:128], T.vs[:, 0:128], T.vt[:])
+        tt(["own", "al%d" % t], ["tz"], T.tz[:], li("own"), T["al%d" % t][:], A_.add)
+        cp(["tz"], ["tl"], T.tl[:], T.tz[:])
+        banks = [[2, 3, 4, 5], [6, 7, 0, 1]]
+
+        def catch(c, b):
+            lo, hi = 192 * c, 192 * c + 192
+            tt(["winx%d" % b, "gap%d" % b, "wind%d" % b, "xh", "tl"], ["zt%d.%d" % (c, b)],
+               T.zt[:, 4 * lo + b:4 * hi:4], T["win%d" % b][:, 0:896].indirect(T.tl[:, 12 * c:12 * c + 12]),
+               T.xh[:, 4 * lo + b:4 * hi:4], A_.add)
+
+        def layer(c):
+            lo, hi = 192 * c, 192 * c + 192
+            quant(["zt%d" % c], ["zq%d" % c], T.zq[:, lo:hi], T.zs[:, lo:hi], T.zt[:, 4 * lo:4 * hi])
+            act(["zt%d" % c], ["zf%d" % c], T.zf[:, 4 * lo:4 * hi], T.zt[:, 4 * lo:4 * hi], 32.0)
+            for b in range(4):
+                k = "P%d" % banks[c][b]
+                mm(["wq", "wsc", "zq%d" % c], [k], T[k][:, 0:192], T.wq[:, 128 * b:128 * b + 128],
+                   T.wsc[:, 128 * b:128 * b + 128], T.zq[:, lo:hi], T.zs[:, lo:hi])
+
+        def state(c, b):
+            lo, hi = 192 * c, 192 * c + 192
+            k = "P%d" % banks[c][b]
+            tt([k, "zf%d" % c], ["xt%d%s.%d" % (t + 1, "ab"[c], b)], T["xt%d" % (t + 1)][:, 4 * lo + b:4 * hi:4],
+               T[k][:, 0:192], T.zf[:, 4 * lo + b:4 * hi:4], A_.add)
+
+        for f, done in ((catch, layer), (state, lambda c: scores(t + 1, c))):
+            for b in range(4):
+                f(0, b)
+            f(1, 0)
+            done(0)
+            for b in range(1, 4):
+                f(1, b)
+            done(1)
+
+    act(["P2"], ["ysb0"], T.ysb[:, 0:192], T.P2[:, 0:192])
+    cp(["P3"], ["ysb1"], T.ysb[:, 192:384], T.P3[:, 0:192])
+    dma("S", "oc0", ["qx3a"], [], lambda: g.sync.dma_start(T.oc[:, 0:768], b8(T.qx3[:, 0:192])))
+    dma("A", "oy0", ["ysb0"], [], lambda: AC.dma_start(T.y[:, 0:192], T.ysb[:, 0:192]))
+    dma("S", "oc1", ["qx3b"], [], lambda: g.sync.dma_start(T.oc[:, 768:1536], b8(T.qx3[:, 192:384])))
+    act(["WT", "rp"], ["WN"], T.WN[:], T.WT[:, 0:C].indirect(T.rp[:, 0:24]))
+    dma("S", "oy1", ["ysb1"], [], lambda: g.sync.dma_start(T.y[:, 192:384], T.ysb[:, 192:384]))
+    for k in range(4):
+        dma("S", "oos%d" % k, ["qx3a", "qx3b"], [], lambda: g.sync.dma_start(
+            T.osc[4 * k:4 * k + 4, 0:C], T.sx3[32 * k:32 * k + 4, 0:C]))
+    dma("A", "ool", ["WN"], [], lambda: AC.dma_start(T.ol[:], T.WN[0:128:16, :]))
+    for s, c in cnt.items():
+        if not any(kn.get(s, 0) >= c for kn in known.values()):
+            g.wait_ge(T.sem[s], c)

@@ -4,26 +4,31 @@ from concourse.mybir import dt, AluOpType, ActivationFunctionType
 C = 384
 ROUNDS = 3
 BIG = 2.0 ** 96
-HOLD = 1048576
-DROP = 2 ** 27
-NA = 1
+HOLD = 4096.0
+FOURS = 1.5 * 2.0 ** 25
+REACH = 1.5 * 2.0 ** 34
+MID = 192.5
+PA = 5
+WA = []
 Q8 = "float8_e4m3fn_x4"
 A_ = AluOpType
 FN = ActivationFunctionType
 COPY = FN.Copy
-INTS = "P24 T16 T1 k24 kb kc ic pi pm k1 k3 xi xj L L2 I I2 cx cx2 r r2 oi own y2 rf b1 b2 b3 b4".split()
-FLOATS = "rs RA KA wa fk".split()
-PARTS = {"rs": 24, "e2": 2, "xi": 2, "X1": 2, "M": 2, "zt0": 4, "zt1": 4, "Ce": 3}
-for _i in range(6):
-    PARTS["C%d" % _i] = 4
-PARTS["C5"] = 4 + NA
+INTS = "P24 T16 T1 k24 ic pi k1 k3 rf b1 b2 b3 b4".split()
+FLOATS = "rs rx RA RB KA wa pm pf kf cv I4".split()
+FRONT = 32
+NW = FRONT + 1200 + 132
+ROW = {}
+_p = FRONT
+for _t in range(11, -1, -1):
+    ROW[_t] = _p
+    ROW[_t + 12] = _p + 44
+    _p += 92
+DIAG = {1: _p, 0: _p + 48}
+CHUNKS = [(768 + FRONT, 1200 + FRONT), (288 + FRONT, 768 + FRONT), (96 + FRONT, 288 + FRONT), (0, 96 + FRONT)]
+PARTS = {"X1": 4, "X0": 3, "Y0": 3, "Y1": 3, "c4": 4, "rs": 24, "rx": 12, "kf": 12, "gt": 4, "win": 4}
 for _i in range(1, ROUNDS + 1):
     PARTS["xt%da" % _i] = PARTS["xt%db" % _i] = 4
-
-
-def _ncols(a):
-    return max(128, 64 * (a + 1))
-
 
 SCRATCH = {"LI": ("sbuf", [128, 24 * len(INTS)], "int32"), "LF": ("sbuf", [128, 24 * len(FLOATS)], "float32")}
 
@@ -40,32 +45,28 @@ for _i in range(ROUNDS + 1):
 for _i in range(ROUNDS):
     _sb("land%d" % _i, C, Q8)
     _sb("lans%d" % _i, C, "uint8")
-    _sb("sl%d" % _i, 24, "int32")
-    _sb("al%d" % _i, 24, "int32")
+    _sb("sl%d" % _i, 96, "float16")
+    _sb("al%d" % _i, 96, "float16")
 for _i in range(4):
-    _sb("win%d" % _i, 896, "bfloat16")
     _sb("eq%d" % _i, 128, Q8)
     _sb("es%d" % _i, 128, "uint8")
-for _i in range(6):
-    _sb("C%d" % _i, 4 * _ncols(_i), "bfloat16")
-    _sb("cq%d" % _i, _ncols(_i), Q8)
-    _sb("cs%d" % _i, _ncols(_i), "uint8")
 for _n, _c, _d in (
-        ("Ce", 4 * C, "bfloat16"), ("ceq", C, Q8), ("ces", C, "uint8"), ("sg", NA * C, "bfloat16"),
+        ("Cm", 4 * NW, "bfloat16"), ("cq", NW, Q8), ("cs", NW, "uint8"), ("junk", 4 * NW, "bfloat16"),
+        ("sg", 4 * NW, "bfloat16"), ("win", 8 * C, "bfloat16"), ("xh", 4 * C, "bfloat16"),
         ("ut", 512, "bfloat16"), ("uq", 128, Q8), ("us", 128, "uint8"), ("u16q", 128, Q8), ("u16s", 128, "uint8"),
         ("vt", 512, "bfloat16"), ("vq", 128, Q8), ("vs", 128, "uint8"),
-        ("wq", 512, Q8), ("wsc", 512, "uint8"), ("xh", 4 * C, "bfloat16"), ("et", 520, "bfloat16"),
+        ("wq", 512, Q8), ("wsc", 512, "uint8"), ("et", 520, "bfloat16"),
         ("zt", 4 * C, "bfloat16"), ("zf", 4 * C, "bfloat16"), ("zq", C, Q8), ("zs", C, "uint8"),
-        ("gt0", 512, "bfloat16"), ("gt", 512, "bfloat16"), ("gq", 128, Q8), ("gs", 128, "uint8"),
-        ("zb", 520, "bfloat16"), ("junk", 24 * C, "bfloat16"),
-        ("D", C, "float32"), ("mb", C, "float32"), ("kf", 8, "float32"), ("d0", C, "float32"),
-        ("c2", C, "float32"), ("M", C, "float32"), ("h", C, "float32"), ("U8", 8, "int32"), ("idx", 2, "int32"),
-        ("pP", 24, "uint16"), ("rp", 24, "uint16"), ("upo", 8, "uint16"), ("e1", C, "float32"), ("ru", 24, "uint16"),
-        ("WT", C, "float32"), ("WN", C, "float32"), ("WS", C, "float32"),
+        ("gt", 512, "bfloat16"), ("gq", 128, Q8), ("gs", 128, "uint8"), ("GI", 32, "float32"),
+        ("D", 208, "float32"), ("mb", 192, "float32"), ("d0", 192, "float32"), ("a16", 208, "float32"),
+        ("c16", 192, "float32"), ("c4", C, "float32"), ("rk", 96, "float32"), ("dm", 192, "bfloat16"),
+        ("dg", C, "bfloat16"), ("M", C, "float32"), ("h", C, "float32"), ("U8", 8, "int32"), ("idx", 2, "int32"),
+        ("pP", 24, "uint16"), ("rp", 24, "uint16"), ("upo", 8, "uint16"), ("e1", 96, "float32"), ("ru", 24, "uint16"),
+        ("WT", C, "float32"), ("WN", C, "float32"), ("WS", C, "float32"), ("WC", C, "float32"),
         ("e2", C, "float32"), ("Lu", 24, "uint16"), ("TLW", 768, "float32"), ("e3", C, "float32"),
-        ("e4", C, "float32"), ("tz", 24, "int32"), ("S", C, "float32"),
-        ("X0", 48, "float32"), ("X1", 48, "float32"), ("so", 48, "float32"), ("tl", 24, "uint16"),
-        ("ysb", C, "float32")):
+        ("e4", C, "float32"), ("own", 96, "float32"), ("tz", 96, "float32"), ("tl", 96, "uint16"),
+        ("X0", 96, "float32"), ("X1", 96, "float32"), ("o1", 96, "float32"),
+        ("Y0", 72, "float32"), ("Y1", 72, "float32"), ("so", 72, "float32"), ("ysb", C, "float32")):
     _sb(_n, _c, _d)
 for _i in range(8):
     SCRATCH["P%d" % _i] = ("psum", [128, 512], "float32")
@@ -145,6 +146,9 @@ def rank_program(g, core, T, topo):
         o = 24 * FLOATS.index(name)
         return T.LF[:, o + lo:o + hi]
 
+    def kf(i):
+        return lf("kf", i, i + 1)
+
     def ts(R, W, out, in0, s1, s2, op0, op1=None):
         if op1 is None:
             op("V", R, W, lambda: V.tensor_scalar(out, in0, s1, None, op0))
@@ -157,8 +161,13 @@ def rank_program(g, core, T, topo):
     def cp(R, W, out, a):
         op("V", R, W, lambda: V.tensor_copy(out, a))
 
-    def act(R, W, out, a, scale=None):
-        if scale is None:
+    def ms(W, out, c):
+        op("V", [], W, lambda: V.memset(out, c))
+
+    def act(R, W, out, a, scale=None, bias=None):
+        if bias is not None:
+            op("A", R, W, lambda: AC.activation(out, a, FN.Identity, bias=bias, scale=scale))
+        elif scale is None:
             op("A", R, W, lambda: AC.activation(out, a, COPY))
         else:
             op("A", R, W, lambda: AC.activation(out, a, COPY, scale=scale))
@@ -185,45 +194,63 @@ def rank_program(g, core, T, topo):
     dma("A", "ly", [], ["xt0b"], lambda: AC.dma_start(T.xt0[:, 768:1536], T.x[:, 768:1536]))
     dma("S", "lp", [], ["pi"], lambda: g.sync.dma_start(li("pi"), T.p[:]))
 
+    zb = 4 * (FRONT + 1200)
     op("G", [], ["P24"], lambda: g.iota(li("P24"), [[0, 24]], 0, 1))
-    op("G", [], ["D"], lambda: g.iota(T.D[:], [[0, 24], [1, 16]], 0, 0, allow_small_or_imprecise_dtypes=True))
+    op("G", [], ["D"], lambda: g.iota(T.D[:], [[0, 13], [1, 16]], 0, 0, allow_small_or_imprecise_dtypes=True))
     op("G", [], ["U8"], lambda: g.iota(T.U8[:], [[16, 8]], 0, 0))
     op("G", [], ["T16"], lambda: g.iota(li("T16"), [[16, 24]], 0, 0))
     op("G", [], ["T1"], lambda: g.iota(li("T1"), [[1, 24]], 0, 0))
-    op("V", [], ["zb"], lambda: V.memset(T.zb[:], 0.0))
-    op("V", [], ["rs"], lambda: V.memset(lf("rs"), 0.0))
-    op("V", [], ["X0"], lambda: V.memset(T.X0[:], 0.0))
+    op("G", [], ["GI"], lambda: g.iota(T.GI[:], [[1, 8], [0, 4]], 0, 0, allow_small_or_imprecise_dtypes=True))
+    ms(["zb"], T.Cm[:, zb:4 * NW], 0.0)
+    ms(["gt"], T.gt[:], 0.0)
     ts(["P24"], ["k24"], li("k24"), li("P24"), 15, None, A_.bitwise_and)
     ts(["P24"], ["idx"], T.idx[:, 0:1], li("P24", 0, 1), 4, None, A_.logical_shift_right)
-    cp(["k24"], ["kf"], T.kf[:, 0:1], li("k24", 0, 1))
-    op("G", ["zb"], ["et"], lambda: g.affine_select(T.et[:], T.zb[:, 0:520], [[1, 520]], A_.not_equal, 1.0, -4, -4))
-    op("G", ["zb"], ["gt0"], lambda: g.affine_select(
-        T.gt0[:], T.zb[:, 0:512], [[16, 8], [0, 64]], A_.is_gt, 1.0, 0, -1))
-    op("G", ["gt0"], ["gt"], lambda: g.affine_select(T.gt[:], T.gt0[:], [[16, 8], [0, 64]], A_.is_ge, 0.0, 15, -1))
-    for a in range(6):
-        lo, hi = 256 * a, max(512, 256 * a + 256)
-        act(["zb"], ["C%d" % a], T["C%d" % a][:, lo:hi], T.zb[:, 0:hi - lo])
-    act(["zb"], ["Ce.0"], T.Ce[:, 0:512], T.zb[:, 0:512])
-    ts(["D", "kf"], ["mb"], T.mb[:], T.D[:], T.kf[:, 0:1], BIG, A_.not_equal, A_.mult)
-    ts(["D", "kf"], ["d0"], T.d0[:], T.D[:], T.kf[:, 0:1], BIG, A_.is_equal, A_.mult)
+    ts(["P24"], ["b1"], li("b1", 0, 1), li("P24", 0, 1), 2, 3, A_.logical_shift_right, A_.bitwise_and)
+    ts(["P24"], ["b2"], li("b2", 0, 1), li("P24", 0, 1), 3, None, A_.bitwise_and)
+    ms(["rs", "rx"], lf("rs", 0, 48), 0.0)
+    cp(["k24"], ["kf.0"], kf(0), li("k24", 0, 1))
+    cp(["idx"], ["kf.1"], kf(1), T.idx[:, 0:1])
+    cp(["b1"], ["kf.2"], kf(2), li("b1", 0, 1))
+    cp(["b2"], ["kf.3"], kf(3), li("b2", 0, 1))
+    ms(["front"], T.Cm[:, 0:4 * FRONT], 0.0)
+    op("G", ["zb"], ["et"], lambda: g.affine_select(T.et[:], T.Cm[:, zb:zb + 520], [[1, 520]], A_.not_equal, 1.0, -4, -4))
+    ts(["D", "kf.0"], ["mb"], T.mb[:], T.D[:, 0:192], kf(0), BIG, A_.not_equal, A_.mult)
+    ts(["D", "kf.0"], ["d0"], T.d0[:], T.D[:, 0:192], kf(0), BIG, A_.is_equal, A_.mult)
     cp(["U8"], ["upo"], T.upo[:], T.U8[:])
     tt(["T16", "k24"], ["ic"], li("ic"), li("T16"), li("k24"), A_.add)
-    op("V", [], ["d0"], lambda: V.memset(T.d0[:, 0:C:16], BIG))
-    ts(["k24"], ["kb"], li("kb"), li("k24"), HOLD, None, A_.mult)
-    ts(["ic"], ["pm"], li("pm"), li("ic"), 1024, 524288, A_.mult, A_.add)
+    ms(["d0"], T.d0[:, 0:192:16], BIG)
     ts(["k24"], ["k1"], li("k1"), li("k24"), 24, None, A_.mult)
-    tt(["pm", "pi"], ["wa"], lf("wa"), li("pm"), li("pi"), A_.add)
+    ts(["ic"], ["pm"], lf("pm"), li("ic"), 4.0, 1536 + MID / 256, A_.mult, A_.add)
+    ts(["pi"], ["pf"], lf("pf"), li("pi"), 1.0 / 256, None, A_.mult)
+    ts(["D", "kf.0"], ["a16"], T.a16[:], T.D[:], kf(0), HOLD, A_.is_equal, A_.mult)
+    tt(["pm", "pf"], ["wa"], lf("wa"), lf("pm"), lf("pf"), A_.add)
     dma("S", "dw0", ["wa"], ["wd0"], lambda: g.sync.dma_start(T.wd0[:], lf("wa")))
-    tt(["kb", "T16"], ["kc"], li("kc"), li("T16"), li("kb"), A_.add)
     tt(["k1", "T1"], ["k3"], li("k3"), li("k1"), li("T1"), A_.add)
-    ts(["kb"], ["fk"], lf("fk"), li("kb"), -1, 15 * HOLD + 511, A_.mult, A_.add)
-    ts(["kc"], ["KA"], lf("KA"), li("kc"), -1 - 15 * HOLD, None, A_.add)
+    ts(["D", "kf.2"], ["I4"], lf("I4", 0, 5), T.D[:, 0:5], kf(2), HOLD, A_.is_equal, A_.mult)
+    ts(["kf.3"], ["kf.4"], kf(4), kf(3), HOLD - 1536, None, A_.add)
     cp(["k3"], ["pP"], T.pP[:], li("k3"))
-    ts(["mb"], ["c2"], T.c2[:], T.mb[:], (DROP + HOLD) / BIG, -float(DROP), A_.mult, A_.add)
+    tt(["I4"], ["cv"], lf("cv", 0, 4), lf("I4", 0, 4), lf("I4", 1, 5), A_.subtract)
+    ts(["I4"], ["kf.5"], kf(5), lf("I4", 3, 4), -2 * HOLD, None, A_.add)
     quant(["ut"], ["uq"], T.uq[:, 0:128], T.us[:, 0:128], T.ut[:])
+    for r in range(4):
+        ts(["GI", "kf.1"], ["gt.%d" % r], T.gt[:, 5 * r:512:16], T.GI[:], kf(1), None, A_.is_equal)
     cp(["uq", "upo"], ["u16q"], T.u16q[:, 0:128].bitcast(dt.uint32),
        T.uq[:, 0:128].bitcast(dt.uint32).indirect(T.upo[:, 0:8]))
+    for c in range(2):
+        act(["zb"], ["TLW"] if c else ["TLWa"], T.TLW[:, 384 * c:384 * c + 384], T.Cm[:, zb:zb + 384])
+    act(["zb"], ["X1.3"], T.X1[:, 3:96:4], T.Cm[:, zb:zb + 24])
+    act(["zb"], ["X0"], T.X0[:, 0:96:4], T.Cm[:, zb:zb + 24])
+    for i, c in ((1, -1.0), (2, -1024.0), (3, 4.0 / 3)):
+        act(["zb"], ["X0.%d" % (i - 1)], T.X0[:, i:96:4], T.Cm[:, zb:zb + 24], 1.0, c)
+    act(["zb"], ["Y0"], T.Y0[:], T.Cm[:, zb:zb + 72])
+    act(["zb"], ["Y1"], T.Y1[:], T.Cm[:, zb:zb + 72])
+    act(["zb"], ["dm"], T.dm[:], T.Cm[:, zb:zb + 192], 1.0, 1.0)
+    act(["zb"], ["dm"], T.dm[:, 0:192:16], T.Cm[:, zb:zb + 12])
+    for i in range(4):
+        act(["zb", "cv", "kf.5"], ["c4.%d" % i], T.c4[:, i:C:4], T.Cm[:, zb:zb + 96], 1.0,
+            lf("cv", i, i + 1) if i < 3 else kf(5))
     act(["uq", "upo"], ["u16s"], T.u16s[:, 0:128], T.us[:, 0:128].indirect(T.upo[:, 0:8]))
+    act(["c4"], ["rk", "rk3"], T.rk[:], T.c4[:, 0:96])
     dma("S", "lw", ["xt0a", "xt0b"], ["wq"], lambda: g.sync.dma_start(b8(T.wq[:, 0:512]), T.wc[:]))
     dma("S", "ls", [], ["wsc"], lambda: g.sync.dma_start(T.wsc[:, 0:512], T.ws[:]))
     dma("S", "lv", [], ["vt"], lambda: g.sync.dma_start(T.vt[:], T.v[:]))
@@ -232,170 +259,228 @@ def rank_program(g, core, T, topo):
         dma("G", "ig%d" % i, ["wd%d" % i, "idx"], ["WT"], lambda: g.indirect_dma_start(
             T.WT[:], None, T["wd%d" % i][:], IndirectOffsetOnAxis(ap=T.idx[:, 0:1], axis=0), bounds_check=7))
 
-    spread(0)
+    S0V, S0A, SV, SA, CNT = "P0", "P1", "P2", "P3", "P4"
+    banks = [[0, 1, 2, 3], [4, 5, 6, 7]]
+    DB = [0, 5, 6, 7]
 
-    def scores(t, c):
-        qx, sx, k = T["qx%d" % t], T["sx%d" % t], "P%d" % (2 + c)
+    def quantx(t, c):
         lo, hi = 192 * c, 192 * c + 192
         kq = "qx%d%s" % (t, "ab"[c])
+        qx, sx = T["qx%d" % t], T["sx%d" % t]
         quant(["xt%d%s" % (t, "ab"[c])], [kq], qx[:, lo:hi], sx[:, lo:hi], T["xt%d" % t][:, 4 * lo:4 * hi])
-        if t < ROUNDS:
-            mm(["u16q", "u16s", kq], [k], T[k][:, 0:192], T.u16q[:, 0:128], T.u16s[:, 0:128], qx[:, lo:hi], sx[:, lo:hi])
-            if c == 0:
-                if t == 0:
-                    act(["zb"], ["Ce.1"], T.Ce[:, 512:1024], T.zb[:, 0:512])
-                act([k], ["S0", "turn0"], T.S[:, 0:192], T[k][:, 0:192])
-                if t == 0:
-                    act(["zb"], ["Ce.2"], T.Ce[:, 1024:1536], T.zb[:, 0:512])
-        else:
+        if t == ROUNDS:
+            k = "P%d" % c
             mm(["vq", kq], [k], T[k][:, 0:192], T.vq[:, 0:128], T.vs[:, 0:128], qx[:, lo:hi], sx[:, lo:hi])
+            return
+        for k in ((SV, SA) if c else (S0V, S0A)):
+            mm(["u16q", "u16s", "qx%da" % t, kq], [k], T[k][:, 0:hi], T.u16q[:, 0:128], T.u16s[:, 0:128], qx[:, 0:hi], sx[:, 0:hi])
+
+    def masked(c):
+        k = SV if c else S0V
+        tt([k, "mb"], ["M%d" % c], T.M[:, 192 * c:192 * c + 192], T[k][:, 192 * c:192 * c + 192], T.mb[:], A_.add)
+
+    def held(c):
+        scan(["d0", "M%d" % c], ["h%d" % c], T.h[:, 192 * c:192 * c + 192], T.d0[:], T.M[:, 192 * c:192 * c + 192], BIG,
+             A_.add, A_.min)
+
+    def hcol(j):
+        return T.h[:, 16 * j + 15:16 * j + 16]
+
+    def span(kind, j):
+        if kind == "X":
+            return 4 * ROW[j], 16 * (j + 13), 16 * (11 - j)
+        if kind == "P":
+            return 4 * ROW[j] + 16 * (11 - j), 0, 16 * j
+        return 4 * ROW[j], 16 * (j - 12), 192
+
+    def vrow(kind, j):
+        e, lo, n = span(kind, j)
+        k = S0V if kind == "P" else SV
+        ts([k, "h%d" % (j // 12)], ["C%s%d" % (kind, j)], T.Cm[:, e:e + n], T[k][:, lo:lo + n], hcol(j), None,
+           A_.is_le if kind == "X" else A_.is_lt)
+
+    def sign(kind, j):
+        e, lo, n = span(kind, j)
+        k = S0A if kind == "P" else SA
+        op("A", [k, "h%d" % (j // 12)], ["sg%d" % j], lambda: AC.activation(
+            T.sg[:, e:e + n], T[k][:, lo:lo + n], FN.Sign, bias=hcol(j), scale=-1.0))
+
+    def relu(kind, j):
+        e, lo, n = span(kind, j)
+        op("A", ["sg%d" % j], ["C%s%d" % (kind, j), "rs.%d" % j], lambda: AC.activation(
+            T.Cm[:, e:e + n], T.sg[:, e:e + n], FN.Relu, accum_out=lf("rs", j, j + 1)))
+
+    def total(j):
+        if j >= 12:
+            keys, dst, (e, lo, n) = ["CW%d" % j], "rs", span("W", j)
+        elif j >= PA:
+            keys, dst, (e, lo, n) = ["CX%d" % j], "rx", span("X", j)
+        else:
+            keys, dst, e, n = ["CX%d" % j, "CP%d" % j], "rs", 4 * ROW[j], 176
+        op("A", keys, ["%s.%d" % (dst, j), "junk%d" % j], lambda: AC.activation(
+            T.junk[:, e:e + n], T.Cm[:, e:e + n], COPY, accum_out=lf(dst, j, j + 1)))
+
+    def diag(c):
+        k = SV if c else S0V
+        e = 4 * DIAG[c]
+        tt([k, "h%d" % c], ["CD%d" % c], T.Cm[:, e:e + 192], T[k][:, 192 * c:192 * c + 192], T.h[:, 192 * c:192 * c + 192],
+           A_.is_le)
+
+    def diagsum(c):
+        e = 4 * DIAG[c]
+        scan(["dm", "CD%d" % c], ["dg%d" % c], T.dg[:, 192 * c:192 * c + 192], T.dm[:], T.Cm[:, e:e + 192], 0.0,
+             A_.mult, A_.add)
+
+    pieces = [("front", 0, FRONT), ("CD1", DIAG[1], DIAG[1] + 48), ("CD0", DIAG[0], DIAG[0] + 48)]
+    for j in range(24):
+        for kind in ("W" if j >= 12 else "XP"):
+            e, lo, n = span(kind, j)
+            if n:
+                pieces.append(("C%s%d" % (kind, j), e // 4, (e + n) // 4))
+
+    def count(i):
+        lo, hi = CHUNKS[i]
+        quant([k for k, a, b in pieces if a < hi and b > lo], ["cq%d" % i], T.cq[:, lo:hi], T.cs[:, lo:hi], T.Cm[:, 4 * lo:4 * hi])
+        rows = [a for a in range(FRONT, FRONT + 1200, 96) if lo <= a < hi][::-1]
+        for a in rows:
+            mm(["gq", "cq%d" % i, "cq%d" % (i - 1)], [CNT], T[CNT][:, 0:128], T.gq[:, 0:128], T.gs[:, 0:128],
+               T.cq[:, a:a + 128], T.cs[:, a:a + 128], i == 0 and a == rows[0], i == len(CHUNKS) - 1)
 
     for t in range(ROUNDS):
         xt, qx, sx = T["xt%d" % t], T["qx%d" % t], T["sx%d" % t]
         kx = ["xt%da" % t, "xt%db" % t]
         kq = "qx%d" % t
 
-        def half(b):
-            act(kx, ["winx%d" % b], T["win%d" % b][:, 0:C], xt[:, b:4 * C:4], 2.0 ** -6)
-
         if t == 0:
-            scores(0, 0)
-            scores(0, 1)
+            quantx(0, 0)
+            quantx(0, 1)
+            quant(["gt"], ["gq"], T.gq[:, 0:128], T.gs[:, 0:128], T.gt[:])
+            quant(["zb"], ["cq-1"], T.cq[:, FRONT + 1200:FRONT + 1328], T.cs[:, FRONT + 1200:FRONT + 1328], T.Cm[:, zb:zb + 512])
+            masked(0)
+            tt(["a16"], ["c16"], T.c16[:], T.a16[:, 0:192], T.a16[:, 1:193], A_.subtract)
+            held(0)
         before("G", [kq + "a", kq + "b"], [])
         g.remote_dma(b8(T["land%d" % t][:, 0:C]), b8(qx[:, 0:C]), T.sem["aq%d" % t], T.sem.loc, pid, rid, mask)
         g.remote_dma(T["lans%d" % t][:, 0:C], sx[:, 0:C], T.sem["aq%d" % t], T.sem.loc, pid, rid, mask)
         cnt["loc"] = cnt.get("loc", 0) + 2 * neng
         if t == 0:
+            spread(0)
+            ts(["a16"], ["c16"], T.c16[:, 15:192:16], T.a16[:, 15:192:16], -2 * HOLD, None, A_.add)
+            ts(["k24", "kf.5"], ["KA"], lf("KA", 0, 12), li("k24", 0, 12), kf(5), 176.0, A_.add, A_.add)
+            ts(["k24", "kf.5"], ["KB"], lf("KA", 12, 24), li("k24", 0, 12), kf(5), 192.0, A_.add, A_.add)
+
+        arows = [("P", j) for j in range(11, PA - 1, -1)]
+        sign(*arows[0])
+        for a, b in zip(arows, arows[1:] + [None]):
+            if b:
+                sign(*b)
+            relu(*a)
+
+        diag(0)
+        for j in range(PA - 1, 0, -1):
+            vrow("P", j)
+        masked(1)
+        vrow("X", 0)
+        total(0)
+        held(1)
+        for j in WA:
+            sign("W", j)
+        for j in WA:
+            relu("W", j)
+        diagsum(0)
+        for j in range(1, 11):
+            vrow("X", j)
+            total(j)
+        diag(1)
+        if t == 0:
             for b in range(4):
                 quant(["et"], ["eq%d" % b], T["eq%d" % b][:, 0:128], T["es%d" % b][:, 0:128], T.et[:, 4 - b:516 - b])
-        tt(["P2", "mb", "turn0"], ["M.0"], T.M[:, 0:192], T.P2[:, 0:192], T.mb[:, 0:192], A_.add)
-        tt(["P3", "mb"], ["M.1", "turn1"], T.M[:, 192:384], T.P3[:, 0:192], T.mb[:, 192:384], A_.add)
-        act(["P3", "turn1"], ["S1"], T.S[:, 192:384], T.P3[:, 0:192])
-        scan(["d0", "M"], ["h"], T.h[:], T.d0[:], T.M[:], BIG, A_.add, A_.min)
-
-        for n in range(NA):
-            b = 3 - n
-            w = 16 * (20 + b)
-            op("A", ["S0", "S1", "h"], ["sg%d" % n], lambda: AC.activation(
-                T.sg[:, C * n:C * n + w], T.S[:, 0:w], FN.Sign, bias=T.h[:, w + 15:w + 16], scale=-1.0))
-            op("A", ["sg%d" % n], ["C5.%d" % (4 + n), "rs.%d" % (20 + b)], lambda: AC.activation(
-                T.C5[:, b:4 * w:4], T.sg[:, C * n:C * n + w], FN.Relu, accum_out=lf("rs", 20 + b, 21 + b)))
-
-        def compare(a):
-            Ct = T["C%d" % a]
-            mine = [b for b in (3, 2, 1, 0) if a < 5 or b < 4 - NA]
-            for b in mine + [b for b in (3, 2, 1, 0) if b not in mine]:
-                w = 16 * (4 * a + b) + 16
-                lo = 0 if b in mine else w - 16
-                ts(["S0", "S1", "h"], ["C%d.%d" % (a, b)], Ct[:, 4 * lo + b:4 * w:4], T.S[:, lo:w], T.h[:, w - 1:w], None,
-                   A_.is_lt)
-            for b in mine:
-                j = 4 * a + b
-                if j:
-                    op("A", ["C%d.%d" % (a, b)], ["rs.%d" % j, "junk%d" % j], lambda: AC.activation(
-                        T.junk[:, C * j:C * j + 16 * j], Ct[:, b:64 * j:4], COPY, accum_out=lf("rs", j, j + 1)))
-
-        def count(a, start=False, stop=False):
-            n = _ncols(a)
-            quant(["C%d" % a], ["cq%d" % a], T["cq%d" % a][:, 0:n], T["cs%d" % a][:, 0:n], T["C%d" % a][:, 0:4 * n])
-            mm(["gq", "cq%d" % a], ["P1"], T.P1[:, 0:n], T.gq[:, 0:128], T.gs[:, 0:128],
-               T["cq%d" % a][:, 0:n], T["cs%d" % a][:, 0:n], start, stop)
-
-        compare(5)
-        if t == 0:
-            quant(["gt"], ["gq"], T.gq[:, 0:128], T.gs[:, 0:128], T.gt[:])
-        compare(4)
-        count(5, start=True)
-        compare(3)
-        count(4)
-        for c in range(2):
-            lo, hi = 192 * c, 192 * c + 192
-            tt(["h", "P%d" % (2 + c), "S%d" % c], ["Ce.%d" % (2 * c), "eqs%d" % c] + (["Ce.1"] if c == 0 else []),
-               T.Ce[:, 4 * lo:4 * hi:4], T.h[:, lo:hi], T["P%d" % (2 + c)][:, 0:192], A_.is_equal)
-        count(3)
-        compare(2)
-        quant(["Ce", "eqs0", "eqs1"], ["ceq"], T.ceq[:, 0:C], T.ces[:, 0:C], T.Ce[:])
-        mm(["gq", "ceq"], ["P1"], T.P1[:, 0:C], T.gq[:, 0:128], T.gs[:, 0:128], T.ceq[:, 0:C], T.ces[:, 0:C], False, False)
-        compare(1)
+        for j in range(12, 24):
+            if j not in WA:
+                vrow("W", j)
+                total(j)
+            if j == 12:
+                diagsum(1)
+            if j == 16:
+                count(0)
+            if j == 17:
+                tt(["KA", "KB", "dg0", "dg1"], ["RA"], lf("RA"), lf("KA"), T.dg[:, 15:C:16], A_.subtract)
+            if j == 19:
+                tt(["RA", "rx"], ["RB"], lf("RB"), lf("RA"), lf("rx"), A_.subtract)
+            if j == 21:
+                count(1)
         count(2)
-        compare(0)
-        count(1)
-        count(0, stop=True)
-        k = "rp" if t else "pP"
-        act(["WT", k], ["WN"], T.WN[:], T.WT[:, 0:C].indirect(T[k][:, 0:24]))
-        for c in range(2):
-            act(["zb"], ["TLW"] if c else ["TLWa"], T.TLW[:, 384 * c:384 * c + 384], T.zb[:, 0:384])
+        count(3)
+        if t == 0:
+            act(["WT", "pP"], ["WN"], T.WN[:], T.WT[:, 0:C].indirect(T.pP[:, 0:24]), 1.0, -(MID + C) / 256)
         for b in range(4):
-            half(b)
-            if t == 0:
-                act(["zb"], ["gap%d" % b], T["win%d" % b][:, 384:512], T.zb[:, 0:128])
-        act(kx, ["xh"], T.xh[:], xt[:], 2.0 ** -6)
-        for b in range(4):
-            mm(["eq%d" % b, "land%d" % t], ["P%d" % (4 + b)], T["P%d" % (4 + b)][:, 0:C], T["eq%d" % b][:, 0:128],
+            k = "P%d" % DB[b]
+            mm(["eq%d" % b, "land%d" % t], [k], T[k][:, 0:C], T["eq%d" % b][:, 0:128],
                T["es%d" % b][:, 0:128], T["land%d" % t][:, 0:C], T["lans%d" % t][:, 0:C])
+        act(kx, ["xw"], T.win[:, 0:4 * C], xt[:], 2.0 ** -6)
         for b in range(4):
-            act(["P%d" % (4 + b)], ["wind%d" % b], T["win%d" % b][:, 512:896], T["P%d" % (4 + b)][:, 0:C], 2.0 ** -6)
-        tt(["KA", "rs"], ["RA"], lf("RA"), lf("KA"), lf("rs"), A_.subtract)
-        scan(["c2", "P1"], ["e1"], T.e1[:], T.c2[:], T.P1[:, 0:C], 0.0, A_.add, A_.max)
-        tt(["e1", "RA"], ["rf"], li("rf"), T.e1[:, 15:C:16], lf("RA"), A_.add)
-        cp(["rf"], ["ru"], T.ru[:], li("rf"))
+            k = "P%d" % DB[b]
+            act([k], ["win.%d" % b], T.win[:, 4 * C + b:8 * C:4], T[k][:, 0:C], 2.0 ** -6)
+        act(kx, ["xh"], T.xh[:], xt[:], 2.0 ** -6)
+        tt(["RB", "rs"], ["rk3"], T.rk[:, 3:96:4], lf("RB"), lf("rs"), A_.subtract)
+        scan([CNT, "rk", "rk3"], ["e1"], T.e1[:], T[CNT][:, 0:96], T.rk[:], 0.0, A_.max, A_.add)
+        ts(["e1"], ["ru"], T.ru[:], T.e1[:, 3:96:4], HOLD, None, A_.add)
         cp(["ru", "WN"], ["WS"], T.WS[:, 0:C].indirect(T.ru[:, 0:24]), T.WN[:])
-        scan(["c2", "WS"], ["e2.0"], T.e2[:, 0:192], T.c2[:, 0:192], T.WS[:, 0:C:2], 0.0, A_.add, A_.max)
-        scan(["c2", "WS"], ["e2.1"], T.e2[:, 192:384], T.c2[:, 0:192], T.WS[:, 1:C:2], 0.0, A_.add, A_.max)
-        cp(["e2"], ["xi.0"], li("xi"), T.e2[:, 15:C:16])
-        cp(["e2"], ["xi.1"], li("xj"), T.e2[:, 15:C:16])
-        ts(["xi"], ["L"], li("L", 0, 48), li("xi", 0, 48), 1023, None, A_.bitwise_and)
-        ts(["xi"], ["I"], li("I", 0, 36), li("xi", 0, 36), 10, 511, A_.logical_shift_right, A_.bitwise_and)
-        tt(["L", "I"], ["cx"], li("cx", 0, 36), li("L", 12, 48), li("I", 0, 36), A_.subtract)
-        tt(["L"], ["X1.0"], T.X1[:, 0:48:2], li("L", 12, 36), li("L", 0, 24), A_.subtract)
-        ts(["cx"], ["r"], li("r", 0, 36), li("cx", 0, 36), -191.5, 1.0 / 384, A_.add, A_.mult)
-        cp(["L"], ["X1.1"], T.X1[:, 1:48:2], li("L"))
-        tt(["r"], ["X0"], T.X0[:, 1:48:2], li("r", 0, 24), li("r", 12, 36), A_.is_equal)
-        scan(["X0", "X1"], ["so"], T.so[:], T.X0[:], T.X1[:], 0.0, A_.mult, A_.add)
-        cp(["so"], ["Lu"], T.Lu[:], T.so[:, 1:48:2])
+        for c in range(2):
+            scan(["c16", "WS"], ["e2%d" % c], T.e2[:, 192 * c:192 * c + 192], T.WS[:, c:C:2], T.c16[:], 0.0, A_.max, A_.add)
+        ts(["WS"], ["WC0"], T.WC[:, 0:192], T.WS[:, 0:C:2], FOURS, FOURS, A_.add, A_.subtract)
+        ts(["e20"], ["X1.2"], T.X1[:, 50:96:4], T.e2[:, 15:192:16], FOURS + HOLD, FOURS, A_.add, A_.subtract)
+        ts(["e21"], ["X1b"], T.X1[:, 2:48:4], T.e2[:, 207:C:16], FOURS + HOLD, FOURS, A_.add, A_.subtract)
+        ts(["e20", "e21"], ["X1.0"], T.X1[:, 0:96:4], T.e2[:, 15:C:16], FOURS + HOLD, FOURS, A_.add, A_.subtract)
+        ts(["e20", "e21"], ["X1.1"], T.X1[:, 1:96:4], T.e2[:, 15:C:16], HOLD + (MID + C) / 256, None, A_.add)
+        ts(["WS"], ["WC1"], T.WC[:, 192:C], T.WS[:, 1:C:2], FOURS, FOURS, A_.add, A_.subtract)
+        scan(["X0", "X1", "X1b"], ["o1"], T.o1[:], T.X0[:], T.X1[:], 0.0, A_.mult, A_.add)
+        ts(["o1"], ["Y0.0"], T.Y0[:, 1:72:3], T.o1[:, 3:96:4], REACH, REACH, A_.add, A_.is_equal)
+        ts(["o1"], ["Y0.1"], T.Y0[:, 2:36:3], T.o1[:, 51:96:4], REACH, REACH, A_.add, A_.is_equal)
+        ts(["o1"], ["Y0.2"], T.Y0[:, 38:72:3], T.o1[:, 3:48:4], REACH, REACH, A_.add, A_.is_equal)
+        tt(["o1"], ["Y1.0"], T.Y1[:, 0:36:3], T.o1[:, 49:96:4], T.o1[:, 1:48:4], A_.subtract)
+        tt(["o1"], ["Y1.1"], T.Y1[:, 36:72:3], T.o1[:, 1:48:4], T.o1[:, 49:96:4], A_.subtract)
+        cp(["o1"], ["Y1.2"], T.Y1[:, 2:72:3], T.o1[:, 1:96:4])
+        scan(["Y0", "Y1"], ["so"], T.so[:], T.Y0[:], T.Y1[:], 0.0, A_.mult, A_.add)
+        ts(["so"], ["Lu"], T.Lu[:], T.so[:, 2:72:3], 256.0, -MID, A_.mult, A_.add)
         kw = "wd%d" % (t + 1)
         if t == ROUNDS - 1:
-            cp(["so"], ["wa"], lf("wa"), T.so[:, 1:48:2])
-            dma("S", "dw%d" % (t + 1), ["wa"], [kw], lambda: g.sync.dma_start(T[kw][:], lf("wa")))
-        cp(["Lu", "WS"], ["TLW", "TLWa"], T.TLW[:, 0:768].indirect(T.Lu[:, 0:12]), T.WS[:, 0:C:2])
-        cp(["Lu", "WS"], ["TLW", "TLWa"], T.TLW[:, 0:768].indirect(T.Lu[:, 12:24]), T.WS[:, 1:C:2])
-        scan(["c2", "TLW"], ["e3"], T.e3[:], T.c2[:], T.TLW[:, 384:768], 0.0, A_.add, A_.max)
+            ts(["so"], ["wa"], lf("wa"), T.so[:, 2:72:3], 256.0, -MID, A_.mult, A_.add)
+        else:
+            tt(["so", "X1.0"], ["wa"], lf("wa"), T.so[:, 2:72:3], T.X1[:, 0:96:4], A_.add)
+        dma("S", "dw%d" % (t + 1), ["wa"], [kw], lambda: g.sync.dma_start(T[kw][:], lf("wa")))
+        cp(["Lu", "WC0", "WC1"], ["TLW", "TLWa"], T.TLW[:, 0:768].indirect(T.Lu[:, 0:24]), T.WC[:])
+        scan(["c4", "TLW"], ["e3"], T.e3[:], T.TLW[:, 384:768], T.c4[:], 0.0, A_.max, A_.add)
         ksl = "sl%d" % t
-        ts(["e3", "fk"], [ksl], T[ksl][:], T.e3[:, 15:C:16], lf("fk", 0, 1), 2.0 ** -10, A_.subtract, A_.mult)
+        ts(["e3"], [ksl], T[ksl][:], T.e3[:, 3:C:4], HOLD, None, A_.add)
         before("G", [ksl], [])
         g.remote_dma(T["al%d" % t][:], T[ksl][:], T.sem["al%d" % t], T.sem.loc, pid, rid, mask)
         cnt["loc"] += neng
-        scan(["c2", "TLW", "TLWa"], ["e4"], T.e4[:], T.c2[:], T.TLW[:, 0:384], 0.0, A_.add, A_.max)
-        if t < ROUNDS - 1:
-            ts(["xi"], ["y2"], li("y2"), li("xi"), 1023 * 1024, None, A_.bitwise_and)
-        cp(["e4"], ["oi"], li("oi"), T.e4[:, 15:C:16])
-        if t < ROUNDS - 1:
-            tt(["so", "y2"], ["wa"], lf("wa"), T.so[:, 1:48:2], li("y2"), A_.add)
-        ts(["oi"], ["own"], li("own"), li("oi"), 10, 511, A_.logical_shift_right, A_.bitwise_and)
-        if t < ROUNDS - 1:
-            dma("S", "dw%d" % (t + 1), ["wa"], [kw], lambda: g.sync.dma_start(T[kw][:], lf("wa")))
         spread(t + 1)
+        scan(["c4", "TLW", "TLWa"], ["e4"], T.e4[:], T.TLW[:, 0:384], T.c4[:], 0.0, A_.max, A_.add)
+        if t == 0:
+            quant(["vt"], ["vq"], T.vq[:, 0:128], T.vs[:, 0:128], T.vt[:])
+        ts(["e1"], ["rf"], li("rf"), T.e1[:, 3:96:4], HOLD, None, A_.add)
+        ts(["e4", "kf.3", "kf.4"], ["own"], T.own[:], T.e4[:, 3:C:4], kf(4), kf(3), A_.add, A_.max)
         ts(["rf"], ["b1"], li("b1"), li("rf"), 31, None, A_.bitwise_and)
         ts(["rf"], ["b2"], li("b2"), li("rf"), 5, None, A_.logical_shift_right)
         ts(["b1"], ["b3"], li("b3"), li("b1"), 12, None, A_.mult)
         tt(["b3", "b2"], ["b4"], li("b4"), li("b3"), li("b2"), A_.add)
         cp(["b4"], ["rp"], T.rp[:], li("b4"))
-        if t == 0:
-            quant(["vt"], ["vq"], T.vq[:, 0:128], T.vs[:, 0:128], T.vt[:])
-        tt(["own", "al%d" % t], ["tz"], T.tz[:], li("own"), T["al%d" % t][:], A_.add)
-        cp(["tz"], ["tl"], T.tl[:], T.tz[:])
-        banks = [[2, 3, 4, 5], [6, 7, 0, 1]]
+        for c in range(2):
+            tt(["own", "al%d" % t], ["tz%d" % c], T.tz[:, 48 * c:48 * c + 48], T.own[:, 48 * c:48 * c + 48],
+               T["al%d" % t][:, 48 * c:48 * c + 48], A_.add)
+        for c in range(2):
+            cp(["tz%d" % c], ["tl%d" % c], T.tl[:, 48 * c:48 * c + 48], T.tz[:, 48 * c:48 * c + 48])
 
-        def catch(c, b):
-            lo, hi = 192 * c, 192 * c + 192
-            tt(["winx%d" % b, "gap%d" % b, "wind%d" % b, "xh", "tl"], ["zt%d.%d" % (c, b)],
-               T.zt[:, 4 * lo + b:4 * hi:4], T["win%d" % b][:, 0:896].indirect(T.tl[:, 12 * c:12 * c + 12]),
-               T.xh[:, 4 * lo + b:4 * hi:4], A_.add)
+        def catch(lo, hi, k):
+            tt(["win", "xw", "xh", "tl%d" % (lo // 192)], [k], T.zt[:, 4 * lo:4 * hi],
+               T.win[:, 0:8 * C].indirect(T.tl[:, lo // 4:hi // 4]), T.xh[:, 4 * lo:4 * hi], A_.add)
 
-        def layer(c):
+        def layer(c, keys):
             lo, hi = 192 * c, 192 * c + 192
-            quant(["zt%d" % c], ["zq%d" % c], T.zq[:, lo:hi], T.zs[:, lo:hi], T.zt[:, 4 * lo:4 * hi])
-            act(["zt%d" % c], ["zf%d" % c], T.zf[:, 4 * lo:4 * hi], T.zt[:, 4 * lo:4 * hi], 32.0)
+            quant(keys, ["zq%d" % c], T.zq[:, lo:hi], T.zs[:, lo:hi], T.zt[:, 4 * lo:4 * hi])
+            act(keys, ["zf%d" % c], T.zf[:, 4 * lo:4 * hi], T.zt[:, 4 * lo:4 * hi], 32.0)
             for b in range(4):
                 k = "P%d" % banks[c][b]
                 mm(["wq", "wsc", "zq%d" % c], [k], T[k][:, 0:192], T.wq[:, 128 * b:128 * b + 128],
@@ -407,26 +492,38 @@ def rank_program(g, core, T, topo):
             tt([k, "zf%d" % c], ["xt%d%s.%d" % (t + 1, "ab"[c], b)], T["xt%d" % (t + 1)][:, 4 * lo + b:4 * hi:4],
                T[k][:, 0:192], T.zf[:, 4 * lo + b:4 * hi:4], A_.add)
 
-        for f, done in ((catch, layer), (state, lambda c: scores(t + 1, c))):
-            for b in range(4):
-                f(0, b)
-            f(1, 0)
-            done(0)
-            for b in range(1, 4):
-                f(1, b)
-            done(1)
+        catch(0, 192, "zt0")
+        catch(192, 256, "zt1")
+        layer(0, ["zt0"])
+        catch(256, 384, "zt2")
+        state(0, 0)
+        layer(1, ["zt1", "zt2"])
+        if t < ROUNDS - 1:
+            act(["WT", "rp"], ["WN"], T.WN[:], T.WT[:, 0:C].indirect(T.rp[:, 0:24]), 1.0, -(MID + C) / 256)
+        else:
+            act(["WT", "rp"], ["WN"], T.WN[:], T.WT[:, 0:C].indirect(T.rp[:, 0:24]))
+        for b in range(1, 4):
+            state(0, b)
+        state(1, 0)
+        quantx(t + 1, 0)
+        for b in range(1, 4):
+            state(1, b)
+        if t < ROUNDS - 1:
+            masked(0)
+        quantx(t + 1, 1)
+        if t < ROUNDS - 1:
+            held(0)
 
-    act(["P2"], ["ysb0"], T.ysb[:, 0:192], T.P2[:, 0:192])
-    cp(["P3"], ["ysb1"], T.ysb[:, 192:384], T.P3[:, 0:192])
+    dma("A", "ool", ["WN"], [], lambda: AC.dma_start(T.ol[:], T.WN[0:128:16, :]))
+    act(["P0"], ["ysb0"], T.ysb[:, 0:192], T.P0[:, 0:192])
+    cp(["P1"], ["ysb1"], T.ysb[:, 192:384], T.P1[:, 0:192])
     dma("S", "oc0", ["qx3a"], [], lambda: g.sync.dma_start(T.oc[:, 0:768], b8(T.qx3[:, 0:192])))
     dma("A", "oy0", ["ysb0"], [], lambda: AC.dma_start(T.y[:, 0:192], T.ysb[:, 0:192]))
     dma("S", "oc1", ["qx3b"], [], lambda: g.sync.dma_start(T.oc[:, 768:1536], b8(T.qx3[:, 192:384])))
-    act(["WT", "rp"], ["WN"], T.WN[:], T.WT[:, 0:C].indirect(T.rp[:, 0:24]))
-    dma("S", "oy1", ["ysb1"], [], lambda: g.sync.dma_start(T.y[:, 192:384], T.ysb[:, 192:384]))
     for k in range(4):
-        dma("S", "oos%d" % k, ["qx3a", "qx3b"], [], lambda: g.sync.dma_start(
+        dma("A" if k % 2 else "S", "oos%d" % k, ["qx3a", "qx3b"], [], lambda: (AC if k % 2 else g.sync).dma_start(
             T.osc[4 * k:4 * k + 4, 0:C], T.sx3[32 * k:32 * k + 4, 0:C]))
-    dma("A", "ool", ["WN"], [], lambda: AC.dma_start(T.ol[:], T.WN[0:128:16, :]))
+    dma("S", "oy1", ["ysb1"], [], lambda: g.sync.dma_start(T.y[:, 192:384], T.ysb[:, 192:384]))
     for s, c in cnt.items():
         if not any(kn.get(s, 0) >= c for kn in known.values()):
             g.wait_ge(T.sem[s], c)

@@ -8,24 +8,29 @@ HOLD = 4096.0
 FOURS = 1.5 * 2.0 ** 25
 REACH = 1.5 * 2.0 ** 34
 MID = 192.5
-PA = 5
-WA = []
 Q8 = "float8_e4m3fn_x4"
 A_ = AluOpType
 FN = ActivationFunctionType
 COPY = FN.Copy
 INTS = "P24 T16 T1 k24 ic pi k1 k3 rf b1 b2 b3 b4".split()
 FLOATS = "rs rx RA RB KA wa pm pf kf cv I4".split()
-FRONT = 32
-NW = FRONT + 1200 + 132
+NW = 1200 + 132
 ROW = {}
-_p = FRONT
+_p = 0
 for _t in range(11, -1, -1):
     ROW[_t] = _p
     ROW[_t + 12] = _p + 44
     _p += 92
 DIAG = {1: _p, 0: _p + 48}
-CHUNKS = [(768 + FRONT, 1200 + FRONT), (288 + FRONT, 768 + FRONT), (96 + FRONT, 288 + FRONT), (0, 96 + FRONT)]
+CHUNKS = [(772, 1200), (488, 772), (0, 236), (236, 488)]
+FOLDS = {0: "P5", 1: "P6", 2: "P7"}
+VORD = "g0 c0 c1 Z0 c2 c3 y00 Z1 y03 y01 y02 y10 q0 y11 y12 y13 M0 q1 H0 P6 D0 M1 P4 X3 H1 X9 X0 X6 P1 X10 X1 W12 X7 X2 X5 P7 P5 D1 W15 P3 X8 S1 W14 P2 W13 W18 Q0 P8 W16 S0 X4 RA Q1 W19 Q2 RB Q3".split()
+AORD = "g1 g2 g3 g4 f0 f1 f2 f3 N0 s11 s9 s10 r9 r11 s20 s23 r10 s21 r23 s17 t7 r21 t3 s22 t10 r20 r17 t6 r22 t8 u2 u1 u13 u15 u12 t9 u0 u16 u4 t19 u5 u18 u14".split()
+VEND = "g0 c0 c1 Z0 c2 c3 y00 Z1 y01 y02 y03 y10 q0 y11 y12 y13 q1".split()
+AEND = "g1 g2 g3 g4 f0 f1 f2 f3 N0".split()
+JOIN = ["g4", "c3", "f3"]
+OWN = [("xh0", 0, 96), ("xh1", 96, 192), ("xh2", 192, 256), ("xh3", 256, 320), ("xh4", 320, C)]
+LAST = 256
 PARTS = {"X1": 4, "X0": 3, "Y0": 3, "Y1": 3, "c4": 4, "rs": 24, "rx": 12, "kf": 12, "gt": 4, "win": 4}
 for _i in range(1, ROUNDS + 1):
     PARTS["xt%da" % _i] = PARTS["xt%db" % _i] = 4
@@ -45,14 +50,15 @@ for _i in range(ROUNDS + 1):
 for _i in range(ROUNDS):
     _sb("land%d" % _i, C, Q8)
     _sb("lans%d" % _i, C, "uint8")
-    _sb("sl%d" % _i, 96, "float16")
-    _sb("al%d" % _i, 96, "float16")
+    _sb("sl%d" % _i, 96, "uint16")
+    _sb("al%d" % _i, 96, "uint16")
 for _i in range(4):
     _sb("eq%d" % _i, 128, Q8)
     _sb("es%d" % _i, 128, "uint8")
 for _n, _c, _d in (
         ("Cm", 4 * NW, "bfloat16"), ("cq", NW, Q8), ("cs", NW, "uint8"), ("junk", 4 * NW, "bfloat16"),
         ("sg", 4 * NW, "bfloat16"), ("win", 8 * C, "bfloat16"), ("xh", 4 * C, "bfloat16"),
+        ("it", 512, "bfloat16"), ("iq", 128, Q8), ("isc", 128, "uint8"),
         ("ut", 512, "bfloat16"), ("uq", 128, Q8), ("us", 128, "uint8"), ("u16q", 128, Q8), ("u16s", 128, "uint8"),
         ("vt", 512, "bfloat16"), ("vq", 128, Q8), ("vs", 128, "uint8"),
         ("wq", 512, Q8), ("wsc", 512, "uint8"), ("et", 520, "bfloat16"),
@@ -64,7 +70,7 @@ for _n, _c, _d in (
         ("pP", 24, "uint16"), ("rp", 24, "uint16"), ("upo", 8, "uint16"), ("e1", 96, "float32"), ("ru", 24, "uint16"),
         ("WT", C, "float32"), ("WN", C, "float32"), ("WS", C, "float32"), ("WC", C, "float32"),
         ("e2", C, "float32"), ("Lu", 24, "uint16"), ("TLW", 768, "float32"), ("e3", C, "float32"),
-        ("e4", C, "float32"), ("own", 96, "float32"), ("tz", 96, "float32"), ("tl", 96, "uint16"),
+        ("e4", C, "float32"), ("tl", 96, "uint16"),
         ("X0", 96, "float32"), ("X1", 96, "float32"), ("o1", 96, "float32"),
         ("Y0", 72, "float32"), ("Y1", 72, "float32"), ("so", 72, "float32"), ("ysb", C, "float32")):
     _sb(_n, _c, _d)
@@ -194,7 +200,7 @@ def rank_program(g, core, T, topo):
     dma("A", "ly", [], ["xt0b"], lambda: AC.dma_start(T.xt0[:, 768:1536], T.x[:, 768:1536]))
     dma("S", "lp", [], ["pi"], lambda: g.sync.dma_start(li("pi"), T.p[:]))
 
-    zb = 4 * (FRONT + 1200)
+    zb = 4 * 1200
     op("G", [], ["P24"], lambda: g.iota(li("P24"), [[0, 24]], 0, 1))
     op("G", [], ["D"], lambda: g.iota(T.D[:], [[0, 13], [1, 16]], 0, 0, allow_small_or_imprecise_dtypes=True))
     op("G", [], ["U8"], lambda: g.iota(T.U8[:], [[16, 8]], 0, 0))
@@ -212,7 +218,7 @@ def rank_program(g, core, T, topo):
     cp(["idx"], ["kf.1"], kf(1), T.idx[:, 0:1])
     cp(["b1"], ["kf.2"], kf(2), li("b1", 0, 1))
     cp(["b2"], ["kf.3"], kf(3), li("b2", 0, 1))
-    ms(["front"], T.Cm[:, 0:4 * FRONT], 0.0)
+    op("G", ["zb"], ["it"], lambda: g.affine_select(T.it[:], T.Cm[:, zb:zb + 512], [[1, 128], [0, 4]], A_.not_equal, 1.0, 0, -1))
     op("G", ["zb"], ["et"], lambda: g.affine_select(T.et[:], T.Cm[:, zb:zb + 520], [[1, 520]], A_.not_equal, 1.0, -4, -4))
     ts(["D", "kf.0"], ["mb"], T.mb[:], T.D[:, 0:192], kf(0), BIG, A_.not_equal, A_.mult)
     ts(["D", "kf.0"], ["d0"], T.d0[:], T.D[:, 0:192], kf(0), BIG, A_.is_equal, A_.mult)
@@ -221,23 +227,28 @@ def rank_program(g, core, T, topo):
     ms(["d0"], T.d0[:, 0:192:16], BIG)
     ts(["k24"], ["k1"], li("k1"), li("k24"), 24, None, A_.mult)
     ts(["ic"], ["pm"], lf("pm"), li("ic"), 4.0, 1536 + MID / 256, A_.mult, A_.add)
-    ts(["pi"], ["pf"], lf("pf"), li("pi"), 1.0 / 256, None, A_.mult)
     ts(["D", "kf.0"], ["a16"], T.a16[:], T.D[:], kf(0), HOLD, A_.is_equal, A_.mult)
-    tt(["pm", "pf"], ["wa"], lf("wa"), lf("pm"), lf("pf"), A_.add)
-    dma("S", "dw0", ["wa"], ["wd0"], lambda: g.sync.dma_start(T.wd0[:], lf("wa")))
     tt(["k1", "T1"], ["k3"], li("k3"), li("k1"), li("T1"), A_.add)
     ts(["D", "kf.2"], ["I4"], lf("I4", 0, 5), T.D[:, 0:5], kf(2), HOLD, A_.is_equal, A_.mult)
     ts(["kf.3"], ["kf.4"], kf(4), kf(3), HOLD - 1536, None, A_.add)
+    ts(["kf.3"], ["kf.6"], kf(6), kf(3), HOLD, None, A_.add)
     cp(["k3"], ["pP"], T.pP[:], li("k3"))
     tt(["I4"], ["cv"], lf("cv", 0, 4), lf("I4", 0, 4), lf("I4", 1, 5), A_.subtract)
     ts(["I4"], ["kf.5"], kf(5), lf("I4", 3, 4), -2 * HOLD, None, A_.add)
-    quant(["ut"], ["uq"], T.uq[:, 0:128], T.us[:, 0:128], T.ut[:])
+    tt(["a16"], ["c16"], T.c16[:], T.a16[:, 0:192], T.a16[:, 1:193], A_.subtract)
     for r in range(4):
         ts(["GI", "kf.1"], ["gt.%d" % r], T.gt[:, 5 * r:512:16], T.GI[:], kf(1), None, A_.is_equal)
+    ts(["a16"], ["c16"], T.c16[:, 15:192:16], T.a16[:, 15:192:16], -2 * HOLD, None, A_.add)
+    ts(["k24", "kf.5"], ["KA"], lf("KA", 0, 12), li("k24", 0, 12), kf(5), 176.0, A_.add, A_.add)
+    ts(["k24", "kf.5"], ["KB"], lf("KA", 12, 24), li("k24", 0, 12), kf(5), 192.0, A_.add, A_.add)
+    quant(["zb"], ["cqz"], T.cq[:, 1200:1328], T.cs[:, 1200:1328], T.Cm[:, zb:zb + 512])
+    quant(["gt"], ["gq"], T.gq[:, 0:128], T.gs[:, 0:128], T.gt[:])
+    ts(["pi"], ["pf"], lf("pf"), li("pi"), 1.0 / 256, None, A_.mult)
+    quant(["ut"], ["uq"], T.uq[:, 0:128], T.us[:, 0:128], T.ut[:])
+    tt(["pm", "pf"], ["wa"], lf("wa"), lf("pm"), lf("pf"), A_.add)
+    dma("S", "dw0", ["wa"], ["wd0"], lambda: g.sync.dma_start(T.wd0[:], lf("wa")))
     cp(["uq", "upo"], ["u16q"], T.u16q[:, 0:128].bitcast(dt.uint32),
        T.uq[:, 0:128].bitcast(dt.uint32).indirect(T.upo[:, 0:8]))
-    for c in range(2):
-        act(["zb"], ["TLW"] if c else ["TLWa"], T.TLW[:, 384 * c:384 * c + 384], T.Cm[:, zb:zb + 384])
     act(["zb"], ["X1.3"], T.X1[:, 3:96:4], T.Cm[:, zb:zb + 24])
     act(["zb"], ["X0"], T.X0[:, 0:96:4], T.Cm[:, zb:zb + 24])
     for i, c in ((1, -1.0), (2, -1024.0), (3, 4.0 / 3)):
@@ -249,8 +260,8 @@ def rank_program(g, core, T, topo):
     for i in range(4):
         act(["zb", "cv", "kf.5"], ["c4.%d" % i], T.c4[:, i:C:4], T.Cm[:, zb:zb + 96], 1.0,
             lf("cv", i, i + 1) if i < 3 else kf(5))
-    act(["uq", "upo"], ["u16s"], T.u16s[:, 0:128], T.us[:, 0:128].indirect(T.upo[:, 0:8]))
     act(["c4"], ["rk", "rk3"], T.rk[:], T.c4[:, 0:96])
+    act(["uq", "upo"], ["u16s"], T.u16s[:, 0:128], T.us[:, 0:128].indirect(T.upo[:, 0:8]))
     dma("S", "lw", ["xt0a", "xt0b"], ["wq"], lambda: g.sync.dma_start(b8(T.wq[:, 0:512]), T.wc[:]))
     dma("S", "ls", [], ["wsc"], lambda: g.sync.dma_start(T.wsc[:, 0:512], T.ws[:]))
     dma("S", "lv", [], ["vt"], lambda: g.sync.dma_start(T.vt[:], T.v[:]))
@@ -263,14 +274,18 @@ def rank_program(g, core, T, topo):
     banks = [[0, 1, 2, 3], [4, 5, 6, 7]]
     DB = [0, 5, 6, 7]
 
+    def run(t, c):
+        m = LAST if t == ROUNDS else 192
+        return (m, C) if c else (0, m)
+
     def quantx(t, c):
-        lo, hi = 192 * c, 192 * c + 192
+        lo, hi = run(t, c)
         kq = "qx%d%s" % (t, "ab"[c])
         qx, sx = T["qx%d" % t], T["sx%d" % t]
         quant(["xt%d%s" % (t, "ab"[c])], [kq], qx[:, lo:hi], sx[:, lo:hi], T["xt%d" % t][:, 4 * lo:4 * hi])
         if t == ROUNDS:
             k = "P%d" % c
-            mm(["vq", kq], [k], T[k][:, 0:192], T.vq[:, 0:128], T.vs[:, 0:128], qx[:, lo:hi], sx[:, lo:hi])
+            mm(["vq", kq], [k], T[k][:, 0:hi - lo], T.vq[:, 0:128], T.vs[:, 0:128], qx[:, lo:hi], sx[:, lo:hi])
             return
         for k in ((SV, SA) if c else (S0V, S0A)):
             mm(["u16q", "u16s", "qx%da" % t, kq], [k], T[k][:, 0:hi], T.u16q[:, 0:128], T.u16s[:, 0:128], qx[:, 0:hi], sx[:, 0:hi])
@@ -299,26 +314,40 @@ def rank_program(g, core, T, topo):
         ts([k, "h%d" % (j // 12)], ["C%s%d" % (kind, j)], T.Cm[:, e:e + n], T[k][:, lo:lo + n], hcol(j), None,
            A_.is_le if kind == "X" else A_.is_lt)
 
-    def sign(kind, j):
+    def sign(j):
+        kind = "PW"[j // 12]
         e, lo, n = span(kind, j)
         k = S0A if kind == "P" else SA
         op("A", [k, "h%d" % (j // 12)], ["sg%d" % j], lambda: AC.activation(
             T.sg[:, e:e + n], T[k][:, lo:lo + n], FN.Sign, bias=hcol(j), scale=-1.0))
 
-    def relu(kind, j):
+    def relu(j):
+        kind = "PW"[j // 12]
         e, lo, n = span(kind, j)
         op("A", ["sg%d" % j], ["C%s%d" % (kind, j), "rs.%d" % j], lambda: AC.activation(
             T.Cm[:, e:e + n], T.sg[:, e:e + n], FN.Relu, accum_out=lf("rs", j, j + 1)))
 
-    def total(j):
+    def made(j):
         if j >= 12:
-            keys, dst, (e, lo, n) = ["CW%d" % j], "rs", span("W", j)
-        elif j >= PA:
-            keys, dst, (e, lo, n) = ["CX%d" % j], "rx", span("X", j)
+            return ["W%d" % j], "rs", 4 * ROW[j], 192
+        if "r%d" % j in AORD:
+            return ["X%d" % j], "rx", 4 * ROW[j], 16 * (11 - j)
+        return ["X%d" % j] + (["P%d" % j] if j else []), "rs", 4 * ROW[j], 176
+
+    def fold(j):
+        e, n = made(j)[2:]
+        return [i for i in FOLDS if CHUNKS[i][0] <= e // 4 and (e + n) // 4 <= CHUNKS[i][1]][0]
+
+    def total(j, folded):
+        keys, dst, e, n = made(j)
+        if folded:
+            a, k = CHUNKS[fold(j)][0], FOLDS[fold(j)]
+            keys, n = [k], n // 4
+            src = T[k][:, e // 4 - a:e // 4 - a + n]
         else:
-            keys, dst, e, n = ["CX%d" % j, "CP%d" % j], "rs", 4 * ROW[j], 176
+            keys, src = ["C" + k for k in keys], T.Cm[:, e:e + n]
         op("A", keys, ["%s.%d" % (dst, j), "junk%d" % j], lambda: AC.activation(
-            T.junk[:, e:e + n], T.Cm[:, e:e + n], COPY, accum_out=lf(dst, j, j + 1)))
+            T.junk[:, e:e + n], src, COPY, accum_out=lf(dst, j, j + 1)))
 
     def diag(c):
         k = SV if c else S0V
@@ -331,117 +360,211 @@ def rank_program(g, core, T, topo):
         scan(["dm", "CD%d" % c], ["dg%d" % c], T.dg[:, 192 * c:192 * c + 192], T.dm[:], T.Cm[:, e:e + 192], 0.0,
              A_.mult, A_.add)
 
-    pieces = [("front", 0, FRONT), ("CD1", DIAG[1], DIAG[1] + 48), ("CD0", DIAG[0], DIAG[0] + 48)]
+    pieces = [("D1", DIAG[1], DIAG[1] + 48), ("D0", DIAG[0], DIAG[0] + 48)]
     for j in range(24):
         for kind in ("W" if j >= 12 else "XP"):
             e, lo, n = span(kind, j)
             if n:
-                pieces.append(("C%s%d" % (kind, j), e // 4, (e + n) // 4))
+                pieces.append(("%s%d" % (kind, j), e // 4, (e + n) // 4))
 
-    def count(i):
+    def under(lo, hi):
+        return [i for i, (a, b) in enumerate(CHUNKS) if a < hi and b > lo]
+
+    def count(i, done):
         lo, hi = CHUNKS[i]
-        quant([k for k, a, b in pieces if a < hi and b > lo], ["cq%d" % i], T.cq[:, lo:hi], T.cs[:, lo:hi], T.Cm[:, 4 * lo:4 * hi])
-        rows = [a for a in range(FRONT, FRONT + 1200, 96) if lo <= a < hi][::-1]
+        quant(["C" + k for k, a, b in pieces if a < hi and b > lo], ["cq%d" % i], T.cq[:, lo:hi], T.cs[:, lo:hi],
+              T.Cm[:, 4 * lo:4 * hi])
+        if any(k[0] == "u" and fold(int(k[1:])) == i for k in AORD):
+            k = FOLDS[i]
+            mm(["iq", "cq%d" % i], [k], T[k][:, 0:hi - lo], T.iq[:, 0:128], T.isc[:, 0:128], T.cq[:, lo:hi], T.cs[:, lo:hi])
+        rows = [a for a in range(0, 1200, 96) if i in under(a, a + 128) and all(n in done + [i] for n in under(a, a + 128))]
         for a in rows:
-            mm(["gq", "cq%d" % i, "cq%d" % (i - 1)], [CNT], T[CNT][:, 0:128], T.gq[:, 0:128], T.gs[:, 0:128],
-               T.cq[:, a:a + 128], T.cs[:, a:a + 128], i == 0 and a == rows[0], i == len(CHUNKS) - 1)
+            mm(["gq", "cqz"] + ["cq%d" % n for n in under(a, a + 128)], [CNT], T[CNT][:, 0:128], T.gq[:, 0:128], T.gs[:, 0:128],
+               T.cq[:, a:a + 128], T.cs[:, a:a + 128], not done and a == rows[0], len(done) == len(CHUNKS) - 1 and a == rows[-1])
+        done.append(i)
+
+    def catch(t, lo, hi, keys):
+        tt(["win", "xw", "al%d" % (t - 1)] + [k for k, a, b in OWN if a < hi and b > lo], keys, T.zt[:, 4 * lo:4 * hi],
+           T.win[:, 0:8 * C].indirect(T["al%d" % (t - 1)][:, lo // 4:hi // 4]), T.xh[:, 4 * lo:4 * hi], A_.add)
+
+    def layer(t, c):
+        lo, hi = run(t, c)
+        quant(["zt1", "zt2", "zt3"] if c else ["zt0"], ["zq%d" % c], T.zq[:, lo:hi], T.zs[:, lo:hi], T.zt[:, 4 * lo:4 * hi])
+        for b in range(4):
+            k = "P%d" % banks[c][b]
+            mm(["wq", "wsc", "zq%d" % c], [k], T[k][:, 0:hi - lo], T.wq[:, 128 * b:128 * b + 128],
+               T.wsc[:, 128 * b:128 * b + 128], T.zq[:, lo:hi], T.zs[:, lo:hi])
+
+    def state(t, c, b):
+        lo, hi = run(t, c)
+        k = "P%d" % banks[c][b]
+        tt([k] + (["zf1", "zf2", "zf3"] if c else ["zf0"]), ["xt%d%s.%d" % (t, "ab"[c], b)],
+           T["xt%d" % t][:, 4 * lo + b:4 * hi:4], T[k][:, 0:hi - lo], T.zf[:, 4 * lo + b:4 * hi:4], A_.add)
+
+    def order(t):
+        skip = "cZyfNg" if t == 0 else "MHPXWDSQRsrtu" if t == ROUNDS else ""
+        vector = [k for k in (VEND if t == ROUNDS else VORD) if k[0] not in skip]
+        scalar = [k for k in (AEND if t == ROUNDS else AORD) if k[0] not in skip]
+        seen, done = set(k for k in VORD + AORD if k[0] in skip), []
+        m = run(t, 0)[1]
+        cuts = [0, m, m + (C - m) // 3 // 8 * 8, m + 2 * (C - m) // 3 // 8 * 8, C]
+
+        def joined(k, rest):
+            ks = [k]
+            while (rest and rest[0] in JOIN and rest[0] == k[0] + str(int(ks[-1][1:]) + 1)
+                   and all(x in seen for x in needs(rest[0]))):
+                ks.append(rest.pop(0))
+            seen.update(ks)
+            return cuts[int(k[1:])], cuts[int(ks[-1][1:]) + 1], [x[1:] for x in ks]
+
+        def needs(k):
+            j = int(k[1:]) if k[1:].isdigit() else None
+            if k[0] == "s":
+                return ["H1"] if j >= 12 else ["H0"]
+            if k[0] == "r":
+                return ["s%d" % j]
+            if k[0] == "f":
+                return ["c%d" % j]
+            if k[0] == "c":
+                return ["g" + x[2:] for x, a, b in OWN if a < cuts[j + 1] and b > cuts[j]]
+            if k[0] == "Z":
+                return ["c1", "c2", "c3"] if j else ["c0"]
+            if k[0] == "y":
+                return ["Z1", "f1", "f2", "f3"] if k[1] == "1" else ["Z0", "f0"]
+            if k[0] == "q":
+                return ["y%d%d" % (j, b) for b in range(4)] + (["q0"] if j else [])
+            if k[0] == "M":
+                return ["q%d" % j]
+            if k[0] == "H":
+                return ["M%d" % j]
+            if k[0] in "DS":
+                return ["HD"["DS".index(k[0])] + k[1]]
+            if k[0] in "PXW":
+                return {"P": ["H0"], "X": ["H0", "q1"], "W": ["H1"]}[k[0]]
+            if k == "RA":
+                return ["S0", "S1"]
+            if k[0] == "t":
+                return made(j)[0]
+            if k[0] == "u":
+                return ["Q%d" % fold(j)]
+            if k[0] == "Q":
+                lo, hi = CHUNKS[j]
+                return [p if p in VORD else "r" + p[1:] for p, a, b in pieces if a < hi and b > lo]
+            if k == "RB":
+                return ["RA"] + [x for x in AORD if x[0] in "tu" and made(int(x[1:]))[1] == "rx"]
+            return []
+
+        def emit(k, rest):
+            j = int(k[1:]) if k[1:].isdigit() else None
+            if k[0] in "PXW":
+                vrow(k[0], j)
+            elif k[0] == "c":
+                lo, hi, ks = joined(k, rest)
+                catch(t, lo, hi, ["zt" + x for x in ks])
+            elif k[0] == "f":
+                lo, hi, ks = joined(k, rest)
+                act(["zt" + x for x in ks], ["zf" + x for x in ks], T.zf[:, 4 * lo:4 * hi], T.zt[:, 4 * lo:4 * hi], 32.0)
+            elif k[0] == "g":
+                ks = [j]
+                while rest and rest[0] in JOIN and rest[0] == "g%d" % (ks[-1] + 1):
+                    ks.append(int(rest.pop(0)[1:]))
+                    seen.add("g%d" % ks[-1])
+                lo, hi = OWN[j][1], OWN[ks[-1]][2]
+                (act if rest is scalar else cp)(
+                    ["xw", "tl%d" % (lo // 192), "tl%d" % ((hi - 1) // 192)], ["xh%d" % x for x in ks],
+                    T.xh[:, 4 * lo:4 * hi], T.win[:, 0:4 * C].indirect(T.tl[:, lo // 4:hi // 4]))
+            elif k[0] == "Z":
+                layer(t, j)
+            elif k[0] == "y":
+                state(t, int(k[1]), int(k[2]))
+            elif k[0] == "q":
+                quantx(t, j)
+                if j and t < ROUNDS:
+                    before("G", ["qx%da" % t, "qx%db" % t], [])
+                    for a, b in (("land", "qx"), ("lans", "sx")):
+                        dst, src = T[a + str(t)][:, 0:C], T[b + str(t)][:, 0:C]
+                        if b == "qx":
+                            dst, src = b8(dst), b8(src)
+                        g.remote_dma(dst, src, T.sem["aq%d" % t], T.sem.loc, pid, rid, mask)
+                    cnt["loc"] = cnt.get("loc", 0) + 2 * neng
+            elif k[0] == "N":
+                if t < ROUNDS:
+                    act(["WT", "rp"], ["WN"], T.WN[:], T.WT[:, 0:C].indirect(T.rp[:, 0:24]), 1.0, -(MID + C) / 256)
+                else:
+                    act(["WT", "rp"], ["WN"], T.WN[:], T.WT[:, 0:C].indirect(T.rp[:, 0:24]))
+            elif k[0] == "Q":
+                count(j, done)
+            elif k[0] in "tu":
+                total(j, k[0] == "u")
+            elif k == "RA":
+                tt(["KA", "KB", "dg0", "dg1"], ["RA"], lf("RA"), lf("KA"), T.dg[:, 15:C:16], A_.subtract)
+            elif k == "RB":
+                tt(["RA", "rx"], ["RB"], lf("RB"), lf("RA"), lf("rx"), A_.subtract)
+            else:
+                {"D": diag, "S": diagsum, "M": masked, "H": held, "s": sign, "r": relu}[k[0]](j)
+            seen.add(k)
+
+        if t == 0:
+            first = ["q0", "q1", "E0", "E1", "M0", "E2", "H0", "E3"]
+            vector = first + [k for k in vector if k not in first]
+            vector.insert(vector.index("H1"), "E4")
+        while vector or scalar:
+            if scalar and all(x in seen for x in needs(scalar[0])):
+                emit(scalar.pop(0), scalar)
+            elif vector[0] == "E4":
+                vector.pop(0)
+                quant(["it"], ["iq"], T.iq[:, 0:128], T.isc[:, 0:128], T.it[:])
+            elif vector[0][0] == "E":
+                b = int(vector.pop(0)[1])
+                quant(["et"], ["eq%d" % b], T["eq%d" % b][:, 0:128], T["es%d" % b][:, 0:128], T.et[:, 4 - b:516 - b])
+            else:
+                assert all(x in seen for x in needs(vector[0])), vector[0]
+                emit(vector.pop(0), vector)
 
     for t in range(ROUNDS):
-        xt, qx, sx = T["xt%d" % t], T["qx%d" % t], T["sx%d" % t]
+        xt = T["xt%d" % t]
         kx = ["xt%da" % t, "xt%db" % t]
-        kq = "qx%d" % t
-
-        if t == 0:
-            quantx(0, 0)
-            quantx(0, 1)
-            quant(["gt"], ["gq"], T.gq[:, 0:128], T.gs[:, 0:128], T.gt[:])
-            quant(["zb"], ["cq-1"], T.cq[:, FRONT + 1200:FRONT + 1328], T.cs[:, FRONT + 1200:FRONT + 1328], T.Cm[:, zb:zb + 512])
-            masked(0)
-            tt(["a16"], ["c16"], T.c16[:], T.a16[:, 0:192], T.a16[:, 1:193], A_.subtract)
-            held(0)
-        before("G", [kq + "a", kq + "b"], [])
-        g.remote_dma(b8(T["land%d" % t][:, 0:C]), b8(qx[:, 0:C]), T.sem["aq%d" % t], T.sem.loc, pid, rid, mask)
-        g.remote_dma(T["lans%d" % t][:, 0:C], sx[:, 0:C], T.sem["aq%d" % t], T.sem.loc, pid, rid, mask)
-        cnt["loc"] = cnt.get("loc", 0) + 2 * neng
+        order(t)
         if t == 0:
             spread(0)
-            ts(["a16"], ["c16"], T.c16[:, 15:192:16], T.a16[:, 15:192:16], -2 * HOLD, None, A_.add)
-            ts(["k24", "kf.5"], ["KA"], lf("KA", 0, 12), li("k24", 0, 12), kf(5), 176.0, A_.add, A_.add)
-            ts(["k24", "kf.5"], ["KB"], lf("KA", 12, 24), li("k24", 0, 12), kf(5), 192.0, A_.add, A_.add)
-
-        arows = [("P", j) for j in range(11, PA - 1, -1)]
-        sign(*arows[0])
-        for a, b in zip(arows, arows[1:] + [None]):
-            if b:
-                sign(*b)
-            relu(*a)
-
-        diag(0)
-        for j in range(PA - 1, 0, -1):
-            vrow("P", j)
-        masked(1)
-        vrow("X", 0)
-        total(0)
-        held(1)
-        for j in WA:
-            sign("W", j)
-        for j in WA:
-            relu("W", j)
-        diagsum(0)
-        for j in range(1, 11):
-            vrow("X", j)
-            total(j)
-        diag(1)
-        if t == 0:
-            for b in range(4):
-                quant(["et"], ["eq%d" % b], T["eq%d" % b][:, 0:128], T["es%d" % b][:, 0:128], T.et[:, 4 - b:516 - b])
-        for j in range(12, 24):
-            if j not in WA:
-                vrow("W", j)
-                total(j)
-            if j == 12:
-                diagsum(1)
-            if j == 16:
-                count(0)
-            if j == 17:
-                tt(["KA", "KB", "dg0", "dg1"], ["RA"], lf("RA"), lf("KA"), T.dg[:, 15:C:16], A_.subtract)
-            if j == 19:
-                tt(["RA", "rx"], ["RB"], lf("RB"), lf("RA"), lf("rx"), A_.subtract)
-            if j == 21:
-                count(1)
-        count(2)
-        count(3)
-        if t == 0:
+            op("G", [], ["TLW"], lambda: g.iota(T.TLW[:], [[-1536, 2], [4, C]], 1536, 0, allow_small_or_imprecise_dtypes=True))
             act(["WT", "pP"], ["WN"], T.WN[:], T.WT[:, 0:C].indirect(T.pP[:, 0:24]), 1.0, -(MID + C) / 256)
         for b in range(4):
             k = "P%d" % DB[b]
             mm(["eq%d" % b, "land%d" % t], [k], T[k][:, 0:C], T["eq%d" % b][:, 0:128],
                T["es%d" % b][:, 0:128], T["land%d" % t][:, 0:C], T["lans%d" % t][:, 0:C])
         act(kx, ["xw"], T.win[:, 0:4 * C], xt[:], 2.0 ** -6)
-        for b in range(4):
-            k = "P%d" % DB[b]
-            act([k], ["win.%d" % b], T.win[:, 4 * C + b:8 * C:4], T[k][:, 0:C], 2.0 ** -6)
-        act(kx, ["xh"], T.xh[:], xt[:], 2.0 ** -6)
         tt(["RB", "rs"], ["rk3"], T.rk[:, 3:96:4], lf("RB"), lf("rs"), A_.subtract)
         scan([CNT, "rk", "rk3"], ["e1"], T.e1[:], T[CNT][:, 0:96], T.rk[:], 0.0, A_.max, A_.add)
+        if t == 0:
+            quant(["vt"], ["vq"], T.vq[:, 0:128], T.vs[:, 0:128], T.vt[:])
         ts(["e1"], ["ru"], T.ru[:], T.e1[:, 3:96:4], HOLD, None, A_.add)
+        ts(["e1"], ["rf"], li("rf"), T.e1[:, 3:96:4], HOLD, None, A_.add)
         cp(["ru", "WN"], ["WS"], T.WS[:, 0:C].indirect(T.ru[:, 0:24]), T.WN[:])
+        ts(["rf"], ["b1"], li("b1"), li("rf"), 31, None, A_.bitwise_and)
+        ts(["rf"], ["b2"], li("b2"), li("rf"), 5, None, A_.logical_shift_right)
         for c in range(2):
             scan(["c16", "WS"], ["e2%d" % c], T.e2[:, 192 * c:192 * c + 192], T.WS[:, c:C:2], T.c16[:], 0.0, A_.max, A_.add)
-        ts(["WS"], ["WC0"], T.WC[:, 0:192], T.WS[:, 0:C:2], FOURS, FOURS, A_.add, A_.subtract)
         ts(["e20"], ["X1.2"], T.X1[:, 50:96:4], T.e2[:, 15:192:16], FOURS + HOLD, FOURS, A_.add, A_.subtract)
+        ts(["WS"], ["WC0"], T.WC[:, 0:192], T.WS[:, 0:C:2], FOURS, FOURS, A_.add, A_.subtract)
         ts(["e21"], ["X1b"], T.X1[:, 2:48:4], T.e2[:, 207:C:16], FOURS + HOLD, FOURS, A_.add, A_.subtract)
         ts(["e20", "e21"], ["X1.0"], T.X1[:, 0:96:4], T.e2[:, 15:C:16], FOURS + HOLD, FOURS, A_.add, A_.subtract)
-        ts(["e20", "e21"], ["X1.1"], T.X1[:, 1:96:4], T.e2[:, 15:C:16], HOLD + (MID + C) / 256, None, A_.add)
+        act(["e20", "e21"], ["X1.1"], T.X1[:, 1:96:4], T.e2[:, 15:C:16], 1.0, HOLD + (MID + C) / 256)
         ts(["WS"], ["WC1"], T.WC[:, 192:C], T.WS[:, 1:C:2], FOURS, FOURS, A_.add, A_.subtract)
         scan(["X0", "X1", "X1b"], ["o1"], T.o1[:], T.X0[:], T.X1[:], 0.0, A_.mult, A_.add)
+        ts(["b1"], ["b3"], li("b3"), li("b1"), 12, None, A_.mult)
         ts(["o1"], ["Y0.0"], T.Y0[:, 1:72:3], T.o1[:, 3:96:4], REACH, REACH, A_.add, A_.is_equal)
         ts(["o1"], ["Y0.1"], T.Y0[:, 2:36:3], T.o1[:, 51:96:4], REACH, REACH, A_.add, A_.is_equal)
         ts(["o1"], ["Y0.2"], T.Y0[:, 38:72:3], T.o1[:, 3:48:4], REACH, REACH, A_.add, A_.is_equal)
         tt(["o1"], ["Y1.0"], T.Y1[:, 0:36:3], T.o1[:, 49:96:4], T.o1[:, 1:48:4], A_.subtract)
         tt(["o1"], ["Y1.1"], T.Y1[:, 36:72:3], T.o1[:, 1:48:4], T.o1[:, 49:96:4], A_.subtract)
-        cp(["o1"], ["Y1.2"], T.Y1[:, 2:72:3], T.o1[:, 1:96:4])
+        act(["o1"], ["Y1.2"], T.Y1[:, 2:72:3], T.o1[:, 1:96:4])
+        for b in range(4):
+            k = "P%d" % DB[b]
+            act([k], ["win.%d" % b], T.win[:, 4 * C + b:8 * C:4], T[k][:, 0:C], 2.0 ** -6)
+        tt(["b3", "b2"], ["b4"], li("b4"), li("b3"), li("b2"), A_.add)
         scan(["Y0", "Y1"], ["so"], T.so[:], T.Y0[:], T.Y1[:], 0.0, A_.mult, A_.add)
+        cp(["b4"], ["rp"], T.rp[:], li("b4"))
         ts(["so"], ["Lu"], T.Lu[:], T.so[:, 2:72:3], 256.0, -MID, A_.mult, A_.add)
         kw = "wd%d" % (t + 1)
         if t == ROUNDS - 1:
@@ -449,81 +572,39 @@ def rank_program(g, core, T, topo):
         else:
             tt(["so", "X1.0"], ["wa"], lf("wa"), T.so[:, 2:72:3], T.X1[:, 0:96:4], A_.add)
         dma("S", "dw%d" % (t + 1), ["wa"], [kw], lambda: g.sync.dma_start(T[kw][:], lf("wa")))
-        cp(["Lu", "WC0", "WC1"], ["TLW", "TLWa"], T.TLW[:, 0:768].indirect(T.Lu[:, 0:24]), T.WC[:])
+        cp(["Lu", "WC0", "WC1"], ["TLW"], T.TLW[:, 0:768].indirect(T.Lu[:, 0:24]), T.WC[:])
         scan(["c4", "TLW"], ["e3"], T.e3[:], T.TLW[:, 384:768], T.c4[:], 0.0, A_.max, A_.add)
+
+        def ownscan(c):
+            lo, hi = 192 * c, 192 * c + 192
+            scan(["c4", "TLW"], ["e4%d" % c], T.e4[:, lo:hi], T.TLW[:, lo:hi], T.c4[:, lo:hi], 0.0, A_.max, A_.add)
+
+        def ownlist(c):
+            ts(["e4%d" % c, "kf.4"], ["tl%d" % c], T.tl[:, 48 * c:48 * c + 48], T.e4[:, 192 * c + 3:192 * c + 192:4], kf(4),
+               None, A_.add)
+
+        ownscan(0)
         ksl = "sl%d" % t
-        ts(["e3"], [ksl], T[ksl][:], T.e3[:, 3:C:4], HOLD, None, A_.add)
+        ts(["e3", "kf.6"], [ksl], T[ksl][:], T.e3[:, 3:C:4], kf(6), None, A_.add)
         before("G", [ksl], [])
         g.remote_dma(T["al%d" % t][:], T[ksl][:], T.sem["al%d" % t], T.sem.loc, pid, rid, mask)
         cnt["loc"] += neng
         spread(t + 1)
-        scan(["c4", "TLW", "TLWa"], ["e4"], T.e4[:], T.TLW[:, 0:384], T.c4[:], 0.0, A_.max, A_.add)
-        if t == 0:
-            quant(["vt"], ["vq"], T.vq[:, 0:128], T.vs[:, 0:128], T.vt[:])
-        ts(["e1"], ["rf"], li("rf"), T.e1[:, 3:96:4], HOLD, None, A_.add)
-        ts(["e4", "kf.3", "kf.4"], ["own"], T.own[:], T.e4[:, 3:C:4], kf(4), kf(3), A_.add, A_.max)
-        ts(["rf"], ["b1"], li("b1"), li("rf"), 31, None, A_.bitwise_and)
-        ts(["rf"], ["b2"], li("b2"), li("rf"), 5, None, A_.logical_shift_right)
-        ts(["b1"], ["b3"], li("b3"), li("b1"), 12, None, A_.mult)
-        tt(["b3", "b2"], ["b4"], li("b4"), li("b3"), li("b2"), A_.add)
-        cp(["b4"], ["rp"], T.rp[:], li("b4"))
-        for c in range(2):
-            tt(["own", "al%d" % t], ["tz%d" % c], T.tz[:, 48 * c:48 * c + 48], T.own[:, 48 * c:48 * c + 48],
-               T["al%d" % t][:, 48 * c:48 * c + 48], A_.add)
-        for c in range(2):
-            cp(["tz%d" % c], ["tl%d" % c], T.tl[:, 48 * c:48 * c + 48], T.tz[:, 48 * c:48 * c + 48])
-
-        def catch(lo, hi, k):
-            tt(["win", "xw", "xh", "tl%d" % (lo // 192)], [k], T.zt[:, 4 * lo:4 * hi],
-               T.win[:, 0:8 * C].indirect(T.tl[:, lo // 4:hi // 4]), T.xh[:, 4 * lo:4 * hi], A_.add)
-
-        def layer(c, keys):
-            lo, hi = 192 * c, 192 * c + 192
-            quant(keys, ["zq%d" % c], T.zq[:, lo:hi], T.zs[:, lo:hi], T.zt[:, 4 * lo:4 * hi])
-            act(keys, ["zf%d" % c], T.zf[:, 4 * lo:4 * hi], T.zt[:, 4 * lo:4 * hi], 32.0)
-            for b in range(4):
-                k = "P%d" % banks[c][b]
-                mm(["wq", "wsc", "zq%d" % c], [k], T[k][:, 0:192], T.wq[:, 128 * b:128 * b + 128],
-                   T.wsc[:, 128 * b:128 * b + 128], T.zq[:, lo:hi], T.zs[:, lo:hi])
-
-        def state(c, b):
-            lo, hi = 192 * c, 192 * c + 192
-            k = "P%d" % banks[c][b]
-            tt([k, "zf%d" % c], ["xt%d%s.%d" % (t + 1, "ab"[c], b)], T["xt%d" % (t + 1)][:, 4 * lo + b:4 * hi:4],
-               T[k][:, 0:192], T.zf[:, 4 * lo + b:4 * hi:4], A_.add)
-
-        catch(0, 192, "zt0")
-        catch(192, 256, "zt1")
-        layer(0, ["zt0"])
-        catch(256, 384, "zt2")
-        state(0, 0)
-        layer(1, ["zt1", "zt2"])
-        if t < ROUNDS - 1:
-            act(["WT", "rp"], ["WN"], T.WN[:], T.WT[:, 0:C].indirect(T.rp[:, 0:24]), 1.0, -(MID + C) / 256)
-        else:
-            act(["WT", "rp"], ["WN"], T.WN[:], T.WT[:, 0:C].indirect(T.rp[:, 0:24]))
-        for b in range(1, 4):
-            state(0, b)
-        state(1, 0)
-        quantx(t + 1, 0)
-        for b in range(1, 4):
-            state(1, b)
-        if t < ROUNDS - 1:
-            masked(0)
-        quantx(t + 1, 1)
-        if t < ROUNDS - 1:
-            held(0)
+        ownscan(1)
+        ownlist(0)
+        ownlist(1)
+    order(ROUNDS)
 
     dma("A", "ool", ["WN"], [], lambda: AC.dma_start(T.ol[:], T.WN[0:128:16, :]))
-    act(["P0"], ["ysb0"], T.ysb[:, 0:192], T.P0[:, 0:192])
-    cp(["P1"], ["ysb1"], T.ysb[:, 192:384], T.P1[:, 0:192])
-    dma("S", "oc0", ["qx3a"], [], lambda: g.sync.dma_start(T.oc[:, 0:768], b8(T.qx3[:, 0:192])))
-    dma("A", "oy0", ["ysb0"], [], lambda: AC.dma_start(T.y[:, 0:192], T.ysb[:, 0:192]))
-    dma("S", "oc1", ["qx3b"], [], lambda: g.sync.dma_start(T.oc[:, 768:1536], b8(T.qx3[:, 192:384])))
+    act(["P0"], ["ysb0"], T.ysb[:, 0:LAST], T.P0[:, 0:LAST])
+    cp(["P1"], ["ysb1"], T.ysb[:, LAST:C], T.P1[:, 0:C - LAST])
+    dma("S", "oc0", ["qx3a"], [], lambda: g.sync.dma_start(T.oc[:, 0:4 * LAST], b8(T.qx3[:, 0:LAST])))
+    dma("A", "oy0", ["ysb0"], [], lambda: AC.dma_start(T.y[:, 0:LAST], T.ysb[:, 0:LAST]))
+    dma("S", "oc1", ["qx3b"], [], lambda: g.sync.dma_start(T.oc[:, 4 * LAST:4 * C], b8(T.qx3[:, LAST:C])))
     for k in range(4):
         dma("A" if k % 2 else "S", "oos%d" % k, ["qx3a", "qx3b"], [], lambda: (AC if k % 2 else g.sync).dma_start(
             T.osc[4 * k:4 * k + 4, 0:C], T.sx3[32 * k:32 * k + 4, 0:C]))
-    dma("S", "oy1", ["ysb1"], [], lambda: g.sync.dma_start(T.y[:, 192:384], T.ysb[:, 192:384]))
+    dma("S", "oy1", ["ysb1"], [], lambda: g.sync.dma_start(T.y[:, LAST:C], T.ysb[:, LAST:C]))
     for s, c in cnt.items():
         if not any(kn.get(s, 0) >= c for kn in known.values()):
             g.wait_ge(T.sem[s], c)

@@ -1,5 +1,5 @@
 from concourse.bass import IndirectOffsetOnAxis
-from concourse.mybir import dt, AluOpType, ActivationFunctionType
+from concourse.mybir import dt, AluOpType, ActivationFunctionType, AxisListType
 
 C = 384
 ROUNDS = 3
@@ -12,8 +12,8 @@ Q8 = "float8_e4m3fn_x4"
 A_ = AluOpType
 FN = ActivationFunctionType
 COPY = FN.Copy
-INTS = "P24 T16 T1 k24 ic pi k1 k3 rf b1 b2 b3 b4".split()
-FLOATS = "rs rx RA RB KA wa pm pf kf cv I4".split()
+INTS = "P4 k4 T1 pi rf b1 b2 b3 b4".split()
+FLOATS = "rs rx RA RB KA KC wa T64 pf kf cv I4".split()
 NW = 1200 + 132
 ROW = {}
 _p = 0
@@ -22,16 +22,18 @@ for _t in range(11, -1, -1):
     ROW[_t + 12] = _p + 44
     _p += 92
 DIAG = {1: _p, 0: _p + 48}
-CHUNKS = [(772, 1200), (488, 772), (0, 236), (236, 488)]
+CHUNKS = [(776, 1200), (488, 776), (0, 288), (288, 488)]
 FOLDS = {0: "P5", 1: "P6", 2: "P7"}
-VORD = "g0 c0 c1 Z0 c2 c3 y00 Z1 y03 y01 y02 y10 q0 y11 y12 y13 M0 q1 H0 P6 D0 M1 P4 X3 H1 X9 X0 X6 P1 X10 X1 W12 X7 X2 X5 P7 P5 D1 W15 P3 X8 S1 W14 P2 W13 W18 Q0 P8 W16 S0 X4 RA Q1 W19 Q2 RB Q3".split()
-AORD = "g1 g2 g3 g4 f0 f1 f2 f3 N0 s11 s9 s10 r9 r11 s20 s23 r10 s21 r23 s17 t7 r21 t3 s22 t10 r20 r17 t6 r22 t8 u2 u1 u13 u15 u12 t9 u0 u16 u4 t19 u5 u18 u14".split()
-VEND = "g0 c0 c1 Z0 c2 c3 y00 Z1 y01 y02 y03 y10 q0 y11 y12 y13 q1".split()
+VORD = ("e2 e0 l2 e3 l0 e1 g0 l3 l1 c0 c1 Z0 c2 c3 y00 Z1 y01 y02 y03 y10 q0 y13 y12 y11 M0 q1 H0 D0 P1 X6 X5 M1 X2 H1 X0 W12 "
+        "P4 W14 X3 W16 P10 X1 P5 W15 W13 X7 X9 D1 P8 Q0 X10 W18 S0 X4 S1 X8 Q1 RA W19 v7 Q2 Q3 RB v16").split()
+AORD = ("g1 g2 g3 g4 f0 f1 f3 f2 N0 s9 s7 s3 s6 s11 r7 s2 t6 r2 s17 s21 r17 r6 s20 r3 t2 r20 s22 r21 r9 r22 s23 r11 t10 r23 t9 "
+        "u1 u12 u0 u13 u15 t8 u14 u3 u4 u5 u18 t19").split()
+VEND = "e2 e0 l2 e3 l0 e1 g0 l3 l1 c0 c1 Z0 c2 c3 y00 Z1 y01 y03 y02 y11 y10 y13 y12 q0 q1".split()
 AEND = "g1 g2 g3 g4 f0 f1 f2 f3 N0".split()
 JOIN = ["g4", "c3", "f3"]
 OWN = [("xh0", 0, 96), ("xh1", 96, 192), ("xh2", 192, 256), ("xh3", 256, 320), ("xh4", 320, C)]
-LAST = 256
-PARTS = {"X1": 4, "X0": 3, "Y0": 3, "Y1": 3, "c4": 4, "rs": 24, "rx": 12, "kf": 12, "gt": 4, "win": 4}
+LAST = 192
+PARTS = {"X1": 4, "X0": 4, "k4": 4, "Y0": 3, "Y1": 3, "c4": 4, "rs": 24, "rx": 12, "kf": 14, "gt": 4, "win": 4, "xw": 2}
 for _i in range(1, ROUNDS + 1):
     PARTS["xt%da" % _i] = PARTS["xt%db" % _i] = 4
 
@@ -63,14 +65,14 @@ for _n, _c, _d in (
         ("vt", 512, "bfloat16"), ("vq", 128, Q8), ("vs", 128, "uint8"),
         ("wq", 512, Q8), ("wsc", 512, "uint8"), ("et", 520, "bfloat16"),
         ("zt", 4 * C, "bfloat16"), ("zf", 4 * C, "bfloat16"), ("zq", C, Q8), ("zs", C, "uint8"),
-        ("gt", 512, "bfloat16"), ("gq", 128, Q8), ("gs", 128, "uint8"), ("GI", 32, "float32"),
-        ("D", 208, "float32"), ("mb", 192, "float32"), ("d0", 192, "float32"), ("a16", 208, "float32"),
-        ("c16", 192, "float32"), ("c4", C, "float32"), ("rk", 96, "float32"), ("dm", 192, "bfloat16"),
-        ("dg", C, "bfloat16"), ("M", C, "float32"), ("h", C, "float32"), ("U8", 8, "int32"), ("idx", 2, "int32"),
+        ("gt", 512, "bfloat16"), ("gq", 128, Q8), ("gs", 128, "uint8"), ("GI", 32, "float32"), ("GA", 32, "float32"),
+        ("D", 192, "float32"), ("mb", 192, "float32"), ("d0", 192, "float32"), ("a16", 192, "float32"),
+        ("c16", 192, "float32"), ("c4", 192, "float32"), ("rk", 96, "float32"), ("dm", 192, "bfloat16"),
+        ("dg", C, "bfloat16"), ("M", C, "float32"), ("h", C, "float32"), ("U8", 8, "int32"),
         ("pP", 24, "uint16"), ("rp", 24, "uint16"), ("upo", 8, "uint16"), ("e1", 96, "float32"), ("ru", 24, "uint16"),
         ("WT", C, "float32"), ("WN", C, "float32"), ("WS", C, "float32"), ("WC", C, "float32"),
-        ("e2", C, "float32"), ("Lu", 24, "uint16"), ("TLW", 768, "float32"), ("e3", C, "float32"),
-        ("e4", C, "float32"), ("tl", 96, "uint16"),
+        ("e2", C, "float32"), ("Lu", 24, "uint16"), ("TLW", 768, "float32"), ("e3", 768, "float32"),
+        ("tl", 96, "uint16"),
         ("X0", 96, "float32"), ("X1", 96, "float32"), ("o1", 96, "float32"),
         ("Y0", 72, "float32"), ("Y1", 72, "float32"), ("so", 72, "float32"), ("ysb", C, "float32")):
     _sb(_n, _c, _d)
@@ -78,7 +80,7 @@ for _i in range(8):
     SCRATCH["P%d" % _i] = ("psum", [128, 512], "float32")
 SEMAPHORES = (["sV", "sA", "sT", "sG", "loc", "lx", "ly", "lp", "lu", "lv", "lw", "ls", "oy0", "oy1", "ool", "oc0", "oc1"]
               + ["oos%d" % k for k in range(4)] + ["dw%d" % k for k in range(4)] + ["ig%d" % k for k in range(4)]
-              + ["aq%d" % k for k in range(3)] + ["al%d" % k for k in range(3)])
+              + ["aq%d" % k for k in range(3)] + ["al%d%d" % (k, c) for k in range(3) for c in range(2)])
 
 
 def rank_program(g, core, T, topo):
@@ -193,7 +195,8 @@ def rank_program(g, core, T, topo):
 
     for t in range(ROUNDS):
         arrives("land%d" % t, "aq%d" % t, 2 * peng)
-        arrives("al%d" % t, "al%d" % t, peng)
+        for c in range(2):
+            arrives("al%d%d" % (t, c), "al%d%d" % (t, c), peng)
 
     dma("S", "lx", [], ["xt0a"], lambda: g.sync.dma_start(T.xt0[:, 0:768], T.x[:, 0:768]))
     dma("A", "lu", [], ["ut"], lambda: AC.dma_start(T.ut[:], T.u[:]))
@@ -201,74 +204,92 @@ def rank_program(g, core, T, topo):
     dma("S", "lp", [], ["pi"], lambda: g.sync.dma_start(li("pi"), T.p[:]))
 
     zb = 4 * 1200
-    op("G", [], ["P24"], lambda: g.iota(li("P24"), [[0, 24]], 0, 1))
-    op("G", [], ["D"], lambda: g.iota(T.D[:], [[0, 13], [1, 16]], 0, 0, allow_small_or_imprecise_dtypes=True))
-    op("G", [], ["U8"], lambda: g.iota(T.U8[:], [[16, 8]], 0, 0))
-    op("G", [], ["T16"], lambda: g.iota(li("T16"), [[16, 24]], 0, 0))
-    op("G", [], ["T1"], lambda: g.iota(li("T1"), [[1, 24]], 0, 0))
-    op("G", [], ["GI"], lambda: g.iota(T.GI[:], [[1, 8], [0, 4]], 0, 0, allow_small_or_imprecise_dtypes=True))
+
+    def zeros(n):
+        return T.Cm[:, zb:zb + n]
+
+    def fn(R, W, out, a, f, scale, bias):
+        op("A", R, W, lambda: AC.activation(out, a, f, bias=bias, scale=scale))
+
+    def iota(W, out, pattern, base, cm=0):
+        op("G", [], W, lambda: g.iota(out, pattern, base, cm, allow_small_or_imprecise_dtypes=True))
+
+    iota(["P4"], li("P4", 0, 4), [[0, 4]], 0, 1)
+    iota(["D"], T.D[:], [[0, 12], [1, 16]], 0)
+    iota(["U8"], T.U8[:], [[16, 8]], 0)
+    iota(["GI"], T.GI[:], [[1, 8], [0, 4]], 0)
+    iota(["T64"], lf("T64"), [[64, 24]], 1536)
+    iota(["T1"], li("T1"), [[1, 24]], 0)
+    iota(["KC"], lf("KC"), [[16, 2], [0, 12]], 176)
     ms(["zb"], T.Cm[:, zb:4 * NW], 0.0)
-    ms(["gt"], T.gt[:], 0.0)
-    ts(["P24"], ["k24"], li("k24"), li("P24"), 15, None, A_.bitwise_and)
-    ts(["P24"], ["idx"], T.idx[:, 0:1], li("P24", 0, 1), 4, None, A_.logical_shift_right)
-    ts(["P24"], ["b1"], li("b1", 0, 1), li("P24", 0, 1), 2, 3, A_.logical_shift_right, A_.bitwise_and)
-    ts(["P24"], ["b2"], li("b2", 0, 1), li("P24", 0, 1), 3, None, A_.bitwise_and)
-    ms(["rs", "rx"], lf("rs", 0, 48), 0.0)
-    cp(["k24"], ["kf.0"], kf(0), li("k24", 0, 1))
-    cp(["idx"], ["kf.1"], kf(1), T.idx[:, 0:1])
-    cp(["b1"], ["kf.2"], kf(2), li("b1", 0, 1))
-    cp(["b2"], ["kf.3"], kf(3), li("b2", 0, 1))
-    op("G", ["zb"], ["it"], lambda: g.affine_select(T.it[:], T.Cm[:, zb:zb + 512], [[1, 128], [0, 4]], A_.not_equal, 1.0, 0, -1))
-    op("G", ["zb"], ["et"], lambda: g.affine_select(T.et[:], T.Cm[:, zb:zb + 520], [[1, 520]], A_.not_equal, 1.0, -4, -4))
-    ts(["D", "kf.0"], ["mb"], T.mb[:], T.D[:, 0:192], kf(0), BIG, A_.not_equal, A_.mult)
-    ts(["D", "kf.0"], ["d0"], T.d0[:], T.D[:, 0:192], kf(0), BIG, A_.is_equal, A_.mult)
+    ts(["P4"], ["k4.0"], li("k4", 0, 1), li("P4", 0, 1), 15, None, A_.bitwise_and)
+    ts(["P4"], ["k4.1"], li("k4", 1, 2), li("P4", 0, 1), 4, None, A_.logical_shift_right)
+    ts(["P4"], ["k4.2"], li("k4", 2, 3), li("P4", 0, 1), 2, 3, A_.logical_shift_right, A_.bitwise_and)
+    ts(["P4"], ["k4.3"], li("k4", 3, 4), li("P4", 0, 1), 3, None, A_.bitwise_and)
+    cp(["k4"], ["kf.0", "kf.1", "kf.2", "kf.3"], lf("kf", 0, 4), li("k4", 0, 4))
+    op("G", ["zb"], ["it"], lambda: g.affine_select(T.it[:], zeros(512), [[1, 128], [0, 4]], A_.not_equal, 1.0, 0, -1))
+    op("G", ["zb"], ["et"], lambda: g.affine_select(T.et[:], zeros(520), [[1, 520]], A_.not_equal, 1.0, -4, -4))
+    ts(["D", "kf.0"], ["d0"], T.d0[:], T.D[:], kf(0), BIG, A_.is_equal, A_.mult)
+    ts(["D", "kf.0"], ["mb"], T.mb[:], T.D[:], kf(0), BIG, A_.not_equal, A_.mult)
     cp(["U8"], ["upo"], T.upo[:], T.U8[:])
-    tt(["T16", "k24"], ["ic"], li("ic"), li("T16"), li("k24"), A_.add)
     ms(["d0"], T.d0[:, 0:192:16], BIG)
-    ts(["k24"], ["k1"], li("k1"), li("k24"), 24, None, A_.mult)
-    ts(["ic"], ["pm"], lf("pm"), li("ic"), 4.0, 1536 + MID / 256, A_.mult, A_.add)
-    ts(["D", "kf.0"], ["a16"], T.a16[:], T.D[:], kf(0), HOLD, A_.is_equal, A_.mult)
-    tt(["k1", "T1"], ["k3"], li("k3"), li("k1"), li("T1"), A_.add)
-    ts(["D", "kf.2"], ["I4"], lf("I4", 0, 5), T.D[:, 0:5], kf(2), HOLD, A_.is_equal, A_.mult)
-    ts(["kf.3"], ["kf.4"], kf(4), kf(3), HOLD - 1536, None, A_.add)
-    ts(["kf.3"], ["kf.6"], kf(6), kf(3), HOLD, None, A_.add)
-    cp(["k3"], ["pP"], T.pP[:], li("k3"))
-    tt(["I4"], ["cv"], lf("cv", 0, 4), lf("I4", 0, 4), lf("I4", 1, 5), A_.subtract)
-    ts(["I4"], ["kf.5"], kf(5), lf("I4", 3, 4), -2 * HOLD, None, A_.add)
-    tt(["a16"], ["c16"], T.c16[:], T.a16[:, 0:192], T.a16[:, 1:193], A_.subtract)
-    for r in range(4):
-        ts(["GI", "kf.1"], ["gt.%d" % r], T.gt[:, 5 * r:512:16], T.GI[:], kf(1), None, A_.is_equal)
-    ts(["a16"], ["c16"], T.c16[:, 15:192:16], T.a16[:, 15:192:16], -2 * HOLD, None, A_.add)
-    ts(["k24", "kf.5"], ["KA"], lf("KA", 0, 12), li("k24", 0, 12), kf(5), 176.0, A_.add, A_.add)
-    ts(["k24", "kf.5"], ["KB"], lf("KA", 12, 24), li("k24", 0, 12), kf(5), 192.0, A_.add, A_.add)
-    quant(["zb"], ["cqz"], T.cq[:, 1200:1328], T.cs[:, 1200:1328], T.Cm[:, zb:zb + 512])
-    quant(["gt"], ["gq"], T.gq[:, 0:128], T.gs[:, 0:128], T.gt[:])
-    ts(["pi"], ["pf"], lf("pf"), li("pi"), 1.0 / 256, None, A_.mult)
     quant(["ut"], ["uq"], T.uq[:, 0:128], T.us[:, 0:128], T.ut[:])
-    tt(["pm", "pf"], ["wa"], lf("wa"), lf("pm"), lf("pf"), A_.add)
-    dma("S", "dw0", ["wa"], ["wd0"], lambda: g.sync.dma_start(T.wd0[:], lf("wa")))
+    act(["zb"], ["gt"], T.gt[:], zeros(512))
+    for i, src, a, b in ((7, 1, -1.0, 0.0), (13, 0, 4.0, MID / 256), (12, 0, 24.0, 0.0), (9, 2, -1.0, 0.5),
+                         (5, 2, HOLD, -4 * HOLD)):
+        act(["kf.%d" % src], ["kf.%d" % i], kf(i), kf(src), a, b)
+    fn(["GI", "kf.7"], ["GA"], T.GA[:], T.GI[:], FN.Abs, 1.0, kf(7))
+    act(["zb"], ["rs", "rx"], lf("rs", 0, 48), zeros(48))
+    act(["kf.0", "kf.5"], ["kf.11"], kf(11), kf(0), 1.0, kf(5))
+    for r in range(4):
+        fn(["GA"], ["gt.%d" % r], T.gt[:, 5 * r:512:16], T.GA[:], FN.Relu, -1.0, 1.0)
+    ts(["pi", "kf.13"], ["pf"], lf("pf"), li("pi"), 1.0 / 256, kf(13), A_.mult, A_.add)
     cp(["uq", "upo"], ["u16q"], T.u16q[:, 0:128].bitcast(dt.uint32),
        T.uq[:, 0:128].bitcast(dt.uint32).indirect(T.upo[:, 0:8]))
-    act(["zb"], ["X1.3"], T.X1[:, 3:96:4], T.Cm[:, zb:zb + 24])
-    act(["zb"], ["X0"], T.X0[:, 0:96:4], T.Cm[:, zb:zb + 24])
-    for i, c in ((1, -1.0), (2, -1024.0), (3, 4.0 / 3)):
-        act(["zb"], ["X0.%d" % (i - 1)], T.X0[:, i:96:4], T.Cm[:, zb:zb + 24], 1.0, c)
-    act(["zb"], ["Y0"], T.Y0[:], T.Cm[:, zb:zb + 72])
-    act(["zb"], ["Y1"], T.Y1[:], T.Cm[:, zb:zb + 72])
-    act(["zb"], ["dm"], T.dm[:], T.Cm[:, zb:zb + 192], 1.0, 1.0)
-    act(["zb"], ["dm"], T.dm[:, 0:192:16], T.Cm[:, zb:zb + 12])
-    for i in range(4):
-        act(["zb", "cv", "kf.5"], ["c4.%d" % i], T.c4[:, i:C:4], T.Cm[:, zb:zb + 96], 1.0,
-            lf("cv", i, i + 1) if i < 3 else kf(5))
-    act(["c4"], ["rk", "rk3"], T.rk[:], T.c4[:, 0:96])
     act(["uq", "upo"], ["u16s"], T.u16s[:, 0:128], T.us[:, 0:128].indirect(T.upo[:, 0:8]))
-    dma("S", "lw", ["xt0a", "xt0b"], ["wq"], lambda: g.sync.dma_start(b8(T.wq[:, 0:512]), T.wc[:]))
-    dma("S", "ls", [], ["wsc"], lambda: g.sync.dma_start(T.wsc[:, 0:512], T.ws[:]))
-    dma("S", "lv", [], ["vt"], lambda: g.sync.dma_start(T.vt[:], T.v[:]))
+    fn(["D", "kf.9"], ["I4"], lf("I4", 0, 3), T.D[:, 0:3], FN.Sign, 1.0, kf(9))
+    fn(["D"], ["dm"], T.dm[:], T.D[:], FN.Sign, 1.0, 0.0)
+    act(["I4"], ["cv"], lf("cv", 0, 3), lf("I4", 0, 3), HOLD)
+    act(["KC", "kf.11"], ["KA"], lf("KA"), lf("KC"), 1.0, kf(11))
+    for i in (3, 0, 1, 2):
+        act(["zb", "cv" if i < 3 else "kf.5"], ["c4.%d" % i], T.c4[:, i:192:4], zeros(48), 1.0,
+            lf("cv", i, i + 1) if i < 3 else kf(5))
+    for i, src, a, b in ((8, 0, -1.0, 0.5), (10, 0, HOLD, -16 * HOLD), (4, 3, 1.0, HOLD - 1536), (6, 3, 1.0, HOLD)):
+        act(["kf.%d" % src], ["kf.%d" % i], kf(i), kf(src), a, b)
+    act(["c4"], ["rk"], T.rk[:], T.c4[:, 0:96])
+
+    def later():
+        fn(["D", "kf.8"], ["a16"], T.a16[:], T.D[:], FN.Sign, 1.0, kf(8))
+        act(["zb"], ["X1.3"], T.X1[:, 3:96:4], zeros(24))
+        for i, c in enumerate((0.0, -1.0, -1024.0, 4.0 / 3)):
+            act(["zb"], ["X0.%d" % i], T.X0[:, i:96:4], zeros(24), 1.0, c)
+        act(["a16"], ["c16"], T.c16[:], T.a16[:], HOLD)
+        act(["zb"], ["Y0"], T.Y0[:], zeros(72))
+        act(["zb"], ["Y1"], T.Y1[:], zeros(72))
+        act(["zb", "kf.10"], ["c16"], T.c16[:, 15:192:16], zeros(12), 1.0, kf(10))
+
+    def unit(b):
+        quant(["et"], ["eq%d" % b], T["eq%d" % b][:, 0:128], T["es%d" % b][:, 0:128], T.et[:, 4 - b:516 - b])
+
+    def filler(i):
+        if i == 0:
+            quant(["gt"], ["gq"], T.gq[:, 0:128], T.gs[:, 0:128], T.gt[:])
+        elif i == 1:
+            quant(["zb"], ["cqz"], T.cq[:, 1200:1328], T.cs[:, 1200:1328], zeros(512))
+        elif i == 2:
+            tt(["T64", "pf"], ["wa"], lf("wa"), lf("T64"), lf("pf"), A_.add)
+            dma("S", "dw0", ["wa"], ["wd0"], lambda: g.sync.dma_start(T.wd0[:], lf("wa")))
+            dma("S", "lw", ["xt0a", "xt0b"], ["wq"], lambda: g.sync.dma_start(b8(T.wq[:, 0:512]), T.wc[:]))
+            dma("S", "ls", [], ["wsc"], lambda: g.sync.dma_start(T.wsc[:, 0:512], T.ws[:]))
+            dma("S", "lv", [], ["vt"], lambda: g.sync.dma_start(T.vt[:], T.v[:]))
+        elif i == 3:
+            ts(["T1", "kf.12"], ["pP"], T.pP[:], li("T1"), kf(12), None, A_.add)
+        else:
+            quant(["it"], ["iq"], T.iq[:, 0:128], T.isc[:, 0:128], T.it[:])
 
     def spread(i):
-        dma("G", "ig%d" % i, ["wd%d" % i, "idx"], ["WT"], lambda: g.indirect_dma_start(
-            T.WT[:], None, T["wd%d" % i][:], IndirectOffsetOnAxis(ap=T.idx[:, 0:1], axis=0), bounds_check=7))
+        dma("G", "ig%d" % i, ["wd%d" % i, "k4.1"], ["WT"], lambda: g.indirect_dma_start(
+            T.WT[:], None, T["wd%d" % i][:], IndirectOffsetOnAxis(ap=li("k4", 1, 2), axis=0), bounds_check=7))
 
     S0V, S0A, SV, SA, CNT = "P0", "P1", "P2", "P3", "P4"
     banks = [[0, 1, 2, 3], [4, 5, 6, 7]]
@@ -384,7 +405,7 @@ def rank_program(g, core, T, topo):
         done.append(i)
 
     def catch(t, lo, hi, keys):
-        tt(["win", "xw", "al%d" % (t - 1)] + [k for k, a, b in OWN if a < hi and b > lo], keys, T.zt[:, 4 * lo:4 * hi],
+        tt(["win", "xw"] + ["al%d%d" % (t - 1, c) for c in range(lo // 192, (hi - 1) // 192 + 1)] + [k for k, a, b in OWN if a < hi and b > lo], keys, T.zt[:, 4 * lo:4 * hi],
            T.win[:, 0:8 * C].indirect(T["al%d" % (t - 1)][:, lo // 4:hi // 4]), T.xh[:, 4 * lo:4 * hi], A_.add)
 
     def layer(t, c):
@@ -402,7 +423,7 @@ def rank_program(g, core, T, topo):
            T["xt%d" % t][:, 4 * lo + b:4 * hi:4], T[k][:, 0:hi - lo], T.zf[:, 4 * lo + b:4 * hi:4], A_.add)
 
     def order(t):
-        skip = "cZyfNg" if t == 0 else "MHPXWDSQRsrtu" if t == ROUNDS else ""
+        skip = "elcZyfNg" if t == 0 else "MHPXWDSQRsrtuv" if t == ROUNDS else ""
         vector = [k for k in (VEND if t == ROUNDS else VORD) if k[0] not in skip]
         scalar = [k for k in (AEND if t == ROUNDS else AORD) if k[0] not in skip]
         seen, done = set(k for k in VORD + AORD if k[0] in skip), []
@@ -425,8 +446,14 @@ def rank_program(g, core, T, topo):
                 return ["s%d" % j]
             if k[0] == "f":
                 return ["c%d" % j]
+            if k[0] == "l":
+                return ["e%d" % j]
+            if k[0] == "g":
+                return ["l%d" % (OWN[j][1] // 192)]
+            if k[0] == "N":
+                return ["l2", "l3"]
             if k[0] == "c":
-                return ["g" + x[2:] for x, a, b in OWN if a < cuts[j + 1] and b > cuts[j]]
+                return ["l2", "l3"] + ["g" + x[2:] for x, a, b in OWN if a < cuts[j + 1] and b > cuts[j]]
             if k[0] == "Z":
                 return ["c1", "c2", "c3"] if j else ["c0"]
             if k[0] == "y":
@@ -443,7 +470,7 @@ def rank_program(g, core, T, topo):
                 return {"P": ["H0"], "X": ["H0", "q1"], "W": ["H1"]}[k[0]]
             if k == "RA":
                 return ["S0", "S1"]
-            if k[0] == "t":
+            if k[0] in "tv":
                 return made(j)[0]
             if k[0] == "u":
                 return ["Q%d" % fold(j)]
@@ -451,7 +478,7 @@ def rank_program(g, core, T, topo):
                 lo, hi = CHUNKS[j]
                 return [p if p in VORD else "r" + p[1:] for p, a, b in pieces if a < hi and b > lo]
             if k == "RB":
-                return ["RA"] + [x for x in AORD if x[0] in "tu" and made(int(x[1:]))[1] == "rx"]
+                return ["RA"] + [x for x in AORD + VORD if x[0] in "tuv" and made(int(x[1:]))[1] == "rx"]
             return []
 
         def emit(k, rest):
@@ -473,6 +500,24 @@ def rank_program(g, core, T, topo):
                 (act if rest is scalar else cp)(
                     ["xw", "tl%d" % (lo // 192), "tl%d" % ((hi - 1) // 192)], ["xh%d" % x for x in ks],
                     T.xh[:, 4 * lo:4 * hi], T.win[:, 0:4 * C].indirect(T.tl[:, lo // 4:hi // 4]))
+            elif k[0] == "e":
+                scan(["c4", "TLW"], [k], T.e3[:, 192 * j:192 * j + 192], T.TLW[:, 192 * j:192 * j + 192], T.c4[:], 0.0,
+                     A_.max, A_.add)
+            elif k[0] == "l":
+                dst, c = (T.tl, j) if j < 2 else (T["sl%d" % (t - 1)], j - 2)
+                ts(["e%d" % j, "kf.4", "kf.6"], ["tl%d" % j], dst[:, 48 * c:48 * c + 48], T.e3[:, 192 * j + 3:192 * j + 192:4],
+                   kf(4 if j < 2 else 6), None, A_.add)
+                if j >= 2:
+                    before("G", ["tl%d" % j], [])
+                    g.remote_dma(T["al%d" % (t - 1)][:, 48 * c:48 * c + 48], dst[:, 48 * c:48 * c + 48],
+                                 T.sem["al%d%d" % (t - 1, c)], T.sem.loc, pid, rid, mask)
+                    cnt["loc"] += neng
+                    if "l%d" % (5 - j) in seen:
+                        spread(t)
+            elif k[0] == "v":
+                keys, dst, e, n = made(j)
+                op("V", ["C" + x for x in keys], ["%s.%d" % (dst, j)], lambda: V.tensor_reduce(
+                    lf(dst, j, j + 1), T.Cm[:, e:e + n], AxisListType.X, A_.add))
             elif k[0] == "Z":
                 layer(t, j)
             elif k[0] == "y":
@@ -480,6 +525,8 @@ def rank_program(g, core, T, topo):
             elif k[0] == "q":
                 quantx(t, j)
                 if j and t < ROUNDS:
+                    if t == 0:
+                        spread(0)
                     before("G", ["qx%da" % t, "qx%db" % t], [])
                     for a, b in (("land", "qx"), ("lans", "sx")):
                         dst, src = T[a + str(t)][:, 0:C], T[b + str(t)][:, 0:C]
@@ -497,7 +544,7 @@ def rank_program(g, core, T, topo):
             elif k[0] in "tu":
                 total(j, k[0] == "u")
             elif k == "RA":
-                tt(["KA", "KB", "dg0", "dg1"], ["RA"], lf("RA"), lf("KA"), T.dg[:, 15:C:16], A_.subtract)
+                tt(["KA", "dg0", "dg1"], ["RA"], lf("RA"), lf("KA"), T.dg[:, 15:C:16], A_.subtract)
             elif k == "RB":
                 tt(["RA", "rx"], ["RB"], lf("RB"), lf("RA"), lf("rx"), A_.subtract)
             else:
@@ -505,41 +552,33 @@ def rank_program(g, core, T, topo):
             seen.add(k)
 
         if t == 0:
-            first = ["q0", "q1", "E0", "E1", "M0", "E2", "H0", "E3"]
+            first = ["E2", "q0", "q1", "E0", "E1", "M0", "E3", "H0", "E4"]
             vector = first + [k for k in vector if k not in first]
-            vector.insert(vector.index("H1"), "E4")
         while vector or scalar:
             if scalar and all(x in seen for x in needs(scalar[0])):
                 emit(scalar.pop(0), scalar)
-            elif vector[0] == "E4":
-                vector.pop(0)
-                quant(["it"], ["iq"], T.iq[:, 0:128], T.isc[:, 0:128], T.it[:])
             elif vector[0][0] == "E":
-                b = int(vector.pop(0)[1])
-                quant(["et"], ["eq%d" % b], T["eq%d" % b][:, 0:128], T["es%d" % b][:, 0:128], T.et[:, 4 - b:516 - b])
+                filler(int(vector.pop(0)[1]))
             else:
                 assert all(x in seen for x in needs(vector[0])), vector[0]
                 emit(vector.pop(0), vector)
 
     for t in range(ROUNDS):
         xt = T["xt%d" % t]
-        kx = ["xt%da" % t, "xt%db" % t]
         order(t)
         if t == 0:
-            spread(0)
-            op("G", [], ["TLW"], lambda: g.iota(T.TLW[:], [[-1536, 2], [4, C]], 1536, 0, allow_small_or_imprecise_dtypes=True))
+            iota(["TLW"], T.TLW[:], [[-1536, 2], [4, C]], 1536)
             act(["WT", "pP"], ["WN"], T.WN[:], T.WT[:, 0:C].indirect(T.pP[:, 0:24]), 1.0, -(MID + C) / 256)
-        for b in range(4):
-            k = "P%d" % DB[b]
-            mm(["eq%d" % b, "land%d" % t], [k], T[k][:, 0:C], T["eq%d" % b][:, 0:128],
-               T["es%d" % b][:, 0:128], T["land%d" % t][:, 0:C], T["lans%d" % t][:, 0:C])
-        act(kx, ["xw"], T.win[:, 0:4 * C], xt[:], 2.0 ** -6)
-        tt(["RB", "rs"], ["rk3"], T.rk[:, 3:96:4], lf("RB"), lf("rs"), A_.subtract)
-        scan([CNT, "rk", "rk3"], ["e1"], T.e1[:], T[CNT][:, 0:96], T.rk[:], 0.0, A_.max, A_.add)
+            later()
+        act(["xt%da" % t], ["xw.0"], T.win[:, 0:768], xt[:, 0:768], 2.0 ** -6)
+        tt(["RB", "rs"], ["rk"], T.rk[:, 3:96:4], lf("RB"), lf("rs"), A_.subtract)
+        scan([CNT, "rk"], ["e1"], T.e1[:], T[CNT][:, 0:96], T.rk[:], 0.0, A_.max, A_.add)
         if t == 0:
             quant(["vt"], ["vq"], T.vq[:, 0:128], T.vs[:, 0:128], T.vt[:])
         ts(["e1"], ["ru"], T.ru[:], T.e1[:, 3:96:4], HOLD, None, A_.add)
         ts(["e1"], ["rf"], li("rf"), T.e1[:, 3:96:4], HOLD, None, A_.add)
+        if t == 0:
+            unit(0)
         cp(["ru", "WN"], ["WS"], T.WS[:, 0:C].indirect(T.ru[:, 0:24]), T.WN[:])
         ts(["rf"], ["b1"], li("b1"), li("rf"), 31, None, A_.bitwise_and)
         ts(["rf"], ["b2"], li("b2"), li("rf"), 5, None, A_.logical_shift_right)
@@ -553,18 +592,27 @@ def rank_program(g, core, T, topo):
         ts(["WS"], ["WC1"], T.WC[:, 192:C], T.WS[:, 1:C:2], FOURS, FOURS, A_.add, A_.subtract)
         scan(["X0", "X1", "X1b"], ["o1"], T.o1[:], T.X0[:], T.X1[:], 0.0, A_.mult, A_.add)
         ts(["b1"], ["b3"], li("b3"), li("b1"), 12, None, A_.mult)
+        if t == 0:
+            unit(1)
         ts(["o1"], ["Y0.0"], T.Y0[:, 1:72:3], T.o1[:, 3:96:4], REACH, REACH, A_.add, A_.is_equal)
         ts(["o1"], ["Y0.1"], T.Y0[:, 2:36:3], T.o1[:, 51:96:4], REACH, REACH, A_.add, A_.is_equal)
         ts(["o1"], ["Y0.2"], T.Y0[:, 38:72:3], T.o1[:, 3:48:4], REACH, REACH, A_.add, A_.is_equal)
         tt(["o1"], ["Y1.0"], T.Y1[:, 0:36:3], T.o1[:, 49:96:4], T.o1[:, 1:48:4], A_.subtract)
         tt(["o1"], ["Y1.1"], T.Y1[:, 36:72:3], T.o1[:, 1:48:4], T.o1[:, 49:96:4], A_.subtract)
         act(["o1"], ["Y1.2"], T.Y1[:, 2:72:3], T.o1[:, 1:96:4])
-        for b in range(4):
-            k = "P%d" % DB[b]
-            act([k], ["win.%d" % b], T.win[:, 4 * C + b:8 * C:4], T[k][:, 0:C], 2.0 ** -6)
+        act(["xt%db" % t], ["xw.1"], T.win[:, 768:4 * C], xt[:, 768:4 * C], 2.0 ** -6)
         tt(["b3", "b2"], ["b4"], li("b4"), li("b3"), li("b2"), A_.add)
+        if t == 0:
+            unit(2)
         scan(["Y0", "Y1"], ["so"], T.so[:], T.Y0[:], T.Y1[:], 0.0, A_.mult, A_.add)
         cp(["b4"], ["rp"], T.rp[:], li("b4"))
+        if t == 0:
+            unit(3)
+        for b in range(4):
+            k = "P%d" % DB[b]
+            mm(["eq%d" % b, "land%d" % t], [k], T[k][:, 0:C], T["eq%d" % b][:, 0:128],
+               T["es%d" % b][:, 0:128], T["land%d" % t][:, 0:C], T["lans%d" % t][:, 0:C])
+            act([k], ["win.%d" % b], T.win[:, 4 * C + b:8 * C:4], T[k][:, 0:C], 2.0 ** -6)
         ts(["so"], ["Lu"], T.Lu[:], T.so[:, 2:72:3], 256.0, -MID, A_.mult, A_.add)
         kw = "wd%d" % (t + 1)
         if t == ROUNDS - 1:
@@ -573,26 +621,6 @@ def rank_program(g, core, T, topo):
             tt(["so", "X1.0"], ["wa"], lf("wa"), T.so[:, 2:72:3], T.X1[:, 0:96:4], A_.add)
         dma("S", "dw%d" % (t + 1), ["wa"], [kw], lambda: g.sync.dma_start(T[kw][:], lf("wa")))
         cp(["Lu", "WC0", "WC1"], ["TLW"], T.TLW[:, 0:768].indirect(T.Lu[:, 0:24]), T.WC[:])
-        scan(["c4", "TLW"], ["e3"], T.e3[:], T.TLW[:, 384:768], T.c4[:], 0.0, A_.max, A_.add)
-
-        def ownscan(c):
-            lo, hi = 192 * c, 192 * c + 192
-            scan(["c4", "TLW"], ["e4%d" % c], T.e4[:, lo:hi], T.TLW[:, lo:hi], T.c4[:, lo:hi], 0.0, A_.max, A_.add)
-
-        def ownlist(c):
-            ts(["e4%d" % c, "kf.4"], ["tl%d" % c], T.tl[:, 48 * c:48 * c + 48], T.e4[:, 192 * c + 3:192 * c + 192:4], kf(4),
-               None, A_.add)
-
-        ownscan(0)
-        ksl = "sl%d" % t
-        ts(["e3", "kf.6"], [ksl], T[ksl][:], T.e3[:, 3:C:4], kf(6), None, A_.add)
-        before("G", [ksl], [])
-        g.remote_dma(T["al%d" % t][:], T[ksl][:], T.sem["al%d" % t], T.sem.loc, pid, rid, mask)
-        cnt["loc"] += neng
-        spread(t + 1)
-        ownscan(1)
-        ownlist(0)
-        ownlist(1)
     order(ROUNDS)
 
     dma("A", "ool", ["WN"], [], lambda: AC.dma_start(T.ol[:], T.WN[0:128:16, :]))

from concourse.bass import IndirectOffsetOnAxis
from concourse.mybir import dt, AluOpType, ActivationFunctionType, AxisListType

C = 384
ROUNDS = 3
BIG = 2.0 ** 96
HOLD = 4096.0
FOURS = 1.5 * 2.0 ** 25
REACH = 1.5 * 2.0 ** 34
MID = 192.5
Q8 = "float8_e4m3fn_x4"
A_ = AluOpType
FN = ActivationFunctionType
COPY = FN.Copy
INTS = "P4 k4 T1 pi rf b1 b2 b3 b4".split()
FLOATS = "rs rx RA RB KA KC wa T64 pf kf cv I4".split()
NW = 1200 + 132
ROW = {}
_p = 0
for _t in range(11, -1, -1):
    ROW[_t] = _p
    ROW[_t + 12] = _p + 44
    _p += 92
DIAG = {1: _p, 0: _p + 48}
CHUNKS = [(776, 1200), (488, 776), (0, 288), (288, 488)]
FOLDS = {0: "P5", 1: "P6", 2: "P7"}
VORD = ("e2 e0 l2 e3 l0 e1 g0 l3 l1 c0 c1 Z0 c2 c3 y00 Z1 y01 y02 y03 y10 q0 y13 y12 y11 M0 q1 H0 D0 P1 X6 X5 M1 X2 H1 X0 W12 "
        "P4 W14 X3 W16 P10 X1 P5 W15 W13 X7 X9 D1 P8 Q0 X10 W18 S0 X4 S1 X8 Q1 RA W19 v7 Q2 Q3 RB v16").split()
AORD = ("g1 g2 g3 g4 f0 f1 f3 f2 N0 s9 s7 s3 s6 s11 r7 s2 t6 r2 s17 s21 r17 r6 s20 r3 t2 r20 s22 r21 r9 r22 s23 r11 t10 r23 t9 "
        "u1 u12 u0 u13 u15 t8 u14 u3 u4 u5 u18 t19").split()
VEND = "e2 e0 l2 e3 l0 e1 g0 l3 l1 c0 c1 Z0 c2 c3 y00 Z1 y01 y03 y02 y11 y10 y13 y12 q0 q1".split()
AEND = "g1 g2 g3 g4 f0 f1 f2 f3 N0".split()
JOIN = ["g4", "c3", "f3"]
OWN = [("xh0", 0, 96), ("xh1", 96, 192), ("xh2", 192, 256), ("xh3", 256, 320), ("xh4", 320, C)]
LAST = 192
PARTS = {"X1": 4, "X0": 4, "k4": 4, "Y0": 3, "Y1": 3, "c4": 4, "rs": 24, "rx": 12, "kf": 14, "gt": 4, "win": 4, "xw": 2}
for _i in range(1, ROUNDS + 1):
    PARTS["xt%da" % _i] = PARTS["xt%db" % _i] = 4

SCRATCH = {"LI": ("sbuf", [128, 24 * len(INTS)], "int32"), "LF": ("sbuf", [128, 24 * len(FLOATS)], "float32")}


def _sb(name, cols, dtype):
    SCRATCH[name] = ("sbuf", [128, cols], dtype)


for _i in range(ROUNDS + 1):
    _sb("xt%d" % _i, 4 * C, "bfloat16")
    _sb("qx%d" % _i, C, Q8)
    _sb("sx%d" % _i, C, "uint8")
    SCRATCH["wd%d" % _i] = ("dram", [8, C], "float32")
for _i in range(ROUNDS):
    _sb("land%d" % _i, C, Q8)
    _sb("lans%d" % _i, C, "uint8")
    _sb("sl%d" % _i, 96, "uint16")
    _sb("al%d" % _i, 96, "uint16")
for _i in range(4):
    _sb("eq%d" % _i, 128, Q8)
    _sb("es%d" % _i, 128, "uint8")
for _n, _c, _d in (
        ("Cm", 4 * NW, "bfloat16"), ("cq", NW, Q8), ("cs", NW, "uint8"), ("junk", 4 * NW, "bfloat16"),
        ("sg", 4 * NW, "bfloat16"), ("win", 8 * C, "bfloat16"), ("xh", 4 * C, "bfloat16"),
        ("it", 512, "bfloat16"), ("iq", 128, Q8), ("isc", 128, "uint8"),
        ("ut", 512, "bfloat16"), ("uq", 128, Q8), ("us", 128, "uint8"), ("u16q", 128, Q8), ("u16s", 128, "uint8"),
        ("vt", 512, "bfloat16"), ("vq", 128, Q8), ("vs", 128, "uint8"),
        ("wq", 512, Q8), ("wsc", 512, "uint8"), ("et", 520, "bfloat16"),
        ("zt", 4 * C, "bfloat16"), ("zf", 4 * C, "bfloat16"), ("zq", C, Q8), ("zs", C, "uint8"),
        ("gt", 512, "bfloat16"), ("gq", 128, Q8), ("gs", 128, "uint8"), ("GI", 32, "float32"), ("GA", 32, "float32"),
        ("D", 192, "float32"), ("mb", 192, "float32"), ("d0", 192, "float32"), ("a16", 192, "float32"),
        ("c16", 192, "float32"), ("c4", 192, "float32"), ("rk", 96, "float32"), ("dm", 192, "bfloat16"),
        ("dg", C, "bfloat16"), ("M", C, "float32"), ("h", C, "float32"), ("U8", 8, "int32"),
        ("pP", 24, "uint16"), ("rp", 24, "uint16"), ("upo", 8, "uint16"), ("e1", 96, "float32"), ("ru", 24, "uint16"),
        ("WT", C, "float32"), ("WN", C, "float32"), ("WS", C, "float32"), ("WC", C, "float32"),
        ("e2", C, "float32"), ("Lu", 24, "uint16"), ("TLW", 768, "float32"), ("e3", 768, "float32"),
        ("tl", 96, "uint16"),
        ("X0", 96, "float32"), ("X1", 96, "float32"), ("o1", 96, "float32"),
        ("Y0", 72, "float32"), ("Y1", 72, "float32"), ("so", 72, "float32"), ("ysb", C, "float32")):
    _sb(_n, _c, _d)
for _i in range(8):
    SCRATCH["P%d" % _i] = ("psum", [128, 512], "float32")
SEMAPHORES = (["sV", "sA", "sT", "sG", "loc", "lx", "ly", "lp", "lu", "lv", "lw", "ls", "oy0", "oy1", "ool", "oc0", "oc1"]
              + ["oos%d" % k for k in range(4)] + ["dw%d" % k for k in range(4)] + ["ig%d" % k for k in range(4)]
              + ["aq%d" % k for k in range(3)] + ["al%d%d" % (k, c) for k in range(3) for c in range(2)])


def rank_program(g, core, T, topo):
    rank = T.rank_of(core)
    if rank is None:
        return
    nxt = T.cores[(rank + 1) % len(T.cores)]
    rid, pid = topo.addr(nxt)[:2]
    mask = topo.mask(core, nxt)
    neng = len(topo.engines(core, nxt))
    prv = T.cores[(rank - 1) % len(T.cores)]
    peng = len(topo.engines(prv, core))
    V, AC, PE = g.vector, g.scalar, g.tensor
    queue = {"V": V, "A": AC, "T": PE, "G": g, "S": g.sync}
    own = {"V": "sV", "A": "sA", "T": "sT", "G": "sG"}
    cnt, known = {}, {q: {} for q in queue}
    wr, rd = {}, {}

    def ex(keys):
        return [p for k in keys for p in (["%s.%d" % (k, i) for i in range(PARTS[k])] if k in PARTS else [k])]

    def before(q, R, W, adds=False):
        toks = []
        for k in ex(R):
            if k in wr:
                toks.append(wr[k])
        for k in ex(W):
            for t in ([wr[k]] if k in wr else []) + rd.get(k, []):
                if adds and t[2] == q:
                    continue
                toks.append(t)
        best = {}
        for t in toks:
            if known[q].get(t[0], 0) < t[1] and (t[0] not in best or best[t[0]][1] < t[1]):
                best[t[0]] = t
        keep = [t for t in best.values() if not any(o is not t and o[3].get(t[0], 0) >= t[1] for o in best.values())]
        for t in keep:
            queue[q].wait_ge(T.sem[t[0]], t[1])
            for s, c in list(t[3].items()) + [(t[0], t[1])]:
                known[q][s] = max(known[q].get(s, 0), c)

    def after(q, sem, n, R, W):
        cnt[sem] = cnt.get(sem, 0) + n
        clk = dict(known[q])
        clk[sem] = cnt[sem]
        tok = (sem, cnt[sem], q, clk)
        for k in ex(R):
            rd[k] = [t for t in rd.get(k, []) if t[0] != sem] + [tok]
        for k in ex(W):
            wr[k] = tok
            rd[k] = []

    def op(q, R, W, f, adds=False):
        before(q, R, W, adds)
        f().then_inc(T.sem[own[q]], 1)
        after(q, own[q], 1, R, W)

    def dma(q, sem, R, W, f):
        before(q, R, W)
        f().then_inc(T.sem[sem], 16)
        after(q, sem, 16, R, W)

    def b8(v):
        return v.bitcast(dt.uint8)

    def li(name, lo=0, hi=24):
        o = 24 * INTS.index(name)
        return T.LI[:, o + lo:o + hi]

    def lf(name, lo=0, hi=24):
        o = 24 * FLOATS.index(name)
        return T.LF[:, o + lo:o + hi]

    def kf(i):
        return lf("kf", i, i + 1)

    def ts(R, W, out, in0, s1, s2, op0, op1=None):
        if op1 is None:
            op("V", R, W, lambda: V.tensor_scalar(out, in0, s1, None, op0))
        else:
            op("V", R, W, lambda: V.tensor_scalar(out, in0, s1, s2, op0, op1))

    def tt(R, W, out, a, b, o):
        op("V", R, W, lambda: V.tensor_tensor(out, a, b, o))

    def cp(R, W, out, a):
        op("V", R, W, lambda: V.tensor_copy(out, a))

    def ms(W, out, c):
        op("V", [], W, lambda: V.memset(out, c))

    def act(R, W, out, a, scale=None, bias=None):
        if bias is not None:
            op("A", R, W, lambda: AC.activation(out, a, FN.Identity, bias=bias, scale=scale))
        elif scale is None:
            op("A", R, W, lambda: AC.activation(out, a, COPY))
        else:
            op("A", R, W, lambda: AC.activation(out, a, COPY, scale=scale))

    def quant(R, W, q, s, t):
        op("V", R, W, lambda: V.quantize_mx(q, s, t))

    def scan(R, W, out, d0, d1, init, o0, o1):
        op("V", R, W, lambda: V.tensor_tensor_scan(out, d0, d1, init, o0, o1))

    def mm(R, W, out, lq, ls_, rq, rs_, start=True, stop=True):
        op("T", R, W, lambda: PE.matmul_mx(out, lq, ls_, rq, rs_, start, stop), not start)

    def arrives(key, sem, n):
        cnt[sem] = n
        wr[key] = (sem, n, "-", {})

    for t in range(ROUNDS):
        arrives("land%d" % t, "aq%d" % t, 2 * peng)
        for c in range(2):
            arrives("al%d%d" % (t, c), "al%d%d" % (t, c), peng)

    dma("S", "lx", [], ["xt0a"], lambda: g.sync.dma_start(T.xt0[:, 0:768], T.x[:, 0:768]))
    dma("A", "lu", [], ["ut"], lambda: AC.dma_start(T.ut[:], T.u[:]))
    dma("A", "ly", [], ["xt0b"], lambda: AC.dma_start(T.xt0[:, 768:1536], T.x[:, 768:1536]))
    dma("S", "lp", [], ["pi"], lambda: g.sync.dma_start(li("pi"), T.p[:]))

    zb = 4 * 1200

    def zeros(n):
        return T.Cm[:, zb:zb + n]

    def fn(R, W, out, a, f, scale, bias):
        op("A", R, W, lambda: AC.activation(out, a, f, bias=bias, scale=scale))

    def iota(W, out, pattern, base, cm=0):
        op("G", [], W, lambda: g.iota(out, pattern, base, cm, allow_small_or_imprecise_dtypes=True))

    iota(["P4"], li("P4", 0, 4), [[0, 4]], 0, 1)
    iota(["D"], T.D[:], [[0, 12], [1, 16]], 0)
    iota(["U8"], T.U8[:], [[16, 8]], 0)
    iota(["GI"], T.GI[:], [[1, 8], [0, 4]], 0)
    iota(["T64"], lf("T64"), [[64, 24]], 1536)
    iota(["T1"], li("T1"), [[1, 24]], 0)
    iota(["KC"], lf("KC"), [[16, 2], [0, 12]], 176)
    ms(["zb"], T.Cm[:, zb:4 * NW], 0.0)
    ts(["P4"], ["k4.0"], li("k4", 0, 1), li("P4", 0, 1), 15, None, A_.bitwise_and)
    ts(["P4"], ["k4.1"], li("k4", 1, 2), li("P4", 0, 1), 4, None, A_.logical_shift_right)
    ts(["P4"], ["k4.2"], li("k4", 2, 3), li("P4", 0, 1), 2, 3, A_.logical_shift_right, A_.bitwise_and)
    ts(["P4"], ["k4.3"], li("k4", 3, 4), li("P4", 0, 1), 3, None, A_.bitwise_and)
    cp(["k4"], ["kf.0", "kf.1", "kf.2", "kf.3"], lf("kf", 0, 4), li("k4", 0, 4))
    op("G", ["zb"], ["it"], lambda: g.affine_select(T.it[:], zeros(512), [[1, 128], [0, 4]], A_.not_equal, 1.0, 0, -1))
    op("G", ["zb"], ["et"], lambda: g.affine_select(T.et[:], zeros(520), [[1, 520]], A_.not_equal, 1.0, -4, -4))
    ts(["D", "kf.0"], ["d0"], T.d0[:], T.D[:], kf(0), BIG, A_.is_equal, A_.mult)
    ts(["D", "kf.0"], ["mb"], T.mb[:], T.D[:], kf(0), BIG, A_.not_equal, A_.mult)
    cp(["U8"], ["upo"], T.upo[:], T.U8[:])
    ms(["d0"], T.d0[:, 0:192:16], BIG)
    quant(["ut"], ["uq"], T.uq[:, 0:128], T.us[:, 0:128], T.ut[:])
    act(["zb"], ["gt"], T.gt[:], zeros(512))
    for i, src, a, b in ((7, 1, -1.0, 0.0), (13, 0, 4.0, MID / 256), (12, 0, 24.0, 0.0), (9, 2, -1.0, 0.5),
                         (5, 2, HOLD, -4 * HOLD)):
        act(["kf.%d" % src], ["kf.%d" % i], kf(i), kf(src), a, b)
    fn(["GI", "kf.7"], ["GA"], T.GA[:], T.GI[:], FN.Abs, 1.0, kf(7))
    act(["zb"], ["rs", "rx"], lf("rs", 0, 48), zeros(48))
    act(["kf.0", "kf.5"], ["kf.11"], kf(11), kf(0), 1.0, kf(5))
    for r in range(4):
        fn(["GA"], ["gt.%d" % r], T.gt[:, 5 * r:512:16], T.GA[:], FN.Relu, -1.0, 1.0)
    ts(["pi", "kf.13"], ["pf"], lf("pf"), li("pi"), 1.0 / 256, kf(13), A_.mult, A_.add)
    cp(["uq", "upo"], ["u16q"], T.u16q[:, 0:128].bitcast(dt.uint32),
       T.uq[:, 0:128].bitcast(dt.uint32).indirect(T.upo[:, 0:8]))
    act(["uq", "upo"], ["u16s"], T.u16s[:, 0:128], T.us[:, 0:128].indirect(T.upo[:, 0:8]))
    fn(["D", "kf.9"], ["I4"], lf("I4", 0, 3), T.D[:, 0:3], FN.Sign, 1.0, kf(9))
    fn(["D"], ["dm"], T.dm[:], T.D[:], FN.Sign, 1.0, 0.0)
    act(["I4"], ["cv"], lf("cv", 0, 3), lf("I4", 0, 3), HOLD)
    act(["KC", "kf.11"], ["KA"], lf("KA"), lf("KC"), 1.0, kf(11))
    for i in (3, 0, 1, 2):
        act(["zb", "cv" if i < 3 else "kf.5"], ["c4.%d" % i], T.c4[:, i:192:4], zeros(48), 1.0,
            lf("cv", i, i + 1) if i < 3 else kf(5))
    for i, src, a, b in ((8, 0, -1.0, 0.5), (10, 0, HOLD, -16 * HOLD), (4, 3, 1.0, HOLD - 1536), (6, 3, 1.0, HOLD)):
        act(["kf.%d" % src], ["kf.%d" % i], kf(i), kf(src), a, b)
    act(["c4"], ["rk"], T.rk[:], T.c4[:, 0:96])

    def later():
        fn(["D", "kf.8"], ["a16"], T.a16[:], T.D[:], FN.Sign, 1.0, kf(8))
        act(["zb"], ["X1.3"], T.X1[:, 3:96:4], zeros(24))
        for i, c in enumerate((0.0, -1.0, -1024.0, 4.0 / 3)):
            act(["zb"], ["X0.%d" % i], T.X0[:, i:96:4], zeros(24), 1.0, c)
        act(["a16"], ["c16"], T.c16[:], T.a16[:], HOLD)
        act(["zb"], ["Y0"], T.Y0[:], zeros(72))
        act(["zb"], ["Y1"], T.Y1[:], zeros(72))
        act(["zb", "kf.10"], ["c16"], T.c16[:, 15:192:16], zeros(12), 1.0, kf(10))

    def unit(b):
        quant(["et"], ["eq%d" % b], T["eq%d" % b][:, 0:128], T["es%d" % b][:, 0:128], T.et[:, 4 - b:516 - b])

    def filler(i):
        if i == 0:
            quant(["gt"], ["gq"], T.gq[:, 0:128], T.gs[:, 0:128], T.gt[:])
        elif i == 1:
            quant(["zb"], ["cqz"], T.cq[:, 1200:1328], T.cs[:, 1200:1328], zeros(512))
        elif i == 2:
            tt(["T64", "pf"], ["wa"], lf("wa"), lf("T64"), lf("pf"), A_.add)
            dma("S", "dw0", ["wa"], ["wd0"], lambda: g.sync.dma_start(T.wd0[:], lf("wa")))
            dma("S", "lw", ["xt0a", "xt0b"], ["wq"], lambda: g.sync.dma_start(b8(T.wq[:, 0:512]), T.wc[:]))
            dma("S", "ls", [], ["wsc"], lambda: g.sync.dma_start(T.wsc[:, 0:512], T.ws[:]))
            dma("S", "lv", [], ["vt"], lambda: g.sync.dma_start(T.vt[:], T.v[:]))
        elif i == 3:
            ts(["T1", "kf.12"], ["pP"], T.pP[:], li("T1"), kf(12), None, A_.add)
        else:
            quant(["it"], ["iq"], T.iq[:, 0:128], T.isc[:, 0:128], T.it[:])

    def spread(i):
        dma("G", "ig%d" % i, ["wd%d" % i, "k4.1"], ["WT"], lambda: g.indirect_dma_start(
            T.WT[:], None, T["wd%d" % i][:], IndirectOffsetOnAxis(ap=li("k4", 1, 2), axis=0), bounds_check=7))

    S0V, S0A, SV, SA, CNT = "P0", "P1", "P2", "P3", "P4"
    banks = [[0, 1, 2, 3], [4, 5, 6, 7]]
    DB = [0, 5, 6, 7]

    def run(t, c):
        m = LAST if t == ROUNDS else 192
        return (m, C) if c else (0, m)

    def quantx(t, c):
        lo, hi = run(t, c)
        kq = "qx%d%s" % (t, "ab"[c])
        qx, sx = T["qx%d" % t], T["sx%d" % t]
        quant(["xt%d%s" % (t, "ab"[c])], [kq], qx[:, lo:hi], sx[:, lo:hi], T["xt%d" % t][:, 4 * lo:4 * hi])
        if t == ROUNDS:
            k = "P%d" % c
            mm(["vq", kq], [k], T[k][:, 0:hi - lo], T.vq[:, 0:128], T.vs[:, 0:128], qx[:, lo:hi], sx[:, lo:hi])
            return
        for k in ((SV, SA) if c else (S0V, S0A)):
            mm(["u16q", "u16s", "qx%da" % t, kq], [k], T[k][:, 0:hi], T.u16q[:, 0:128], T.u16s[:, 0:128], qx[:, 0:hi], sx[:, 0:hi])

    def masked(c):
        k = SV if c else S0V
        tt([k, "mb"], ["M%d" % c], T.M[:, 192 * c:192 * c + 192], T[k][:, 192 * c:192 * c + 192], T.mb[:], A_.add)

    def held(c):
        scan(["d0", "M%d" % c], ["h%d" % c], T.h[:, 192 * c:192 * c + 192], T.d0[:], T.M[:, 192 * c:192 * c + 192], BIG,
             A_.add, A_.min)

    def hcol(j):
        return T.h[:, 16 * j + 15:16 * j + 16]

    def span(kind, j):
        if kind == "X":
            return 4 * ROW[j], 16 * (j + 13), 16 * (11 - j)
        if kind == "P":
            return 4 * ROW[j] + 16 * (11 - j), 0, 16 * j
        return 4 * ROW[j], 16 * (j - 12), 192

    def vrow(kind, j):
        e, lo, n = span(kind, j)
        k = S0V if kind == "P" else SV
        ts([k, "h%d" % (j // 12)], ["C%s%d" % (kind, j)], T.Cm[:, e:e + n], T[k][:, lo:lo + n], hcol(j), None,
           A_.is_le if kind == "X" else A_.is_lt)

    def sign(j):
        kind = "PW"[j // 12]
        e, lo, n = span(kind, j)
        k = S0A if kind == "P" else SA
        op("A", [k, "h%d" % (j // 12)], ["sg%d" % j], lambda: AC.activation(
            T.sg[:, e:e + n], T[k][:, lo:lo + n], FN.Sign, bias=hcol(j), scale=-1.0))

    def relu(j):
        kind = "PW"[j // 12]
        e, lo, n = span(kind, j)
        op("A", ["sg%d" % j], ["C%s%d" % (kind, j), "rs.%d" % j], lambda: AC.activation(
            T.Cm[:, e:e + n], T.sg[:, e:e + n], FN.Relu, accum_out=lf("rs", j, j + 1)))

    def made(j):
        if j >= 12:
            return ["W%d" % j], "rs", 4 * ROW[j], 192
        if "r%d" % j in AORD:
            return ["X%d" % j], "rx", 4 * ROW[j], 16 * (11 - j)
        return ["X%d" % j] + (["P%d" % j] if j else []), "rs", 4 * ROW[j], 176

    def fold(j):
        e, n = made(j)[2:]
        return [i for i in FOLDS if CHUNKS[i][0] <= e // 4 and (e + n) // 4 <= CHUNKS[i][1]][0]

    def total(j, folded):
        keys, dst, e, n = made(j)
        if folded:
            a, k = CHUNKS[fold(j)][0], FOLDS[fold(j)]
            keys, n = [k], n // 4
            src = T[k][:, e // 4 - a:e // 4 - a + n]
        else:
            keys, src = ["C" + k for k in keys], T.Cm[:, e:e + n]
        op("A", keys, ["%s.%d" % (dst, j), "junk%d" % j], lambda: AC.activation(
            T.junk[:, e:e + n], src, COPY, accum_out=lf(dst, j, j + 1)))

    def diag(c):
        k = SV if c else S0V
        e = 4 * DIAG[c]
        tt([k, "h%d" % c], ["CD%d" % c], T.Cm[:, e:e + 192], T[k][:, 192 * c:192 * c + 192], T.h[:, 192 * c:192 * c + 192],
           A_.is_le)

    def diagsum(c):
        e = 4 * DIAG[c]
        scan(["dm", "CD%d" % c], ["dg%d" % c], T.dg[:, 192 * c:192 * c + 192], T.dm[:], T.Cm[:, e:e + 192], 0.0,
             A_.mult, A_.add)

    pieces = [("D1", DIAG[1], DIAG[1] + 48), ("D0", DIAG[0], DIAG[0] + 48)]
    for j in range(24):
        for kind in ("W" if j >= 12 else "XP"):
            e, lo, n = span(kind, j)
            if n:
                pieces.append(("%s%d" % (kind, j), e // 4, (e + n) // 4))

    def under(lo, hi):
        return [i for i, (a, b) in enumerate(CHUNKS) if a < hi and b > lo]

    def count(i, done):
        lo, hi = CHUNKS[i]
        quant(["C" + k for k, a, b in pieces if a < hi and b > lo], ["cq%d" % i], T.cq[:, lo:hi], T.cs[:, lo:hi],
              T.Cm[:, 4 * lo:4 * hi])
        if any(k[0] == "u" and fold(int(k[1:])) == i for k in AORD):
            k = FOLDS[i]
            mm(["iq", "cq%d" % i], [k], T[k][:, 0:hi - lo], T.iq[:, 0:128], T.isc[:, 0:128], T.cq[:, lo:hi], T.cs[:, lo:hi])
        rows = [a for a in range(0, 1200, 96) if i in under(a, a + 128) and all(n in done + [i] for n in under(a, a + 128))]
        for a in rows:
            mm(["gq", "cqz"] + ["cq%d" % n for n in under(a, a + 128)], [CNT], T[CNT][:, 0:128], T.gq[:, 0:128], T.gs[:, 0:128],
               T.cq[:, a:a + 128], T.cs[:, a:a + 128], not done and a == rows[0], len(done) == len(CHUNKS) - 1 and a == rows[-1])
        done.append(i)

    def catch(t, lo, hi, keys):
        tt(["win", "xw"] + ["al%d%d" % (t - 1, c) for c in range(lo // 192, (hi - 1) // 192 + 1)] + [k for k, a, b in OWN if a < hi and b > lo], keys, T.zt[:, 4 * lo:4 * hi],
           T.win[:, 0:8 * C].indirect(T["al%d" % (t - 1)][:, lo // 4:hi // 4]), T.xh[:, 4 * lo:4 * hi], A_.add)

    def layer(t, c):
        lo, hi = run(t, c)
        quant(["zt1", "zt2", "zt3"] if c else ["zt0"], ["zq%d" % c], T.zq[:, lo:hi], T.zs[:, lo:hi], T.zt[:, 4 * lo:4 * hi])
        for b in range(4):
            k = "P%d" % banks[c][b]
            mm(["wq", "wsc", "zq%d" % c], [k], T[k][:, 0:hi - lo], T.wq[:, 128 * b:128 * b + 128],
               T.wsc[:, 128 * b:128 * b + 128], T.zq[:, lo:hi], T.zs[:, lo:hi])

    def state(t, c, b):
        lo, hi = run(t, c)
        k = "P%d" % banks[c][b]
        tt([k] + (["zf1", "zf2", "zf3"] if c else ["zf0"]), ["xt%d%s.%d" % (t, "ab"[c], b)],
           T["xt%d" % t][:, 4 * lo + b:4 * hi:4], T[k][:, 0:hi - lo], T.zf[:, 4 * lo + b:4 * hi:4], A_.add)

    def order(t):
        skip = "elcZyfNg" if t == 0 else "MHPXWDSQRsrtuv" if t == ROUNDS else ""
        vector = [k for k in (VEND if t == ROUNDS else VORD) if k[0] not in skip]
        scalar = [k for k in (AEND if t == ROUNDS else AORD) if k[0] not in skip]
        seen, done = set(k for k in VORD + AORD if k[0] in skip), []
        m = run(t, 0)[1]
        cuts = [0, m, m + (C - m) // 3 // 8 * 8, m + 2 * (C - m) // 3 // 8 * 8, C]

        def joined(k, rest):
            ks = [k]
            while (rest and rest[0] in JOIN and rest[0] == k[0] + str(int(ks[-1][1:]) + 1)
                   and all(x in seen for x in needs(rest[0]))):
                ks.append(rest.pop(0))
            seen.update(ks)
            return cuts[int(k[1:])], cuts[int(ks[-1][1:]) + 1], [x[1:] for x in ks]

        def needs(k):
            j = int(k[1:]) if k[1:].isdigit() else None
            if k[0] == "s":
                return ["H1"] if j >= 12 else ["H0"]
            if k[0] == "r":
                return ["s%d" % j]
            if k[0] == "f":
                return ["c%d" % j]
            if k[0] == "l":
                return ["e%d" % j]
            if k[0] == "g":
                return ["l%d" % (OWN[j][1] // 192)]
            if k[0] == "N":
                return ["l2", "l3"]
            if k[0] == "c":
                return ["l2", "l3"] + ["g" + x[2:] for x, a, b in OWN if a < cuts[j + 1] and b > cuts[j]]
            if k[0] == "Z":
                return ["c1", "c2", "c3"] if j else ["c0"]
            if k[0] == "y":
                return ["Z1", "f1", "f2", "f3"] if k[1] == "1" else ["Z0", "f0"]
            if k[0] == "q":
                return ["y%d%d" % (j, b) for b in range(4)] + (["q0"] if j else [])
            if k[0] == "M":
                return ["q%d" % j]
            if k[0] == "H":
                return ["M%d" % j]
            if k[0] in "DS":
                return ["HD"["DS".index(k[0])] + k[1]]
            if k[0] in "PXW":
                return {"P": ["H0"], "X": ["H0", "q1"], "W": ["H1"]}[k[0]]
            if k == "RA":
                return ["S0", "S1"]
            if k[0] in "tv":
                return made(j)[0]
            if k[0] == "u":
                return ["Q%d" % fold(j)]
            if k[0] == "Q":
                lo, hi = CHUNKS[j]
                return [p if p in VORD else "r" + p[1:] for p, a, b in pieces if a < hi and b > lo]
            if k == "RB":
                return ["RA"] + [x for x in AORD + VORD if x[0] in "tuv" and made(int(x[1:]))[1] == "rx"]
            return []

        def emit(k, rest):
            j = int(k[1:]) if k[1:].isdigit() else None
            if k[0] in "PXW":
                vrow(k[0], j)
            elif k[0] == "c":
                lo, hi, ks = joined(k, rest)
                catch(t, lo, hi, ["zt" + x for x in ks])
            elif k[0] == "f":
                lo, hi, ks = joined(k, rest)
                act(["zt" + x for x in ks], ["zf" + x for x in ks], T.zf[:, 4 * lo:4 * hi], T.zt[:, 4 * lo:4 * hi], 32.0)
            elif k[0] == "g":
                ks = [j]
                while rest and rest[0] in JOIN and rest[0] == "g%d" % (ks[-1] + 1):
                    ks.append(int(rest.pop(0)[1:]))
                    seen.add("g%d" % ks[-1])
                lo, hi = OWN[j][1], OWN[ks[-1]][2]
                (act if rest is scalar else cp)(
                    ["xw", "tl%d" % (lo // 192), "tl%d" % ((hi - 1) // 192)], ["xh%d" % x for x in ks],
                    T.xh[:, 4 * lo:4 * hi], T.win[:, 0:4 * C].indirect(T.tl[:, lo // 4:hi // 4]))
            elif k[0] == "e":
                scan(["c4", "TLW"], [k], T.e3[:, 192 * j:192 * j + 192], T.TLW[:, 192 * j:192 * j + 192], T.c4[:], 0.0,
                     A_.max, A_.add)
            elif k[0] == "l":
                dst, c = (T.tl, j) if j < 2 else (T["sl%d" % (t - 1)], j - 2)
                ts(["e%d" % j, "kf.4", "kf.6"], ["tl%d" % j], dst[:, 48 * c:48 * c + 48], T.e3[:, 192 * j + 3:192 * j + 192:4],
                   kf(4 if j < 2 else 6), None, A_.add)
                if j >= 2:
                    before("G", ["tl%d" % j], [])
                    g.remote_dma(T["al%d" % (t - 1)][:, 48 * c:48 * c + 48], dst[:, 48 * c:48 * c + 48],
                                 T.sem["al%d%d" % (t - 1, c)], T.sem.loc, pid, rid, mask)
                    cnt["loc"] += neng
                    if "l%d" % (5 - j) in seen:
                        spread(t)
            elif k[0] == "v":
                keys, dst, e, n = made(j)
                op("V", ["C" + x for x in keys], ["%s.%d" % (dst, j)], lambda: V.tensor_reduce(
                    lf(dst, j, j + 1), T.Cm[:, e:e + n], AxisListType.X, A_.add))
            elif k[0] == "Z":
                layer(t, j)
            elif k[0] == "y":
                state(t, int(k[1]), int(k[2]))
            elif k[0] == "q":
                quantx(t, j)
                if j and t < ROUNDS:
                    if t == 0:
                        spread(0)
                    before("G", ["qx%da" % t, "qx%db" % t], [])
                    for a, b in (("land", "qx"), ("lans", "sx")):
                        dst, src = T[a + str(t)][:, 0:C], T[b + str(t)][:, 0:C]
                        if b == "qx":
                            dst, src = b8(dst), b8(src)
                        g.remote_dma(dst, src, T.sem["aq%d" % t], T.sem.loc, pid, rid, mask)
                    cnt["loc"] = cnt.get("loc", 0) + 2 * neng
            elif k[0] == "N":
                if t < ROUNDS:
                    act(["WT", "rp"], ["WN"], T.WN[:], T.WT[:, 0:C].indirect(T.rp[:, 0:24]), 1.0, -(MID + C) / 256)
                else:
                    act(["WT", "rp"], ["WN"], T.WN[:], T.WT[:, 0:C].indirect(T.rp[:, 0:24]))
            elif k[0] == "Q":
                count(j, done)
            elif k[0] in "tu":
                total(j, k[0] == "u")
            elif k == "RA":
                tt(["KA", "dg0", "dg1"], ["RA"], lf("RA"), lf("KA"), T.dg[:, 15:C:16], A_.subtract)
            elif k == "RB":
                tt(["RA", "rx"], ["RB"], lf("RB"), lf("RA"), lf("rx"), A_.subtract)
            else:
                {"D": diag, "S": diagsum, "M": masked, "H": held, "s": sign, "r": relu}[k[0]](j)
            seen.add(k)

        if t == 0:
            first = ["E2", "q0", "q1", "E0", "E1", "M0", "E3", "H0", "E4"]
            vector = first + [k for k in vector if k not in first]
        while vector or scalar:
            if scalar and all(x in seen for x in needs(scalar[0])):
                emit(scalar.pop(0), scalar)
            elif vector[0][0] == "E":
                filler(int(vector.pop(0)[1]))
            else:
                assert all(x in seen for x in needs(vector[0])), vector[0]
                emit(vector.pop(0), vector)

    for t in range(ROUNDS):
        xt = T["xt%d" % t]
        order(t)
        if t == 0:
            iota(["TLW"], T.TLW[:], [[-1536, 2], [4, C]], 1536)
            act(["WT", "pP"], ["WN"], T.WN[:], T.WT[:, 0:C].indirect(T.pP[:, 0:24]), 1.0, -(MID + C) / 256)
            later()
        act(["xt%da" % t], ["xw.0"], T.win[:, 0:768], xt[:, 0:768], 2.0 ** -6)
        tt(["RB", "rs"], ["rk"], T.rk[:, 3:96:4], lf("RB"), lf("rs"), A_.subtract)
        scan([CNT, "rk"], ["e1"], T.e1[:], T[CNT][:, 0:96], T.rk[:], 0.0, A_.max, A_.add)
        if t == 0:
            quant(["vt"], ["vq"], T.vq[:, 0:128], T.vs[:, 0:128], T.vt[:])
        ts(["e1"], ["ru"], T.ru[:], T.e1[:, 3:96:4], HOLD, None, A_.add)
        ts(["e1"], ["rf"], li("rf"), T.e1[:, 3:96:4], HOLD, None, A_.add)
        if t == 0:
            unit(0)
        cp(["ru", "WN"], ["WS"], T.WS[:, 0:C].indirect(T.ru[:, 0:24]), T.WN[:])
        ts(["rf"], ["b1"], li("b1"), li("rf"), 31, None, A_.bitwise_and)
        ts(["rf"], ["b2"], li("b2"), li("rf"), 5, None, A_.logical_shift_right)
        for c in range(2):
            scan(["c16", "WS"], ["e2%d" % c], T.e2[:, 192 * c:192 * c + 192], T.WS[:, c:C:2], T.c16[:], 0.0, A_.max, A_.add)
        ts(["e20"], ["X1.2"], T.X1[:, 50:96:4], T.e2[:, 15:192:16], FOURS + HOLD, FOURS, A_.add, A_.subtract)
        ts(["WS"], ["WC0"], T.WC[:, 0:192], T.WS[:, 0:C:2], FOURS, FOURS, A_.add, A_.subtract)
        ts(["e21"], ["X1b"], T.X1[:, 2:48:4], T.e2[:, 207:C:16], FOURS + HOLD, FOURS, A_.add, A_.subtract)
        ts(["e20", "e21"], ["X1.0"], T.X1[:, 0:96:4], T.e2[:, 15:C:16], FOURS + HOLD, FOURS, A_.add, A_.subtract)
        act(["e20", "e21"], ["X1.1"], T.X1[:, 1:96:4], T.e2[:, 15:C:16], 1.0, HOLD + (MID + C) / 256)
        ts(["WS"], ["WC1"], T.WC[:, 192:C], T.WS[:, 1:C:2], FOURS, FOURS, A_.add, A_.subtract)
        scan(["X0", "X1", "X1b"], ["o1"], T.o1[:], T.X0[:], T.X1[:], 0.0, A_.mult, A_.add)
        ts(["b1"], ["b3"], li("b3"), li("b1"), 12, None, A_.mult)
        if t == 0:
            unit(1)
        ts(["o1"], ["Y0.0"], T.Y0[:, 1:72:3], T.o1[:, 3:96:4], REACH, REACH, A_.add, A_.is_equal)
        ts(["o1"], ["Y0.1"], T.Y0[:, 2:36:3], T.o1[:, 51:96:4], REACH, REACH, A_.add, A_.is_equal)
        ts(["o1"], ["Y0.2"], T.Y0[:, 38:72:3], T.o1[:, 3:48:4], REACH, REACH, A_.add, A_.is_equal)
        tt(["o1"], ["Y1.0"], T.Y1[:, 0:36:3], T.o1[:, 49:96:4], T.o1[:, 1:48:4], A_.subtract)
        tt(["o1"], ["Y1.1"], T.Y1[:, 36:72:3], T.o1[:, 1:48:4], T.o1[:, 49:96:4], A_.subtract)
        act(["o1"], ["Y1.2"], T.Y1[:, 2:72:3], T.o1[:, 1:96:4])
        act(["xt%db" % t], ["xw.1"], T.win[:, 768:4 * C], xt[:, 768:4 * C], 2.0 ** -6)
        tt(["b3", "b2"], ["b4"], li("b4"), li("b3"), li("b2"), A_.add)
        if t == 0:
            unit(2)
        scan(["Y0", "Y1"], ["so"], T.so[:], T.Y0[:], T.Y1[:], 0.0, A_.mult, A_.add)
        cp(["b4"], ["rp"], T.rp[:], li("b4"))
        if t == 0:
            unit(3)
        for b in range(4):
            k = "P%d" % DB[b]
            mm(["eq%d" % b, "land%d" % t], [k], T[k][:, 0:C], T["eq%d" % b][:, 0:128],
               T["es%d" % b][:, 0:128], T["land%d" % t][:, 0:C], T["lans%d" % t][:, 0:C])
            act([k], ["win.%d" % b], T.win[:, 4 * C + b:8 * C:4], T[k][:, 0:C], 2.0 ** -6)
        ts(["so"], ["Lu"], T.Lu[:], T.so[:, 2:72:3], 256.0, -MID, A_.mult, A_.add)
        kw = "wd%d" % (t + 1)
        if t == ROUNDS - 1:
            ts(["so"], ["wa"], lf("wa"), T.so[:, 2:72:3], 256.0, -MID, A_.mult, A_.add)
        else:
            tt(["so", "X1.0"], ["wa"], lf("wa"), T.so[:, 2:72:3], T.X1[:, 0:96:4], A_.add)
        dma("S", "dw%d" % (t + 1), ["wa"], [kw], lambda: g.sync.dma_start(T[kw][:], lf("wa")))
        cp(["Lu", "WC0", "WC1"], ["TLW"], T.TLW[:, 0:768].indirect(T.Lu[:, 0:24]), T.WC[:])
    order(ROUNDS)

    dma("A", "ool", ["WN"], [], lambda: AC.dma_start(T.ol[:], T.WN[0:128:16, :]))
    act(["P0"], ["ysb0"], T.ysb[:, 0:LAST], T.P0[:, 0:LAST])
    cp(["P1"], ["ysb1"], T.ysb[:, LAST:C], T.P1[:, 0:C - LAST])
    dma("S", "oc0", ["qx3a"], [], lambda: g.sync.dma_start(T.oc[:, 0:4 * LAST], b8(T.qx3[:, 0:LAST])))
    dma("A", "oy0", ["ysb0"], [], lambda: AC.dma_start(T.y[:, 0:LAST], T.ysb[:, 0:LAST]))
    dma("S", "oc1", ["qx3b"], [], lambda: g.sync.dma_start(T.oc[:, 4 * LAST:4 * C], b8(T.qx3[:, LAST:C])))
    for k in range(4):
        dma("A" if k % 2 else "S", "oos%d" % k, ["qx3a", "qx3b"], [], lambda: (AC if k % 2 else g.sync).dma_start(
            T.osc[4 * k:4 * k + 4, 0:C], T.sx3[32 * k:32 * k + 4, 0:C]))
    dma("S", "oy1", ["ysb1"], [], lambda: g.sync.dma_start(T.y[:, LAST:C], T.ysb[:, LAST:C]))
    for s, c in cnt.items():
        if not any(kn.get(s, 0) >= c for kn in known.values()):
            g.wait_ge(T.sem[s], c)
